import numpy as np, ml_dtypes
CORES = [2,6,10,14,18,22,26,30]
N = 8
BF = ml_dtypes.bfloat16
def gentries(a):
    return np.ascontiguousarray(a.reshape(8, 16, -1).transpose(0, 2, 1)).reshape(8, -1)
def gtable(e):
    e = np.asarray(e); return np.ascontiguousarray(e.reshape(8, -1, 16).transpose(0, 2, 1)).reshape(128, -1).astype(np.int32)
R0, P0, S, L, RO = 8192, 576, 16, 13, 2
P = P0 + RO * S; R = R0 + RO * (N - 1) * S
def counts(rng, share):
    return np.where(rng.random((N, 8, P0)) < share, rng.integers(L, 17, (N, 8, P0)), rng.integers(1, L, (N, 8, P0)))
def world(rng, cnt):
    post = rng.integers(0, R0, (N, 8, P0, 16)); home = np.full((N, 8, R0), 65535)
    on = np.argsort(rng.random((N, 8, P0, 16)), axis=-1) < cnt[..., None]
    for q in range(N):
        for g in range(8):
            ix = np.flatnonzero(on[q, g])[:R0]; c = rng.permutation(R0); n = len(ix)
            post[q, g].reshape(-1)[ix] = c[:n]; home[q, g, c[:n]] = ix
            if n: home[q, g, c[n:]] = np.where(rng.random(R0 - n) < 0.5, 65535, ix[rng.integers(0, n, R0 - n)])
    cl = rng.integers(0, 24, (N, 8, P0)); pr = rng.integers(40, 200, (8, 24, 14)); gi = np.arange(8)[None, :, None]
    at = np.minimum(home >> 4, P0 - 1)
    kc = np.where(home == 65535, rng.integers(0, 24, home.shape), np.take_along_axis(cl, at, 2))
    x = np.clip(pr[gi, kc] + rng.integers(-40, 41, (N, 8, R0, 14)), 0, 255)
    cen = rng.integers(0, 256, (N, 8, P0, 16)); cen[..., :14] = pr[gi, cl] + rng.integers(-16, 17, (N, 8, P0, 14))
    m = N * P0; w = m // 24; od = np.argsort(cl.transpose(1, 0, 2).reshape(8, m) + rng.random((8, m)), axis=1); pos = np.argsort(od, axis=1)
    z = np.take_along_axis(od, ((pos[:, :, None] + rng.integers(-w, w + 1, (8, m, 16))) % m).reshape(8, 16 * m), 1)
    near = (P * (z // P0) + z % P0).reshape(8, N, P0, 16).transpose(1, 0, 2, 3)
    near = np.where(rng.random(near.shape) < 0.15, rng.integers(0, N * P, near.shape), near)
    sl = 16 * at[:, :, None, :] + rng.integers(0, 16, (N, 8, RO, R0))
    ab = np.take_along_axis(post.reshape(N, 8, 16 * P0), sl.reshape(N, 8, RO * R0), 2).reshape(N, 8, RO, R0); u = rng.random(ab.shape)
    ab = np.where(u < 0.3, np.arange(R0), np.where(u < 0.5, rng.integers(0, R, ab.shape), ab))
    return {"x": x, "home": home, "cen": cen, "post": post, "near": near, "ab": ab}
def pack(d):
    h = d["home"][..., None]; v = np.concatenate([d["x"], h >> 8, h & 255], axis=-1).astype(np.float32)
    def turn(a): return np.ascontiguousarray(a.transpose(0, 1, 3, 2)).reshape(N, 128, -1)
    return {"rec": turn(v).astype(BF), "post": turn(d["post"]).astype(np.int32), "cen": turn(d["cen"].astype(np.float32)).astype(BF), "near": turn(d["near"]).astype(np.int32),
            "absorb": np.stack([gtable(a.reshape(8, -1)) for a in d["ab"]])}
def setup_inputs(rng):
    return pack(world(rng, counts(rng, rng.choice(np.array([0.2, 0.4, 0.6]), (N, 8, 1)))))
def setup_inputs_room(rng):
    nf = rng.choice(np.array([0, 1, S - 1, S, S + 1, 3 * S]), (N, 8)); nf[0] = (S, S + 1, S - 1, 0, 1, 3 * S, S, 2 * S); nf[1, 0] = S
    fm = np.argsort(rng.random((N, 8, P0)), axis=-1) < nf[..., None]
    cnt = np.where(fm, rng.choice(np.array([L, 16]), fm.shape), np.where(rng.random(fm.shape) < 0.5, L - 1, rng.integers(1, L, fm.shape)))
    d = world(rng, cnt); d["x"][:, 0] = rng.integers(128, 256, (N, R0, 14)); d["cen"][:, 0, :, :14] = 0
    fp = np.flatnonzero(fm[1, 0]); fq = np.flatnonzero(~fm[0, 0])
    d["near"][0, 0, fq] = (P + fp[np.arange(len(fq)) % S])[:, None]
    return pack(d)
def setup_inputs_ties(rng):
    cnt = counts(rng, 0.5); cnt[:, :, :6] = 16
    d = world(rng, cnt); d["x"] = rng.integers(0, 3, (N, 8, R0, 14)); d["cen"][..., :14] = rng.integers(0, 3, (N, 8, P0, 14))
    d["x"][:, 0] = 7; d["cen"][:, 0, :, :14] = np.where(rng.random((N, P0, 1)) < 0.5, 7, rng.integers(5, 9, (N, P0, 14)))
    d["x"][:, 2] *= rng.random((N, R0, 1)) < 0.5; d["cen"][:, 2, :, :14] = rng.integers(5, 9, (N, P0, 14))
    d["ab"][:, :4] = np.arange(R0)
    d["near"][:, 1::2] = P * rng.integers(0, N, (N, 4, P0, 16)) + rng.integers(0, 6, (N, 4, P0, 16))
    return pack(d)
def setup_inputs_ends(rng):
    q = rng.permutation(N); cnt = counts(rng, 0.3); cnt[q[0]] = rng.integers(0, L, (8, P0)); cnt[q[1]] = L
    ch = rng.permutation(P0)[:5]; cnt[:, 3] = rng.integers(1, L, (N, P0)); cnt[:, 3, ch] = 16
    cnt[:, 4] = rng.integers(1, L, (N, P0)); cnt[:, 4, 0] = 16; cnt[:, 4, P0 - 1] = L
    d = world(rng, cnt); ab = d["ab"]; near = d["near"]; d["cen"][:, 3, :, :14] = 0
    ab[:, 1] = rng.choice(np.array([0, R0 - 1]), (N, RO, R0)); ab[:, 2] = rng.integers(R0, R, (N, RO, R0)); ab[:, 5] = rng.integers(0, R0, (N, 1, 1)); ab[:, 3] = np.arange(R0)
    near[:, 4] = P * rng.integers(0, N, (N, P0, 16)) + rng.choice(np.array([0, P0 - 1, P0, P - 1]), (N, P0, 16))
    near[:, 3] = P * rng.integers(0, N, (N, P0, 16)) + np.where(rng.random((N, P0, 16)) < 0.5, P0 + rng.integers(0, 5, (N, P0, 16)), ch[rng.integers(0, 5, (N, P0, 16))])
    for a in range(N):
        s = d["post"][a, 3, ch]; d["x"][a, 3, s[:, 0]] = 0; d["x"][a, 3, s[:, 1:].reshape(-1)] = rng.integers(200, 256, (75, 14))
    return pack(d)
def setup_inputs_sharp(rng):
    d = world(rng, counts(rng, 0.4)); E = N * S - 32; n = P0 - S; i = np.arange(n)
    tg = np.where(i < n - 32, i % E, E + i - (n - 32))
    for g in range(0, 8, 2):
        fs = [np.sort(rng.permutation(P0)[:S]) for q in range(N)]; to = np.concatenate([P * q + fs[q] for q in range(N)])
        for q in range(N):
            fp = fs[q]; fq = np.setdiff1d(np.arange(P0), fp); po = d["post"][q, g]
            dull = (rng.random(n) < 0.5) & ((i < E) | ((i >= 2 * E) & (i < n - 32)))
            z = int(np.flatnonzero(tg == q * S)[0]); dull[z] = False
            cnt = np.zeros(P0, np.int64); cnt[fp] = rng.integers(L, 16, S); cnt[fq] = rng.integers(1, 5, n); cnt[fq[z]] = 1
            key = rng.random((P0, 16)); key[fp, 0] = 2
            on = np.argsort(np.argsort(key, axis=1), axis=1) < cnt[:, None]
            ix = np.flatnonzero(on); m = len(ix); c = 1 + rng.permutation(R0 - 1); dead = c[m:]; low = dead[:len(dead) // 2]; high = dead[len(dead) // 2:]
            po[fp] = rng.choice(high, (S, 16)); po[fq] = rng.choice(low, (n, 16))
            po[on] = c[:m]; po[fq[z], int(np.argmax(on[fq[z]]))] = 0
            h = np.where(rng.random(R0) < 0.5, 65535, ix[rng.integers(0, m, R0)]); h[po[on]] = ix; d["home"][q, g] = h
            x = rng.integers(130, 201, (R0, 14)); x[low] = 0; x[high] = 255
            e = fp[::2]; x[po[e][on[e]]] = 0
            e = fp[1::2]; s = po[e][on[e]]; x[s] = rng.integers(0, 3, (len(s), 14))
            e = fq[~dull]; x[po[e][on[e]]] = 127
            d["x"][q, g] = x; d["cen"][q, g, fq, :14] = 255; d["ab"][q, g, 0] = np.arange(R0)
            d["near"][q, g, fq] = np.where(np.arange(16) < rng.integers(0, 15, (n, 1)), (P * q + fq)[:, None], to[tg][:, None])
    return pack(d)
def setup_inputs_spread(rng):
    d = world(rng, counts(rng, rng.random((N, 8, 1))))
    d["x"] = np.minimum((np.exp2(8 * rng.random((N, 8, R0, 1))) * rng.random((N, 8, R0, 14))).astype(np.int64), 255)
    d["cen"] = rng.integers(0, 256, (N, 8, P0, 16)) >> rng.integers(0, 8, (N, 8, P0, 1))
    d["near"] = rng.integers(0, N * P, (N, 8, P0, 16)); d["ab"] = rng.integers(0, R, (N, 8, RO, R0))
    return pack(d)
def check_inputs(d):
    bad = []
    for k, hi in (("rec", 255), ("cen", 255), ("post", R0 - 1), ("near", N * P - 1), ("absorb", R - 1)):
        v = np.asarray(d[k]).astype(np.float64)
        if not (np.min(v) >= 0 and np.max(v) <= hi) or np.any(v != np.floor(v)): bad.append("range of " + k)
    v = np.asarray(d["rec"]).astype(np.float64).reshape(N, 8, 16, R0); h = v[:, :, 14] * 256 + v[:, :, 15]
    if np.any((h >= 16 * P0) & (h != 65535)): bad.append("homes of rec")
    return bad
def reference(rec, post, cen, near, absorb):
    w = rec.astype(np.float32).astype(np.int32).reshape(N, 8, 16, R0)
    x = np.zeros((N, 8, 14, R), np.int32); x[..., :R0] = w[:, :, :14]
    home = np.full((N, 8, R), 65535, np.int64); home[..., :R0] = w[:, :, 14] * 256 + w[:, :, 15]
    po = np.zeros((N, 8, P, 16), np.int64); po[:, :, :P0] = post.reshape(N, 8, 16, P0).transpose(0, 1, 3, 2)
    ne = np.zeros((N, 8, P, 16), np.int64); ne[:, :, :P0] = near.reshape(N, 8, 16, P0).transpose(0, 1, 3, 2)
    ce = np.zeros((N, 8, 14, P), np.int32); ce[..., :P0] = cen.astype(np.float32).astype(np.int32).reshape(N, 8, 16, P0)[:, :, :14]
    al = np.stack([gentries(a) for a in absorb]).astype(np.int64).reshape(N, 8, RO, R0)
    for t in range(RO):
        new = P0 + S * t
        for q in range(N): x[q, :, :, :R0] = np.maximum(x[q, :, :, :R0], np.take_along_axis(x[q], al[q, :, t][:, None, :], 2))
        live = (np.take_along_axis(home, po.reshape(N, 8, 16 * P), 2) == np.arange(16 * P)).reshape(N, 8, P, 16)
        full = (np.add.reduce(live.astype(np.int64), axis=3) >= L).astype(np.int64)
        num = np.add.accumulate(full, axis=2) - full; sp = (full == 1) & (num < S)
        b = np.zeros((N, 8, S, 14), np.int32); row = np.zeros((N, 8, S), np.int64)
        for q in range(N):
            for g in range(8):
                for k, p in enumerate(np.flatnonzero(sp[q, g])):
                    f = new + k; ix = po[q, g, p].copy(); v = x[q, g][:, ix]; on = live[q, g, p]
                    va = v[:, np.argmax(on)]; da = np.add.reduce(np.abs(v - va[:, None]), axis=0)
                    vb = v[:, np.argmax(np.where(on, da, -1))]; db = np.add.reduce(np.abs(v - vb[:, None]), axis=0)
                    go = on & (db < da)
                    po[q, g, f] = ix; ne[q, g, f] = ne[q, g, p]; ce[q, g, :, p] = va; ce[q, g, :, f] = vb
                    home[q, g, ix[go]] = 16 * f + np.flatnonzero(go)
                    b[q, g, k] = vb; row[q, g, k] = np.argmin(go)
        tab = np.where(sp, num + S * np.arange(N)[:, None, None], -1).transpose(1, 0, 2).reshape(8, N * P)
        mov = np.full((N, 8, N * S), -1, np.int64)
        for q in range(N):
            tj = np.take_along_axis(tab, ne[q].reshape(8, 16 * P), 1).reshape(8, P, 16)
            tg = np.take_along_axis(tj, np.argmax(tj >= 0, axis=2)[:, :, None], 2)[:, :, 0]
            for g in range(8):
                Q = np.flatnonzero((tg[g] >= 0) & ~sp[q, g]); v = x[q, g][:, po[q, g, Q]]
                vb = b[:, g].reshape(N * S, 14).T[:, tg[g, Q]]
                gain = np.add.reduce(np.abs(v - ce[q, g][:, Q][:, :, None]), axis=0) - np.add.reduce(np.abs(v - vb[:, :, None]), axis=0)
                gain = np.where(live[q, g, Q], gain, 0); m = np.argmax(gain, axis=1); ok = np.any(gain > 0, axis=1)
                Q = Q[ok]; m = m[ok]; u, i = np.unique(tg[g, Q], return_index=True)
                mov[q, g, u] = po[q, g, Q[i], m[i]]
        for r in range(N):
            win = mov[r, :, r * S:(r + 1) * S].copy()
            for o, q in enumerate([a for a in range(N) if a != r]):
                c = mov[q, :, r * S:(r + 1) * S]; e = R0 + ((N - 1) * t + o) * S
                x[r, :, :, e:e + S] = np.where((c >= 0)[:, None, :], np.take_along_axis(x[q], np.maximum(c, 0)[:, None, :], 2), 0)
                gg, kk = np.nonzero(c >= 0); home[q, gg, c[gg, kk]] = 65535
                win = np.where((win < 0) & (c >= 0), e + np.arange(S), win)
            gg, kk = np.nonzero(win >= 0); m = row[r, gg, kk]
            home[r, gg, win[gg, kk]] = 16 * (new + kk) + m; po[r, gg, new + kk, m] = win[gg, kk]
    hh = np.stack([home >> 8, home & 255], axis=2)
    ya = np.concatenate([x[..., R0:], hh[..., R0:].astype(np.int32)], axis=2).reshape(N, 128, R - R0)
    return {"ypost": np.ascontiguousarray(po.transpose(0, 1, 3, 2)).reshape(N, 128, P).astype(np.float32),
            "yh": hh[..., :R0].reshape(N, 16, R0).astype(np.float32).astype(BF), "ya": ya.astype(np.float32).astype(BF)}

@@ -1,0 +1,677 @@
+import comms_topo
+from concourse.bass import DstId, RemoteDMATransfer
+from concourse.mybir import AluOpType as A, AxisListType as AX, ActivationFunctionType as AF
+
+XW = 8704
+PW = 736
+CH = [[(0, 224), (224, 448), (448, 576)], [(0, 224), (224, 448), (448, 608)]]
+SCRATCH = {}
+for _d, _l in [("bfloat16", "REC:8704 X1:8704 X2:8704 V:9728 MC0:3584 MC1:3584 MB0:3584 MB1:3584 HG:9728 TAB0:4992 TAB1:4992 PL:2048 PLF:2048 PLN:2048 PLH:2048 "
+                "BD:128 D128:128 D16:16 TRI:128 WM:128 R15:128 BDm:128 CW:128 BW:128 CV:128 HV0:256 HV1:256 C255:128 RST:224 ONE:224 ZER:224 LV:736 LVN:736 CIN:576 C:736 "
+                "BT0:144 BT1:144 ARR0:112 ARR1:112 BA:4096 BL:4096 E:1792 SC:1792"),
+               ("float32", "BDf:128 D16f:16 R15f:128 M30:16 TC:8 TCN:8 NJC:8 DM:16 K16:16 CK:64 IOJ:256 IOG:128 IOM:128 IOS:608 IOQ:8 SLOT:608 CUM:608 "
+                "RZ0:32 RZ1:32 RV0:32 RV1:32 POSTF:736 K1:736 ST:736 FT:2048 FLT:768 KT:224 SG:224"),
+               ("int32", "PI:8 POSTI:576 NEI:736 ABI:1024"), ("uint16", "RL8:8 ABU:1024 POSTU:608 NLU:608 UT:1024")]:
+    for _x in _l.split():
+        SCRATCH[_x.split(":")[0]] = ("sbuf", [128, int(_x.split(":")[1])], _d)
+for _i in range(8):
+    SCRATCH["q%d" % _i] = ("psum", [128, 512], "float32")
+NDMA = 22
+SEMAPHORES = ["V", "S", "P", "G", "LS"] + ["d%d" % i for i in range(NDMA)] + [m + str(t) for m in ("mz", "mb", "mv", "ma") for t in (0, 1)]
+EPS, WAKE, MSG = 50, 100, 4200
+FLEX = 5
+
+
+def rank_program(g, core, T, topo):
+    rank = T.rank_of(core)
+    if rank is None:
+        return
+    eng = {"V": g.vector, "S": g.scalar, "P": g.tensor, "G": g, "Y": g.sync}
+    nodes, wlist, rlist, bank, top = [], {}, {}, {}, {}
+
+    def R(name, a=0, b=None, st=1):
+        return (name, a, SCRATCH[name][1][1] if b is None else b, st)
+
+    def I(win, off):
+        return ("I", win, off)
+
+    def cols(r, a, b, st=1):
+        return (r[0], r[1] + a, r[1] + b, st)
+
+    def ap(r):
+        if not isinstance(r, tuple):
+            return r
+        if r[0] == "I":
+            return ap(r[1]).indirect(ap(r[2]))
+        return T[r[0]][:, r[1]:r[2]] if r[3] == 1 else T[r[0]][:, r[1]:r[2]:r[3]]
+
+    def wide(r):
+        return 16 * (r[2][2] - r[2][1]) if r[0] == "I" else (r[2] - r[1] + r[3] - 1) // r[3]
+
+    def two(*rs):
+        return all([SCRATCH[r[0]][2] in ("bfloat16", "uint16") for r in rs if isinstance(r, tuple) and r[0] != "I" and wide(r) > 1])
+
+    def meet(x, y):
+        if x[1] >= y[2] or y[1] >= x[2]:
+            return False
+        return not (x[3] > 1 and x[3] == y[3] and (x[1] - y[1]) % x[3])
+
+    def node(e, call, outs, ins, cost, lat=0, kind="c", src=None, amount=1, after=()):
+        k = len(nodes)
+        deps = set(after)
+        w, rd = [], []
+        for o in outs:
+            if o[0] == "I":
+                w.append(o[1])
+                rd.append(o[2])
+            else:
+                w.append(o)
+        for i in ins:
+            if isinstance(i, tuple):
+                rd += [i[1], i[2]] if i[0] == "I" else [i]
+        for wr, rs in ((False, rd), (True, w)):
+            for r in rs:
+                b = r[0]
+                if b[0] == "q":
+                    old = bank.get(b, [])
+                    for (j, r2, wr2, e2) in old:
+                        if j != k and (e2 != e or e == "P" or len(e) > 1 or ((wr or wr2) and meet(r, r2))):
+                            deps.add(j)
+                    if e == "P" or (wr and all([r[1] <= x[1][1] and x[1][2] <= r[2] and r[3] == 1 for x in old])):
+                        old = []
+                    bank[b] = old + [(k, r, wr, e)]
+                    continue
+                for j, r2 in wlist.get(b, []):
+                    if j != k and meet(r, r2):
+                        deps.add(j)
+                if wr:
+                    for j, r2 in rlist.get(b, []):
+                        if j != k and meet(r, r2):
+                            deps.add(j)
+                    for L in (wlist, rlist):
+                        L[b] = [x for x in L.get(b, []) if x[0] == k or not (r[3] == 1 and r[1] <= x[1][1] and x[1][2] <= r[2])]
+                    wlist[b] = wlist[b] + [(k, r)]
+                else:
+                    rlist[b] = rlist.get(b, []) + [(k, r)]
+        nodes.append({"e": e, "call": call, "deps": deps, "cost": cost, "lat": lat, "kind": kind, "src": src, "amount": amount})
+        return k
+
+    def schedule():
+        n = len(nodes)
+        prio, users, left = [0] * n, [[] for _ in nodes], [len(x["deps"]) for x in nodes]
+        for k in range(n - 1, -1, -1):
+            x = nodes[k]
+            prio[k] += x["cost"] + x["lat"]
+            for d in x["deps"]:
+                prio[d] = max(prio[d], prio[k] + WAKE)
+                users[d].append(k)
+        free = {e: 0 for e in eng}
+        ready = {e: [] for e in eng}
+        order = []
+
+        def done(k, t):
+            nodes[k]["end"] = t
+            for u in users[k]:
+                left[u] -= 1
+                if left[u] == 0:
+                    offer(u)
+
+        def offer(u):
+            x = nodes[u]
+            t = max([0] + [nodes[d]["end"] + WAKE for d in x["deps"]])
+            if x["kind"] == "a":
+                order.append(u)
+                done(u, t + x["lat"])
+            else:
+                x["ready"] = t
+                for e in x["e"]:
+                    ready[e].append(u)
+        for k in range(n):
+            if not nodes[k]["deps"] and "ready" not in nodes[k]:
+                offer(k)
+        while len(order) < n:
+            pick, ok = None, {}
+            for e in eng:
+                ok[e] = ready[e]
+                if e == "V" and len([k for k in ready["S"] if len(nodes[k]["e"]) > 1]) < FLEX:
+                    ok[e] = [k for k in ready[e] if len(nodes[k]["e"]) == 1]
+                if ok[e]:
+                    s = min([max(free[e], nodes[k]["ready"]) for k in ok[e]])
+                    if pick is None or s < pick[0]:
+                        pick = (s, e)
+            s, e = pick
+            k = max([k for k in ok[e] if max(free[e], nodes[k]["ready"]) <= s + EPS], key=lambda k: (prio[k], -k))
+            x = nodes[k]
+            for f in x["e"]:
+                ready[f].remove(k)
+            x["e"] = e
+            s = max(free[e], x["ready"])
+            free[e] = s + x["cost"]
+            order.append(k)
+            done(k, free[e] + x["lat"])
+        return order
+
+    def emit():
+        seq, know, clocks, total = {}, {e: {} for e in eng}, {}, {}
+        for k in schedule():
+            x = nodes[k]
+            if x["kind"] == "a":
+                x["num"], x["amt"], clocks[(x["src"], 1)] = 1, x["amount"], {}
+                total[x["src"]] = x["amount"]
+                continue
+            e = x["e"]
+            need = {}
+            for d in x["deps"]:
+                y = nodes[d]
+                if y["kind"] == "r" or (e == "P" and y["e"] == "P"):
+                    continue
+                need[y["src"]] = max(need.get(y["src"], (0, 0)), (y["num"], y["num"] * y["amt"]))
+            for s, (num, val) in sorted(need.items()):
+                if know[e].get(s, 0) < num:
+                    eng[e].wait_ge(T.sem[s], val)
+                    for c, v in clocks[(s, num)].items():
+                        know[e][c] = max(know[e].get(c, 0), v)
+                    know[e][s] = num
+            if x["kind"] == "r":
+                x["call"](e)
+                total["LS"] = total.get("LS", 0) + x["amount"]
+                continue
+            if x["kind"] == "c":
+                x["src"] = e
+                seq[e] = seq.get(e, 0) + 1
+                x["num"], x["amt"] = seq[e], 1
+            else:
+                x["num"], x["amt"] = 1, 16
+            x["call"](e).then_inc(T.sem[x["src"]], x["amt"])
+            total[x["src"]] = x["num"] * x["amt"]
+            clocks[(x["src"], x["num"])] = dict(know[e])
+            clocks[(x["src"], x["num"])][x["src"]] = x["num"]
+        for s, v in sorted(total.items()):
+            g.wait_ge(T.sem[s], v)
+
+    def vcost(n, f):
+        return max(64, n * f) + 30
+
+    def fill(o, c):
+        node("V", lambda e: g.vector.memset(ap(o), c), [o], [], vcost(wide(o), 0.5 if two(o) else 1))
+
+    def vc(o, i):
+        n = wide(i) if o[0] == "I" else wide(o)
+        c = 50 + 3.5 * n if o[0] == "I" else 80 + 1.5 * n if i[0] == "I" else vcost(n, 0.5 if two(o, i) else 1)
+        node("V", lambda e: g.vector.tensor_copy(ap(o), ap(i)), [o], [i], c)
+        return o
+
+    def tt(o, a, b, f):
+        n = wide(o)
+        c = 80 + 1.5 * n if a[0] == "I" else vcost(n, 1 if "q" in (a[0][0], b[0][0]) else 2)
+        node("V", lambda e: g.vector.tensor_tensor(ap(o), ap(a), ap(b), f), [o], [a, b], c)
+        return o
+
+    def ts(o, a, s1, f1, s2=None, f2=None):
+        if f2 is None:
+            call = lambda e: g.vector.tensor_scalar(ap(o), ap(a), ap(s1), None, f1)
+        else:
+            call = lambda e: g.vector.tensor_scalar(ap(o), ap(a), ap(s1), ap(s2), f1, f2)
+        node("V", call, [o], [a, s1, s2], vcost(wide(o), 0.5 if two(o, a) else 1))
+        return o
+
+    def red(o, i, f):
+        node("V", lambda e: g.vector.tensor_reduce(ap(o), ap(i), AX.X, f), [o], [i], vcost(wide(i), 1))
+        return o
+
+    def scan(o, a, b, init, f0, f1):
+        node("V", lambda e: g.vector.tensor_tensor_scan(ap(o), ap(a), ap(b), ap(init), f0, f1), [o], [a, b, init], vcost(wide(o), 0.5 if two(o, a, b) else 1))
+        return o
+
+    def turn(o, i):
+        node("V", lambda e: g.vector.transpose(ap(o), ap(i)), [o], [i], vcost(wide(o), 1))
+        return o
+
+    def act(o, i, f=AF.Copy, **kw):
+        k2 = {k: ap(v) for k, v in kw.items()}
+        node("S", lambda e: g.scalar.activation(ap(o), ap(i), f, **k2), [o], [i] + list(kw.values()), 100 + wide(o) * (1.5 if i[0] == "I" else 1))
+        return o
+
+    def either(o, i):
+        n = wide(o)
+        node("VS", lambda e: g.vector.tensor_copy(ap(o), ap(i)) if e == "V" else g.scalar.activation(ap(o), ap(i), AF.Copy), [o], [i], 90 + (1.5 if i[0] == "I" else 1) * n)
+        return o
+
+    def mm(o, l, r, start=True, stop=True):
+        node("P", lambda e: g.tensor.matmul(ap(o), ap(l), ap(r), start, stop), [o], [l, r], max(64, wide(o)) * (1 if two(l) else 4))
+        return o
+
+    def iota(o, pat, mult=0, after=()):
+        kw = {} if SCRATCH[o[0]][2] == "int32" else {"allow_small_or_imprecise_dtypes": True}
+        return node("G", lambda e: g.iota(ap(o), pat, 0, mult, **kw), [o], [], 130 + 2 * wide(o), 0, "c", None, 1, after)
+
+    def dma(e, out, in_, outs, ins, lat):
+        src = "d%d" % top.get("d", 0)
+        top["d"] = top.get("d", 0) + 1
+        node(e, lambda e: eng[e].dma_start(out, in_), outs, ins, 60, lat, "d", src)
+
+    def dests():
+        return [d for d in T.cores if d != core]
+
+    def ident(d):
+        a = topo.addr(d)
+        return DstId(rid=a[0], pnc=a[1])
+
+    lanes = [i for i in topo.engines(core, dests()[0]) if all([i in topo.engines(core, d) for d in dests()])][:8]
+
+    def arrive(sem, cnt, outs, sent):
+        node("G", None, outs, [], 0, MSG, "a", sem, cnt, [sent])
+
+    def send_all(src, sem, dst, lands):
+        mask = sum([1 << i for i in lanes])
+        k = node("G", lambda e: g.remote_dma_fused([RemoteDMATransfer(dst_ids=[ident(d) for d in dests()], dma_engine_mask=mask, remote_sem=T.sem[sem], srcs=[ap(src)],
+                                                                      dsts=[ap(dst) for d in dests()])], local_sem=T.sem.LS), [], [src], 1000, 0, "r", None, len(lanes))
+        arrive(sem, 7 * len(lanes), lands, k)
+        return k
+
+    def send_each(src, sem, dst, lands):
+        ds = dests()
+        k = node("G", lambda e: g.remote_dma_fused([RemoteDMATransfer(dst_ids=[ident(d)], dma_engine_mask=1 << lanes[i], remote_sem=T.sem[sem], srcs=[ap(src(d))], dsts=[ap(dst(d))])
+                                                    for i, d in enumerate(ds)], local_sem=T.sem.LS), [], [src(d) for d in ds], 1000, 0, "r", None, len(ds))
+        arrive(sem, 7, lands, k)
+
+    def spread(o, pl, src, n):
+        h = [0, n] if n < 128 else [0, 112, n] if n > 128 else [0, 64, n]
+        for x, y in zip(h[:-1], h[1:]):
+            for m in range(16):
+                i = src(m)
+                mm(cols(o, x, y), R(pl, 128 * m, 128 * m + 128), (i[0], i[1] + x * i[3], min(i[2], i[1] + y * i[3]), i[3]), m == 0, m == 15)
+
+    def arena(name, ring):
+        def new(n):
+            w = (n + 15) // 16 * 16
+            a = top.get(name, 0)
+            if a + w > SCRATCH[name][1][1]:
+                assert ring, name
+                a = 0
+            top[name] = a + w
+            return R(name, a, a + n)
+        return new
+    F, B, U, FL, BL = arena("FT", True), arena("BA", True), arena("UT", False), arena("FLT", False), arena("BL", False)
+
+    dma("S", T.POSTI[:], T.post[:], [R("POSTI")], [], 3000)
+    dma("Y", T.REC[:, 0:8192], T.rec[:], [R("REC", 0, 8192)], [], 9000)
+    dma("S", T.ABI[:, 0:512], T.absorb[:, 0:512], [R("ABI", 0, 512)], [], 4000)
+    dma("Y", T.V[:, 0:4096], T.rec[:, 0:4096], [R("V", 0, 4096)], [], 12000)
+    dma("S", T.NEI[:, 0:576], T.near[:], [R("NEI", 0, 576)], [], 5000)
+    dma("Y", T.V[:, 4096:8192], T.rec[:, 4096:8192], [R("V", 4096, 8192)], [], 15000)
+    dma("S", T.CIN[:], T.cen[:], [R("CIN")], [], 5000)
+    dma("S", T.ABI[:, 512:1024], T.absorb[:, 512:1024], [R("ABI", 512, 1024)], [], 6000)
+
+    PI = lambda k: R("PI", k, k + 1)
+    CK = lambda k: R("CK", k, k + 1)
+    r_, g_, fm, i14, i15, f32c, fNc, hc, r0, f16, fN16 = [CK(k) for k in range(11)]
+    iota(PI(0), [[0, 1]], 1)
+    iota(R("IOG"), [[1, 8], [0, 16]])
+    iota(R("IOM"), [[0, 8], [1, 16]])
+    iota(R("IOQ"), [[16, 8]])
+    iota(R("IOJ"), [[1, 256]])
+    iota(R("IOS"), [[16, 608]])
+    for a in range(0, 4992, 1248):
+        iota(R("TAB0", a, a + 1248), [[0, 1248]])
+    node("V", lambda e: g.vector.tensor_scalar(ap(PI(1)), ap(PI(0)), 15, None, A.bitwise_and), [PI(1)], [PI(0)], 94)
+    node("V", lambda e: g.vector.tensor_scalar(ap(PI(2)), ap(PI(0)), 4, None, A.arith_shift_right), [PI(2)], [PI(0)], 94)
+    vc(r_, PI(1))
+    vc(g_, PI(2))
+    ts(fm, r_, 13.5, A.is_lt)
+    ts(i14, r_, 14.0, A.is_equal)
+    ts(i15, r_, 15.0, A.is_equal)
+    ts(r0, r_, 0.0, A.is_equal)
+    ts(hc, i14, 256.0, A.mult, i15, A.add)
+    for c, v in ((f32c, 32.0), (fNc, -32.0), (f16, 16.0), (fN16, -16.0)):
+        ts(c, fm, v, A.mult)
+    ts(R("BD"), R("IOG"), g_, A.is_equal)
+    fill(R("PL"), 0.0)
+    for m in range(16):
+        vc(R("PL", 128 * m + m, 128 * m + 128, 16), R("BD", m, 128, 16))
+    for p, c in (("PLH", hc), ("PLF", f32c), ("PLN", fNc)):
+        ts(R(p), R("PL"), c, A.mult)
+    vc(R("POSTU", 0, 576), R("POSTI"))
+    fill(R("POSTU", 576, 608), 0)
+    vc(R("ABU", 0, 512), R("ABI", 0, 512))
+    vc(R("ABU", 512, 1024), R("ABI", 512, 1024))
+    ts(R("SLOT"), R("IOS"), r_, A.add)
+    fill(R("REC", 8192, XW), 0.0)
+    fill(R("ZER"), 0.0)
+    ts(R("BDf"), R("IOG"), g_, A.is_equal)
+    ts(R("D128"), R("IOM"), r_, A.is_equal)
+    ts(R("D16"), R("IOM", 0, 16), r_, A.is_equal)
+    ts(R("D16f"), R("IOM", 0, 16), r_, A.is_equal)
+    x = ts(B(128), R("IOM"), r_, A.is_gt)
+    tt(R("TRI"), R("BD"), x, A.mult)
+    y = tt(B(128), R("BD"), R("D128"), A.mult)
+    x = ts(B(128), R("TRI"), -256.0, A.mult)
+    tt(R("WM"), x, y, A.add)
+    ts(R("RL8"), R("IOQ"), 0.0, A.mult, r_, A.add)
+    fill(R("LV", 576, PW), 0.0)
+    for t in (0, 1):
+        pc = 576 + 32 * t
+        ts(CK(16 + 4 * t), r_, float(608 - pc), A.add)
+        ts(CK(17 + 4 * t), r_, float(4864 + 16 * rank - 608 * rank - pc), A.add)
+        ts(CK(18 + 4 * t), i14, float(36 + t), A.mult)
+    ts(R("CV"), R("IOJ", 0, 128), 16.0, A.add, r0, A.mult)
+    vc(R("POSTF", 0, 576), R("POSTI"))
+    fill(R("POSTF", 576, 608), 0.0)
+    ts(R("POSTF", 608, PW), R("IOJ", 0, 128), 8416.0, A.add, r0, A.mult)
+    vc(R("NLU", 0, 576), R("NEI", 0, 576))
+    fill(R("NLU", 576, 608), 0)
+    fill(R("NEI", 576, PW), 0)
+    ts(R("M30"), R("IOM", 0, 16), -2.0, A.mult, 30.0, A.add)
+    ts(R("BW"), R("BD"), f16, A.mult)
+    x = ts(F(128), R("IOM"), -1.0, A.mult, 15.0, A.add)
+    y = ts(F(128), x, i14, A.mult, fN16, A.add)
+    tt(R("CW"), y, R("BD"), A.mult)
+    ts(R("R15"), R("BD"), i15, A.mult)
+    ts(R("R15f"), R("BDf"), i15, A.mult)
+    ts(R("BDm"), R("BD"), r_, A.mult)
+    ts(R("RST"), R("IOJ", 0, 224), 0.0, A.is_gt)
+    fill(R("RST", 0, 224, 16), 0.0)
+    fill(R("ONE"), 1.0)
+    x = ts(F(8), R("IOQ"), r_, A.add)
+    ts(R("TC"), x, 16.0, A.add)
+    ts(R("TCN"), R("TC"), -4096.0, A.mult)
+    ts(R("NJC"), x, -1.0, A.mult)
+    ts(R("C", 0, 576), R("CIN"), fm, A.mult, i14, A.add)
+    ts(R("C", 576, PW), R("IOS", 0, 160), 0.0, A.mult, i14, A.add)
+    for t in (0, 1):
+        fill(R("BT%d" % t, 0, 16), 512.0)
+        ts(R("HV%d" % t), R("IOJ"), i15, A.mult, CK(18 + 4 * t), A.add)
+    fill(R("K1", 576, PW), 0.0)
+    fill(R("ST", 576, PW), 0.0)
+    fill(R("C255"), 255.0)
+    ts(R("K16"), R("IOJ", 0, 16), 16.0, A.mult)
+    x = ts(F(16), R("K16"), r_, A.add)
+    ts(R("DM"), x, 8416.0, A.add)
+    ts(CK(24), r_, 8544.0, A.add)
+    fill(CK(25), -15.5)
+    fill(R("X1", 8192, XW), 0.0)
+    fill(R("X2", 8304, XW), 0.0)
+
+    KEYQ = ["q0", "q1", "q0"]
+
+    def absorb(X, Y, t, a, n):
+        tt(R(Y, a, a + n), I(R(X, 0, 8416), R("ABU", 512 * t + a // 16, 512 * t + (a + n) // 16)), R("V", a, a + n), A.max)
+
+    def gather(o, win, lst, a, b, e="VS"):
+        for x in range(a, b, 56):
+            y = min(b, x + 56)
+            (act if e == "S" else either)(R(o, 16 * x, 16 * y), I(win, R(lst, x, y)))
+
+    def live(c):
+        a, b = CH[0][c]
+        q = R(KEYQ[c], 0, b - a)
+        spread(q, "PLH", lambda m: R("HG", 16 * a + m, 16 * b, 16), b - a)
+        tt(R("LV", a, b), q, R("SLOT", a, b), A.is_equal)
+
+    def count(t, c, S):
+        a, b = CH[t][c]
+        n = b - a
+        q = R("q7", 0, n)
+        mm(q, R("BD"), R("LV", a, b))
+        fu = ts(B(n), q, 12.5, A.is_ge)
+        scan(R("CUM", a, b), fu, R("ZER", 0, n), R("CUM", a - 1, a) if a else 0.0, A.add, A.add)
+        le = ts(B(n), R("CUM", a, b), r_, A.is_le)
+        red(cols(S["pc"], c, c + 1), le, A.add)
+
+    def split(t, S):
+        last = CH[t][2][1]
+        inv = ts(F(1), R("CUM", last - 1, last), r_, A.is_le)
+        pz = red(F(1), S["pc"], A.add)
+        z = R("RZ%d" % t, 4 * rank, 4 * rank + 1)
+        ts(z, inv, CK(17 + 4 * t), A.mult, pz, A.add)
+        send_all(z, "mz%d" % t, z, [R("RZ%d" % t, 4 * s, 4 * s + 1) for s in range(8) if s != rank])
+        plf = ts(F(1), inv, CK(16 + 4 * t), A.mult, pz, A.add)
+        S["pl"] = ts(U(1), plf, float(-608 * rank), A.add)
+        vc(R("LVN"), R("LV"))
+        vc(I(R("LVN"), S["pl"]), R("ZER", 0, 16))
+
+    def centres(t, X, S):
+        pl = S["pl"]
+        PS = S["PS"] = vc(FL(16), I(R("POSTF"), pl))
+        LS = S["LS"] = vc(BL(16), I(R("LV"), pl))
+        mm(R("q6", 0, 16), R("TRI"), LS)
+        PSu = vc(U(16), PS)
+        EXL = tt(B(128), I(LS, R("RL8")), R("BD"), A.mult)
+        cz = ts(B(16), R("q6", 0, 16), 0.5, A.is_lt)
+        mm(R("q7", 0, 16), EXL, R("D16"))
+        oneA = tt(F(16), cz, LS, A.mult)
+        XS = vc(BL(256), I(R(X), PSu))
+        PRA = tt(F(16), oneA, PS, A.mult)
+        mm(R("q6", 16, 32), R("BDf"), PRA)
+        EXP = tt(F(128), I(PS, R("RL8")), R("BDf"), A.mult)
+        rA = vc(U(16), R("q6", 16, 32))
+        DA = tt(BL(256), I(R(X), rA), XS, A.subtract)
+        LST = vc(FL(16), R("q7", 0, 16))
+        mm(R("q7", 32, 48), EXP, R("D16f"))
+        PST = vc(F(16), R("q7", 32, 48))
+        AA = act(B(256), DA, AF.Abs)
+        spread(R("q6", 32, 48), "PLF", lambda k: cols(AA, 16 * k, 16 * k + 16), 16)
+        kb = tt(F(16), R("q6", 32, 48), R("M30"), A.add)
+        kb = tt(F(16), kb, LST, A.mult)
+        mx = red(F(1), kb, A.max)
+        OB = ts(F(16), kb, mx, A.is_equal)
+        rb = tt(F(16), OB, PST, A.mult)
+        rB = red(FL(1), rb, A.add)
+        rBu = vc(U(1), rB)
+        bt = R("BT%d" % t, 16 + 16 * rank, 32 + 16 * rank)
+        vc(bt, I(R(X), rBu))
+        S["sent"] = send_all(bt, "mb%d" % t, bt, [R("BT%d" % t, 16 + 16 * s, 32 + 16 * s) for s in range(8) if s != rank])
+        S["XS"], S["DA"], S["LST"], S["rB"], S["bt"] = XS, DA, LST, rB, bt
+        S["dA"] = vc(FL(16), R("q6", 32, 48))
+
+    def moved(t, X, S):
+        PS, LS, XS, LST = S["PS"], S["LS"], S["XS"], S["LST"]
+        dg = ts(F(16), R("D16f"), S["rB"], A.mult)
+        mm(R("q6", 64, 80), R("BDf"), dg)
+        rb = vc(U(16), R("q6", 64, 80))
+        DB = tt(B(256), I(R(X), rb), XS, A.subtract)
+        AB = act(B(256), DB, AF.Abs)
+        spread(R("q6", 96, 112), "PLF", lambda k: cols(AB, 16 * k, 16 * k + 16), 16)
+        go = tt(F(16), R("q6", 96, 112), S["dA"], A.is_lt)
+        go = tt(B(16), go, LST, A.mult)
+        EX = tt(B(128), I(go, R("RL8")), R("BD"), A.mult)
+        mm(R("q6", 128, 144), EX, R("D16"))
+        mm(R("q6", 160, 176), R("BD"), LS)
+        goN = S["goN"] = vc(BL(16), R("q6", 128, 144))
+        made = ts(F(16), R("q6", 160, 176), 0.5, A.is_gt)
+        nf = ts(B(16), goN, -1.0, A.mult, 1.0, A.add)
+        mm(R("q6", 192, 208), R("TRI"), nf)
+        pf = tt(F(16), PS, made, A.mult)
+        x = tt(F(16), PS, R("DM"), A.subtract)
+        cf = ts(B(16), R("q6", 192, 208), 0.5, A.is_lt)
+        x = tt(F(16), x, goN, A.mult)
+        FR = S["FREE"] = tt(BL(16), cf, nf, A.mult)
+        mm(R("q6", 224, 240), R("BDm"), FR)
+        x = tt(F(16), x, R("DM"), A.add)
+        pfr = tt(F(16), pf, FR, A.mult)
+        mm(R("q6", 256, 272), R("BDf"), pfr)
+        sl = vc(U(16), x)
+        S["PNF"] = tt(FL(16), pf, pfr, A.subtract)
+        w = tt(F(16), R("q6", 224, 240), R("K16"), A.add)
+        pv = tt(F(16), R("q6", 256, 272), R("D16f"), A.mult)
+        S["WV"] = ts(BL(16), w, i15, A.mult, CK(18 + 4 * t), A.add)
+        pv = red(F(1), pv, A.add)
+        S["CD"] = FL(16)
+        ts(cols(S["CD"], 0, 1), pv, -1.0, A.mult, 9000.0, A.add)
+        vc(I(R("REC"), sl), R("HV%d" % t))
+
+    def table(t):
+        zl = vc(U(8), R("RZ%d" % t, 0, 32, 4))
+        vc(I(R("TAB%d" % t), zl), R("CV"))
+
+    def target(t, c, S):
+        a, b = CH[t][c]
+        n = b - a
+        spread(R("q2", 0, n), "PL", lambda m: R("HG", 16 * a + m, 16 * b, 16), n)
+        x = either(B(n), R("q2", 0, n))
+        mm(R("q3", 0, n), R("WM"), x)
+        u = ts(B(n), R("q3", 0, n), 0.0, A.max)
+        spread(R("q3", 448, 448 + n // 16), "PL", lambda m: cols(u, m, n, 16), n // 16)
+        mm(R("q3", 224, 224 + n), R("BD"), u)
+        tu = vc(U(n // 16), R("q3", 448, 448 + n // 16))
+        S["tg%d" % c] = either(BL(n), R("q3", 224, 224 + n))
+        S["b%d" % c] = act(BL(n), I(R("BT%d" % t), tu))
+
+    def gains(t, c, S):
+        a, b = CH[t][c]
+        n = b - a
+        q = R(KEYQ[c], 0, n)
+        mm(q, R("CW"), R("C", a, b), True, False)
+        act(R("q5", 0, n), R("C", a, b))
+        for m in range(16):
+            o = R("MC%d" % (c % 2), m * n, m * n + n)
+            tt(o, R("V", 16 * a + m, 16 * b, 16), R("q5", 0, n), A.max)
+            mm(q, R("PLF", 128 * m, 128 * m + 128), o, False, False)
+        act(R("q4", 0, n), S["b%d" % c])
+        mm(q, R("BW"), S["b%d" % c], False, False)
+        for m in range(16):
+            o = R("MB%d" % (c % 2), m * n, m * n + n)
+            tt(o, R("V", 16 * a + m, 16 * b, 16), R("q4", 0, n), A.max)
+            mm(q, R("PLN", 128 * m, 128 * m + 128), o, False, m == 15)
+
+    def best(t, c, S):
+        a, b = CH[t][c]
+        n = b - a
+        tt(R("K1", a, b), R(KEYQ[c], 0, n), R("LVN", a, b), A.mult)
+        kt = turn(R("KT", 0, n), R("K1", a, b))
+        sc = scan(R("SG", 0, n), R("RST", 0, n), kt, 0.0, A.mult, A.max)
+        turn(R("ST", a, b), sc)
+        of = act(B(n), R("ST", a, b), AF.Sign, bias=CK(25))
+        mm(R("q7", 0, n), R("R15"), of)
+        tg = tt(B(n), R("q7", 0, n), S["tg%d" % c], A.mult)
+        QS = [0, 1, 2, 3] if c == 2 else [0, 1, 2, 3, 4, 5, 6, 7]
+        for q in range(8):
+            o, s = R("E", q * n, q * n + n), R("SC", q * n, q * n + n)
+            if q in QS:
+                act(o, tg, AF.Abs, bias=R("TCN", q, q + 1), scale=4096.0)
+            else:
+                ts(o, tg, R("TC", q, q + 1), A.not_equal, 4096.0, A.mult)
+            scan(s, o, R("ONE", 0, n), 4096.0, A.min, A.subtract)
+        x = ts(F(8), R("SC", n - 1, 8 * n, n), -1.0, A.mult, float(608 - b), A.add)
+        S["G"] = tt(FL(8), x, S["G"], A.max)
+
+    def movers(t, X, S):
+        arr = "ARR%d" % t
+        ql = ts(U(8), S["G"], -1.0, A.mult, 608.0, A.add)
+        val = ts(FL(8), S["G"], 0.5, A.is_gt)
+        fill(R("RV%d" % t, 4 * rank, 4 * rank + 1), 0.0)
+        send_each(lambda d: cols(val, T.rank_of(d), T.rank_of(d) + 1), "mv%d" % t, lambda d: R("RV%d" % t, 4 * rank, 4 * rank + 1),
+                  [R("RV%d" % t, 4 * s, 4 * s + 1) for s in range(8) if s != rank])
+        st = vc(F(128), I(R("ST"), ql))
+        mm(R("q7", 0, 128), R("R15f"), st)
+        k1 = vc(F(128), I(R("K1"), ql))
+        pm = vc(F(128), I(R("POSTF"), ql))
+        OB = tt(BL(128), k1, R("q7", 0, 128), A.is_equal)
+        pr = tt(F(128), OB, pm, A.mult)
+        mm(R("q7", 128, 256), R("BDf"), pr)
+        dd = tt(F(128), R("q7", 128, 256), R("D128"), A.mult)
+        sc = scan(FL(128), R("RST", 0, 128), dd, 0.0, A.mult, A.max)
+        idl = vc(U(8), cols(sc, 15, 128, 16))
+        MV = vc(BL(128), I(R(X), idl))
+        send_each(lambda d: cols(MV, 16 * T.rank_of(d), 16 * T.rank_of(d) + 16), "ma%d" % t,
+                  lambda d: (lambda o: R(arr, 16 * o, 16 * o + 16))(rank if rank < T.rank_of(d) else rank - 1), [R(arr)])
+        S["ql"], S["OB"], S["val"] = ql, OB, val
+        S["own"] = cols(sc, 16 * rank + 15, 16 * rank + 16)
+        vc(I(R("REC"), idl), R("C255"))
+
+    def winner(t, S):
+        RV, CD = "RV%d" % t, S["CD"]
+        tab = FL(8)
+        fill(tab, 0.0)
+        for s in range(8):
+            if s != rank:
+                ts(cols(tab, s, s + 1), r_, -1.0, A.mult, float(20000 - 8192 - (7 * t + (s if s < rank else s - 1)) * 16), A.add)
+        ow = ts(F(1), S["own"], -1.0, A.mult, 30000.0, A.add)
+        tt(cols(CD, 1, 2), ow, cols(S["val"], rank, rank + 1), A.mult)
+        tt(cols(CD, 2, 10), R(RV, 0, 32, 4), tab, A.mult)
+        c = red(F(1), cols(CD, 0, 10), A.max)
+        hw = ts(F(1), c, 10000.0, A.is_gt)
+        b1 = ts(F(1), c, 20500.0, A.is_gt, 10000.0, A.mult)
+        w = ts(F(1), hw, 11000.0, A.mult, c, A.subtract)
+        w = ts(F(1), w, b1, A.add, 9000.0, A.add)
+        dg = F(32)
+        ts(cols(dg, 0, 16), R("D16f"), w, A.mult)
+        ts(cols(dg, 16, 32), R("D16f"), hw, A.mult)
+        mm(R("q7", 288, 320), R("BDf"), dg)
+        x = ts(F(1), w, CK(24), A.subtract, hw, A.mult)
+        wl = ts(U(1), x, CK(24), A.add)
+        f = tt(F(16), S["FREE"], R("q7", 288, 304), A.mult)
+        n = 576 + 16 * t
+        tt(R("POSTF", n, n + 16), f, S["PNF"], A.add)
+        if t == 0:
+            f = tt(B(16), S["FREE"], R("q7", 304, 320), A.mult)
+            tt(R("LV", n, n + 16), f, S["goN"], A.add)
+            vc(R("POSTU", n, n + 16), R("POSTF", n, n + 16))
+        vc(I(R("REC"), wl), S["WV"])
+
+    def update(S):
+        pl = S["pl"]
+        ls = tt(B(16), S["LS"], S["goN"], A.subtract)
+        vc(I(R("LV"), pl), ls)
+        lm = vc(B(128), I(R("LV"), S["ql"]))
+        lm = tt(B(128), lm, S["OB"], A.subtract)
+        lm = ts(B(128), lm, 0.0, A.max)
+        vc(I(R("LV"), S["ql"]), lm)
+        at = tt(B(16), cols(S["DA"], 0, 256, 16), cols(S["XS"], 0, 256, 16), A.add)
+        at = ts(B(16), at, fm, A.mult, i14, A.add)
+        vc(I(R("C"), pl), at)
+        ts(R("C", 576, 592), S["bt"], fm, A.mult, i14, A.add)
+        vc(R("NLU", 576, 592), I(R("NEI"), pl))
+
+    SS = [{"pc": FL(4), "G": R("NJC")}, {"pc": FL(4), "G": R("NJC")}]
+    for t in (0, 1):
+        S, X, W = SS[t], "X2" if t else "X1", "X1" if t else "REC"
+        fill(cols(S["pc"], 3, 4), float(608 * rank))
+        if t == 0:
+            for c in range(3):
+                gather("HG", R("REC", 0, 8192), "POSTU", CH[0][c][0], CH[0][c][1], "S")
+                live(c)
+                count(0, c, S)
+        else:
+            for c in range(3):
+                count(1, c, S)
+        split(t, S)
+        if t:
+            vc(R("X1", 8192, 8304), R("ARR0"))
+            vc(R("X2", 8192, 8304), R("ARR0"))
+            for a in (0, 4096):
+                dma("Y", T.V[:, a:a + 4096], T.X1[:, a:a + 4096], [R("V", a, a + 4096)], [R("X1", a, a + 4096)], 5500)
+        for a in range(0, 8192, 2048):
+            absorb(W, X, t, a, 2048)
+        if t == 0:
+            fill(R("REC", 8192, 8416), 255.0)
+        centres(t, X, S)
+        if t == 0:
+            for a in range(0, 4992, 1248):
+                iota(R("TAB1", a, a + 1248), [[0, 1248]], 0, [S["sent"]])
+        moved(t, X, S)
+        table(t)
+        for c in range(3):
+            gather("HG", R("TAB%d" % t), "NLU", *CH[t][c])
+        for c in range(3):
+            gather("V", R(X, 0, 8304) if t else R(X, 0, 8192), "POSTU", *CH[t][c])
+        for c in range(3):
+            target(t, c, S)
+        for c in range(3):
+            gains(t, c, S)
+            best(t, c, S)
+        movers(t, X, S)
+        if t == 0:
+            update(S)
+        winner(t, S)
+    dma("Y", T.ypost[:], T.POSTF[:, 0:608], [], [R("POSTF", 0, 608)], 3000)
+    for k in range(8):
+        dma("YS"[k % 2], T.yh[2 * k:2 * k + 2, :], T.REC[16 * k + 14:16 * k + 16, 0:8192], [], [R("REC", 0, 8192)], 3000)
+    y = ts(B(224), R("REC", 8192, 8416), fm, A.mult)
+    h = tt(B(224), R("REC", 8192, 8416), y, A.subtract)
+    y = B(224)
+    ts(cols(y, 0, 112), R("ARR0"), fm, A.mult)
+    ts(cols(y, 112, 224), R("ARR1"), fm, A.mult)
+    ya = tt(B(224), y, h, A.add)
+    dma("Y", T.ya[:], ap(ya), [], [ya], 2500)
+    emit()

@@ -3,23 +3,29 @@ from concourse.bass import DstId, RemoteDMATransfer
 from concourse.mybir import AluOpType as A, AxisListType as AX, ActivationFunctionType as AF
 
 XW = 8704
-PW = 736
-CH = [[(0, 224), (224, 448), (448, 576)], [(0, 224), (224, 448), (448, 608)]]
+X1W = 8464
+PW = 768
+BIG = 131072.0
+CH = [[(0, 256), (256, 512), (512, 576)], [(0, 256), (256, 512), (512, 592)]]
 SCRATCH = {}
-for _d, _l in [("bfloat16", "REC:8704 X1:8704 X2:8704 V:9728 MC0:3584 MC1:3584 MB0:3584 MB1:3584 HG:9728 TAB0:4992 TAB1:4992 PL:2048 PLF:2048 PLN:2048 PLH:2048 "
-                "BD:128 D128:128 D16:16 TRI:128 WM:128 R15:128 BDm:128 CW:128 BW:128 CV:128 HV0:256 HV1:256 C255:128 RST:224 ONE:224 ZER:224 LV:736 LVN:736 CIN:576 C:736 "
-                "BT0:144 BT1:144 ARR0:112 ARR1:112 BA:4096 BL:4096 E:1792 SC:1792"),
-               ("float32", "BDf:128 D16f:16 R15f:128 M30:16 TC:8 TCN:8 NJC:8 DM:16 K16:16 CK:64 IOJ:256 IOG:128 IOM:128 IOS:608 IOQ:8 SLOT:608 CUM:608 "
-                "RZ0:32 RZ1:32 RV0:32 RV1:32 POSTF:736 K1:736 ST:736 FT:2048 FLT:768 KT:224 SG:224"),
-               ("int32", "PI:8 POSTI:576 NEI:736 ABI:1024"), ("uint16", "RL8:8 ABU:1024 POSTU:608 NLU:608 UT:1024")]:
+for _d, _l in [("bfloat16", "REC:8704 X1:8464 V1:9984 V2:9744 MC0:4096 MC1:4096 MB0:4096 MB1:4096 HG:9472 TAB0:4992 TAB1:4992 PLW:2048 ZH:144 Z1:144 ZF:144 ZN:144 ZM:144 "
+                "BD:128 D128:128 I128:128 BIGI:128 BIGD:16 TRI:128 WM:128 BDm:128 CW:128 CS:128 BW:128 NI:128 CV:128 EY:128 EM:128 P0:128 W32:8 WN32:8 HV0:256 HV1:256 C255:128 RST:256 ONE:256 "
+                "ZER:16 SXT:512 LV:768 C:768 BT0:144 BT1:144 ARR1:112 BA:4096 BL:5120 E:2048 SC:2048 STG:1024 QA:608 QB:608 M15:256 K16:16"),
+               ("float32", "BDf:128 If:128 D16f:16 WC:16 TC:8 TCN:8 NJC:8 DM:16 CK:64 IOJ:256 IOG:128 IOM:128 IOS:768 IOQ:8 SLOT:768 SLS:768 LF:624 "
+                "RZ0:32 RZ1:32 RV0:8 RV1:8 POSTF:768 FT:2048 FLT:768 SX0:256 SX1:256"),
+               ("int32", "PI:8 XI:512 POSTI:576 NEI:624 ABI:1024 IT:256"), ("uint16", "RL8:8 S16:16 ABU:512 POSTU:592 NLU:592 LU:592 UT:1024")]:
     for _x in _l.split():
         SCRATCH[_x.split(":")[0]] = ("sbuf", [128, int(_x.split(":")[1])], _d)
 for _i in range(8):
     SCRATCH["q%d" % _i] = ("psum", [128, 512], "float32")
-NDMA = 22
+NDMA = 38
 SEMAPHORES = ["V", "S", "P", "G", "LS"] + ["d%d" % i for i in range(NDMA)] + [m + str(t) for m in ("mz", "mb", "mv", "ma") for t in (0, 1)]
-EPS, WAKE, MSG = 50, 100, 4200
-FLEX = 5
+CY, GA, SCA = 0.83, 1.3, 3.1
+EPS, WAKE, MSG, ISSUE = 150, 80, 3500, 800
+FLEX = 1200
+SHORT, TURNS, KEPT = 200, 8, {}
+GS, AS = 64, 1024
+NS = [[0, 0, 0], [0, 0, 0]]
 
 
 def rank_program(g, core, T, topo):
@@ -29,21 +35,24 @@ def rank_program(g, core, T, topo):
     eng = {"V": g.vector, "S": g.scalar, "P": g.tensor, "G": g, "Y": g.sync}
     nodes, wlist, rlist, bank, top = [], {}, {}, {}, {}
 
-    def R(name, a=0, b=None, st=1):
-        return (name, a, SCRATCH[name][1][1] if b is None else b, st)
+    def R(name, a=0, b=None, st=1, pn=128):
+        return (name, a, SCRATCH[name][1][1] if b is None else b, st, pn)
 
     def I(win, off):
         return ("I", win, off)
 
     def cols(r, a, b, st=1):
-        return (r[0], r[1] + a, r[1] + b, st)
+        return (r[0], r[1] + a, r[1] + b, st, r[4])
+
+    def rows(r, pn):
+        return r[:4] + (pn,)
 
     def ap(r):
         if not isinstance(r, tuple):
             return r
         if r[0] == "I":
             return ap(r[1]).indirect(ap(r[2]))
-        return T[r[0]][:, r[1]:r[2]] if r[3] == 1 else T[r[0]][:, r[1]:r[2]:r[3]]
+        return T[r[0]][0:r[4], r[1]:r[2]] if r[3] == 1 else T[r[0]][0:r[4], r[1]:r[2]:r[3]]
 
     def wide(r):
         return 16 * (r[2][2] - r[2][1]) if r[0] == "I" else (r[2] - r[1] + r[3] - 1) // r[3]
@@ -89,66 +98,90 @@ def rank_program(g, core, T, topo):
                         if j != k and meet(r, r2):
                             deps.add(j)
                     for L in (wlist, rlist):
-                        L[b] = [x for x in L.get(b, []) if x[0] == k or not (r[3] == 1 and r[1] <= x[1][1] and x[1][2] <= r[2])]
+                        L[b] = [x for x in L.get(b, []) if x[0] == k or not (r[3] == 1 and r[4] == 128 and r[1] <= x[1][1] and x[1][2] <= r[2])]
                     wlist[b] = wlist[b] + [(k, r)]
                 else:
                     rlist[b] = rlist.get(b, []) + [(k, r)]
-        nodes.append({"e": e, "call": call, "deps": deps, "cost": cost, "lat": lat, "kind": kind, "src": src, "amount": amount})
+        nodes.append({"e": e, "call": call, "deps": deps, "cost": cost if isinstance(cost, dict) else {e: cost}, "lat": lat, "kind": kind, "src": src, "amount": amount})
         return k
 
     def schedule():
         n = len(nodes)
-        prio, users, left = [0] * n, [[] for _ in nodes], [len(x["deps"]) for x in nodes]
-        for k in range(n - 1, -1, -1):
-            x = nodes[k]
-            prio[k] += x["cost"] + x["lat"]
-            for d in x["deps"]:
-                prio[d] = max(prio[d], prio[k] + WAKE)
-                users[d].append(k)
-        free = {e: 0 for e in eng}
-        ready = {e: [] for e in eng}
-        order = []
-
-        def done(k, t):
-            nodes[k]["end"] = t
-            for u in users[k]:
-                left[u] -= 1
-                if left[u] == 0:
-                    offer(u)
-
-        def offer(u):
-            x = nodes[u]
-            t = max([0] + [nodes[d]["end"] + WAKE for d in x["deps"]])
-            if x["kind"] == "a":
-                order.append(u)
-                done(u, t + x["lat"])
-            else:
-                x["ready"] = t
-                for e in x["e"]:
-                    ready[e].append(u)
+        users = [[] for _ in nodes]
         for k in range(n):
-            if not nodes[k]["deps"] and "ready" not in nodes[k]:
+            for d in nodes[k]["deps"]:
+                users[d].append(k)
+        gap = lambda a, b: 0 if nodes[a]["e"] == "P" and nodes[b]["e"] == "P" else WAKE
+
+        def lay(before, after, where, prio, back):
+            left, end, at, on = [len(x) for x in before], [0] * n, [0] * n, [None] * n
+            prio = [p + (0 if back else x.get("soon", 0)) for p, x in zip(prio, nodes)]
+            free, ready, order = {e: 0 for e in eng}, {e: [] for e in eng}, []
+
+            def done(k, t):
+                end[k] = t
+                order.append(k)
+                for u in after[k]:
+                    left[u] -= 1
+                    if left[u] == 0:
+                        offer(u)
+
+            def offer(u):
+                t = max([0] + [end[d] + gap(u, d) for d in before[u]])
+                if nodes[u]["kind"] == "a":
+                    done(u, t + nodes[u]["lat"])
+                else:
+                    at[u] = t + (nodes[u]["lat"] if back else 0)
+                    for e in where[u]:
+                        ready[e].append(u)
+            for k in [k for k in range(n) if not before[k]]:
                 offer(k)
-        while len(order) < n:
-            pick, ok = None, {}
-            for e in eng:
-                ok[e] = ready[e]
-                if e == "V" and len([k for k in ready["S"] if len(nodes[k]["e"]) > 1]) < FLEX:
-                    ok[e] = [k for k in ready[e] if len(nodes[k]["e"]) == 1]
-                if ok[e]:
-                    s = min([max(free[e], nodes[k]["ready"]) for k in ok[e]])
-                    if pick is None or s < pick[0]:
-                        pick = (s, e)
-            s, e = pick
-            k = max([k for k in ok[e] if max(free[e], nodes[k]["ready"]) <= s + EPS], key=lambda k: (prio[k], -k))
-            x = nodes[k]
-            for f in x["e"]:
-                ready[f].remove(k)
-            x["e"] = e
-            s = max(free[e], x["ready"])
-            free[e] = s + x["cost"]
-            order.append(k)
-            done(k, free[e] + x["lat"])
+            while len(order) < n:
+                pick = None
+                for e in eng:
+                    if ready[e]:
+                        s = max(free[e], min([at[k] for k in ready[e]]))
+                        ok = [k for k in ready[e] if at[k] <= s + EPS]
+                        if e == "V" and not back:
+                            own = [k for k in ok if len(where[k]) == 1]
+                            best = max(ok, key=lambda k: prio[k])
+                            if len(where[best]) > 1 and nodes[best]["cost"]["V"] < SHORT and free["S"] > s + SHORT:
+                                ok = [best]
+                            elif own:
+                                ok = own
+                            elif free["S"] + sum([nodes[k]["cost"]["S"] for k in ready["S"] if at[k] <= s + EPS]) - s < FLEX:
+                                later = [k for k in ready[e] if len(where[k]) == 1]
+                                if not later:
+                                    continue
+                                s = max(free[e], min([at[k] for k in later]))
+                                ok = [k for k in later if at[k] <= s + EPS]
+                        if pick is None or s < pick[0]:
+                            pick = (s, e, ok)
+                s, e, ok = pick
+                k = max(ok, key=lambda k: (prio[k], -k))
+                while not back and nodes[k].get("behind") in ready[e]:
+                    k = nodes[k]["behind"]
+                for f in where[k]:
+                    ready[f].remove(k)
+                on[k] = e
+                free[e] = max(free[e], at[k]) + nodes[k]["cost"][e]
+                done(k, free[e] + (0 if back else nodes[k]["lat"]))
+            return end, order, on
+
+        deps, where = [x["deps"] for x in nodes], [x["e"] for x in nodes]
+        if "prio" not in KEPT:
+            prio, best = [0] * n, None
+            for k in range(n - 1, -1, -1):
+                prio[k] = min(nodes[k]["cost"].values()) + nodes[k]["lat"] + max([0] + [prio[u] + gap(k, u) for u in users[k]])
+            for turn in range(TURNS):
+                end, order, on = lay(deps, users, where, prio, False)
+                if best is None or max(end) < best[0]:
+                    best = (max(end), prio)
+                prio = lay(users, deps, on, end, True)[0]
+            KEPT["prio"], KEPT["end"] = best[1], best[0]
+        end, order, on = lay(deps, users, where, KEPT["prio"], False)
+        for k in range(n):
+            nodes[k]["e"] = on[k] or nodes[k]["e"]
         return order
 
     def emit():
@@ -189,66 +222,82 @@ def rank_program(g, core, T, topo):
         for s, v in sorted(total.items()):
             g.wait_ge(T.sem[s], v)
 
-    def vcost(n, f):
-        return max(64, n * f) + 30
+    def vcost(o, i, f):
+        if o[0] == "I":
+            return 50 + SCA * wide(i)
+        return 50 + GA * wide(o) if i[0] == "I" else max(64, max(wide(o), wide(i)) * f) * CY
+
+    def scost(o, i):
+        return 65 + wide(o) * (GA if i[0] == "I" else CY)
 
     def fill(o, c):
-        node("V", lambda e: g.vector.memset(ap(o), c), [o], [], vcost(wide(o), 0.5 if two(o) else 1))
+        node("V", lambda e: g.vector.memset(ap(o), c), [o], [], vcost(o, o, 0.5 if two(o) else 1))
 
     def vc(o, i):
-        n = wide(i) if o[0] == "I" else wide(o)
-        c = 50 + 3.5 * n if o[0] == "I" else 80 + 1.5 * n if i[0] == "I" else vcost(n, 0.5 if two(o, i) else 1)
-        node("V", lambda e: g.vector.tensor_copy(ap(o), ap(i)), [o], [i], c)
+        node("V", lambda e: g.vector.tensor_copy(ap(o), ap(i)), [o], [i], vcost(o, i, 0.5 if two(o, i) else 1))
         return o
 
     def tt(o, a, b, f):
-        n = wide(o)
-        c = 80 + 1.5 * n if a[0] == "I" else vcost(n, 1 if "q" in (a[0][0], b[0][0]) else 2)
-        node("V", lambda e: g.vector.tensor_tensor(ap(o), ap(a), ap(b), f), [o], [a, b], c)
+        node("V", lambda e: g.vector.tensor_tensor(ap(o), ap(a), ap(b), f), [o], [a, b], vcost(o, a, 1 if "q" in (a[0][0], b[0][0]) else 2))
         return o
 
-    def ts(o, a, s1, f1, s2=None, f2=None):
+    def tsc(o, a, s1, f1, s2, f2):
         if f2 is None:
-            call = lambda e: g.vector.tensor_scalar(ap(o), ap(a), ap(s1), None, f1)
-        else:
-            call = lambda e: g.vector.tensor_scalar(ap(o), ap(a), ap(s1), ap(s2), f1, f2)
-        node("V", call, [o], [a, s1, s2], vcost(wide(o), 0.5 if two(o, a) else 1))
+            return g.vector.tensor_scalar(ap(o), ap(a), ap(s1), None, f1)
+        return g.vector.tensor_scalar(ap(o), ap(a), ap(s1), ap(s2), f1, f2)
+
+    def ts(o, a, s1, f1, s2=None, f2=None):
+        node("V", lambda e: tsc(o, a, s1, f1, s2, f2), [o], [a, s1, s2], vcost(o, a, 0.5 if two(o, a) else 1))
         return o
 
     def red(o, i, f):
-        node("V", lambda e: g.vector.tensor_reduce(ap(o), ap(i), AX.X, f), [o], [i], vcost(wide(i), 1))
+        node("V", lambda e: g.vector.tensor_reduce(ap(o), ap(i), AX.X, f), [o], [i], vcost(o, i, 1))
         return o
 
     def scan(o, a, b, init, f0, f1):
-        node("V", lambda e: g.vector.tensor_tensor_scan(ap(o), ap(a), ap(b), ap(init), f0, f1), [o], [a, b, init], vcost(wide(o), 0.5 if two(o, a, b) else 1))
+        node("V", lambda e: g.vector.tensor_tensor_scan(ap(o), ap(a), ap(b), ap(init), f0, f1), [o], [a, b, init], vcost(o, a, 0.5 if two(o, a, b) else 1))
         return o
 
-    def turn(o, i):
-        node("V", lambda e: g.vector.transpose(ap(o), ap(i)), [o], [i], vcost(wide(o), 1))
-        return o
-
-    def act(o, i, f=AF.Copy, **kw):
+    def act(o, i, f=AF.Copy, acc=None, **kw):
         k2 = {k: ap(v) for k, v in kw.items()}
-        node("S", lambda e: g.scalar.activation(ap(o), ap(i), f, **k2), [o], [i] + list(kw.values()), 100 + wide(o) * (1.5 if i[0] == "I" else 1))
+        if acc:
+            k2["accum_out"] = ap(acc)
+        node("S", lambda e: g.scalar.activation(ap(o), ap(i), f, **k2), [o] + ([acc] if acc else []), [i] + list(kw.values()), scost(o, i))
+        return o
+
+    def both(o, i, fv, fs, more=()):
+        node("VS", lambda e: fv() if e == "V" else fs(), [o], [i] + list(more), {"V": vcost(o, i, 0.5 if two(o, i) else 1), "S": scost(o, i)})
         return o
 
     def either(o, i):
-        n = wide(o)
-        node("VS", lambda e: g.vector.tensor_copy(ap(o), ap(i)) if e == "V" else g.scalar.activation(ap(o), ap(i), AF.Copy), [o], [i], 90 + (1.5 if i[0] == "I" else 1) * n)
-        return o
+        return both(o, i, lambda: g.vector.tensor_copy(ap(o), ap(i)), lambda: g.scalar.activation(ap(o), ap(i), AF.Copy))
+
+    def relu(o, i):
+        return both(o, i, lambda: tsc(o, i, 0.0, A.max, None, None), lambda: g.scalar.activation(ap(o), ap(i), AF.Relu))
+
+    def times(o, i, c, d=0.0):
+        return both(o, i, lambda: tsc(o, i, c, A.mult, d, A.add),
+                    lambda: g.scalar.activation(ap(o), ap(i), AF.Identity if isinstance(d, tuple) else AF.Copy, scale=ap(c), bias=ap(d)), [c, d])
 
     def mm(o, l, r, start=True, stop=True):
-        node("P", lambda e: g.tensor.matmul(ap(o), ap(l), ap(r), start, stop), [o], [l, r], max(64, wide(o)) * (1 if two(l) else 4))
+        node("P", lambda e: g.tensor.matmul(ap(o), ap(l), ap(r), start, stop), [o], [l, r], max(min(64, wide(l)), wide(o)) * CY * (1 if two(l) else 4))
         return o
 
-    def iota(o, pat, mult=0, after=()):
-        kw = {} if SCRATCH[o[0]][2] == "int32" else {"allow_small_or_imprecise_dtypes": True}
-        return node("G", lambda e: g.iota(ap(o), pat, 0, mult, **kw), [o], [], 130 + 2 * wide(o), 0, "c", None, 1, after)
+    def group(o, terms):
+        for j, (x, l, r) in enumerate(terms):
+            mm(x, l, r, j == 0, j == len(terms) - 1)
+        return o
 
-    def dma(e, out, in_, outs, ins, lat):
+    def iota(o, pat, base=0, mult=0, after=()):
+        kw = {} if SCRATCH[o[0]][2] == "int32" else {"allow_small_or_imprecise_dtypes": True}
+        return node("G", lambda e: g.iota(ap(o), pat, base, mult, **kw), [o], [], 130 + 2 * CY * wide(o), 0, "c", None, 1, after)
+
+    def dma(e, out, in_, outs, ins, lat, behind=None):
         src = "d%d" % top.get("d", 0)
         top["d"] = top.get("d", 0) + 1
-        node(e, lambda e: eng[e].dma_start(out, in_), outs, ins, 60, lat, "d", src)
+        k = node(e, lambda e: eng[e].dma_start(out, in_), outs, ins, 60, lat, "d", src)
+        nodes[k]["behind"] = behind
+        return k
 
     def dests():
         return [d for d in T.cores if d != core]
@@ -265,22 +314,21 @@ def rank_program(g, core, T, topo):
     def send_all(src, sem, dst, lands):
         mask = sum([1 << i for i in lanes])
         k = node("G", lambda e: g.remote_dma_fused([RemoteDMATransfer(dst_ids=[ident(d) for d in dests()], dma_engine_mask=mask, remote_sem=T.sem[sem], srcs=[ap(src)],
-                                                                      dsts=[ap(dst) for d in dests()])], local_sem=T.sem.LS), [], [src], 1000, 0, "r", None, len(lanes))
+                                                                      dsts=[ap(dst) for d in dests()])], local_sem=T.sem.LS), [], [src], ISSUE, 0, "r", None, len(lanes))
         arrive(sem, 7 * len(lanes), lands, k)
         return k
 
     def send_each(src, sem, dst, lands):
         ds = dests()
         k = node("G", lambda e: g.remote_dma_fused([RemoteDMATransfer(dst_ids=[ident(d)], dma_engine_mask=1 << lanes[i], remote_sem=T.sem[sem], srcs=[ap(src(d))], dsts=[ap(dst(d))])
-                                                    for i, d in enumerate(ds)], local_sem=T.sem.LS), [], [src(d) for d in ds], 1000, 0, "r", None, len(ds))
+                                                    for i, d in enumerate(ds)], local_sem=T.sem.LS), [], [src(d) for d in ds], ISSUE, 0, "r", None, len(ds))
         arrive(sem, 7, lands, k)
 
-    def spread(o, pl, src, n):
-        h = [0, n] if n < 128 else [0, 112, n] if n > 128 else [0, 64, n]
-        for x, y in zip(h[:-1], h[1:]):
-            for m in range(16):
-                i = src(m)
-                mm(cols(o, x, y), R(pl, 128 * m, 128 * m + 128), (i[0], i[1] + x * i[3], min(i[2], i[1] + y * i[3]), i[3]), m == 0, m == 15)
+    def Z(z, m):
+        return R(z, 15 - m, 143 - m)
+
+    def place(d):
+        return rank if rank < T.rank_of(d) else rank - 1
 
     def arena(name, ring):
         def new(n):
@@ -292,213 +340,224 @@ def rank_program(g, core, T, topo):
             top[name] = a + w
             return R(name, a, a + n)
         return new
-    F, B, U, FL, BL = arena("FT", True), arena("BA", True), arena("UT", False), arena("FLT", False), arena("BL", False)
+    F, B, U, FL, BL, IT = arena("FT", True), arena("BA", True), arena("UT", False), arena("FLT", False), arena("BL", False), arena("IT", True)
 
-    dma("S", T.POSTI[:], T.post[:], [R("POSTI")], [], 3000)
-    dma("Y", T.REC[:, 0:8192], T.rec[:], [R("REC", 0, 8192)], [], 9000)
-    dma("S", T.ABI[:, 0:512], T.absorb[:, 0:512], [R("ABI", 0, 512)], [], 4000)
-    dma("Y", T.V[:, 0:4096], T.rec[:, 0:4096], [R("V", 0, 4096)], [], 12000)
-    dma("S", T.NEI[:, 0:576], T.near[:], [R("NEI", 0, 576)], [], 5000)
-    dma("Y", T.V[:, 4096:8192], T.rec[:, 4096:8192], [R("V", 4096, 8192)], [], 15000)
-    dma("S", T.CIN[:], T.cen[:], [R("CIN")], [], 5000)
-    dma("S", T.ABI[:, 512:1024], T.absorb[:, 512:1024], [R("ABI", 512, 1024)], [], 6000)
+    dma("S", T.POSTI[:], T.post[:], [R("POSTI")], [], 2500)
+    k = dma("Y", T.ABI[:], T.absorb[:], [R("ABI")], [], 2800)
+    k = dma("Y", T.V1[:, 0:1024], T.rec[:, 0:1024], [R("V1", 0, 1024)], [], 3300, k)
+    k = dma("Y", T.REC[:, 0:8192], T.rec[:], [R("REC", 0, 8192)], [], 6700, k)
+    for a, b in ((1024, 3072), (3072, 5120), (5120, 8192)):
+        k = dma("Y", T.V1[:, a:b], T.rec[:, a:b], [R("V1", a, b)], [], 6300 + b * 0.45, k)
+    k = dma("Y", T.NEI[:, 0:576], T.near[:], [R("NEI", 0, 576)], [], 10500, k)
+    dma("Y", T.C[:, 0:576], T.cen[:], [R("C", 0, 576)], [], 11000, k)
 
     PI = lambda k: R("PI", k, k + 1)
     CK = lambda k: R("CK", k, k + 1)
-    r_, g_, fm, i14, i15, f32c, fNc, hc, r0, f16, fN16 = [CK(k) for k in range(11)]
-    iota(PI(0), [[0, 1]], 1)
+    r_, g_, fm, i14, i15, f32c, fNc, hc, r0, f16, fN16, p_, p0, c15, c33, cN33, nfm, cB, g2, cH = [CK(k) for k in range(20)]
+    iota(PI(0), [[0, 1]], 0, 1)
+    iota(R("IOJ"), [[1, 256]])
     iota(R("IOG"), [[1, 8], [0, 16]])
     iota(R("IOM"), [[0, 8], [1, 16]])
+    iota(R("IOS"), [[16, PW]])
     iota(R("IOQ"), [[16, 8]])
-    iota(R("IOJ"), [[1, 256]])
-    iota(R("IOS"), [[16, 608]])
+    iota(R("M15"), [[0, 16], [-1, 16]], 15)
+    iota(R("K16"), [[16, 16]])
+    iota(R("SXT"), [[0, 512]], 16)
+    iota(R("QA"), [[256, 38], [0, 16]])
+    iota(R("QB"), [[0, 38], [16, 16]], 15)
+    iota(R("ONE"), [[0, 256]], 1)
+    iota(R("C255"), [[0, 128]], 255)
     for a in range(0, 4992, 1248):
         iota(R("TAB0", a, a + 1248), [[0, 1248]])
-    node("V", lambda e: g.vector.tensor_scalar(ap(PI(1)), ap(PI(0)), 15, None, A.bitwise_and), [PI(1)], [PI(0)], 94)
-    node("V", lambda e: g.vector.tensor_scalar(ap(PI(2)), ap(PI(0)), 4, None, A.arith_shift_right), [PI(2)], [PI(0)], 94)
+    iota(R("V1", 9216, 9984), [[0, 768]])
+    iota(R("V2", 9472, 9744), [[0, 272]])
+    node("V", lambda e: g.vector.tensor_scalar(ap(PI(1)), ap(PI(0)), 15, None, A.bitwise_and), [PI(1)], [PI(0)], 60)
+    vc(p_, PI(0))
     vc(r_, PI(1))
-    vc(g_, PI(2))
+    ts(g_, p_, r_, A.subtract, 1.0 / 16, A.mult)
     ts(fm, r_, 13.5, A.is_lt)
+    ts(nfm, r_, 13.5, A.is_gt)
     ts(i14, r_, 14.0, A.is_equal)
     ts(i15, r_, 15.0, A.is_equal)
     ts(r0, r_, 0.0, A.is_equal)
-    ts(hc, i14, 256.0, A.mult, i15, A.add)
+    ts(p0, p_, 0.0, A.is_equal)
+    times(hc, i14, 256.0, i15)
+    times(c15, g_, 16.0, 15.0)
+    times(c33, i14, 33.0)
+    times(cN33, i14, -33.0)
+    times(cB, r_, 16.0, 15.0)
+    times(cH, r_, 1.0, 0.5)
     for c, v in ((f32c, 32.0), (fNc, -32.0), (f16, 16.0), (fN16, -16.0)):
-        ts(c, fm, v, A.mult)
-    ts(R("BD"), R("IOG"), g_, A.is_equal)
-    fill(R("PL"), 0.0)
-    for m in range(16):
-        vc(R("PL", 128 * m + m, 128 * m + 128, 16), R("BD", m, 128, 16))
-    for p, c in (("PLH", hc), ("PLF", f32c), ("PLN", fNc)):
-        ts(R(p), R("PL"), c, A.mult)
+        times(c, fm, v)
     vc(R("POSTU", 0, 576), R("POSTI"))
-    fill(R("POSTU", 576, 608), 0)
-    vc(R("ABU", 0, 512), R("ABI", 0, 512))
-    vc(R("ABU", 512, 1024), R("ABI", 512, 1024))
-    ts(R("SLOT"), R("IOS"), r_, A.add)
+    vc(R("ABU"), R("ABI", 0, 512))
     fill(R("REC", 8192, XW), 0.0)
-    fill(R("ZER"), 0.0)
-    ts(R("BDf"), R("IOG"), g_, A.is_equal)
+    ts(R("Z1"), R("IOJ", 0, 144), c15, A.is_equal)
+    for z, c in (("ZH", hc), ("ZF", f32c), ("ZN", fNc), ("ZM", fN16)):
+        times(R(z), R("Z1"), c)
+    ts(R("BD"), R("IOG"), g_, A.is_equal)
+    either(R("BDf"), R("BD"))
     ts(R("D128"), R("IOM"), r_, A.is_equal)
-    ts(R("D16"), R("IOM", 0, 16), r_, A.is_equal)
-    ts(R("D16f"), R("IOM", 0, 16), r_, A.is_equal)
-    x = ts(B(128), R("IOM"), r_, A.is_gt)
-    tt(R("TRI"), R("BD"), x, A.mult)
-    y = tt(B(128), R("BD"), R("D128"), A.mult)
-    x = ts(B(128), R("TRI"), -256.0, A.mult)
-    tt(R("WM"), x, y, A.add)
+    either(R("D16f"), R("D128", 0, 16))
+    times(R("BIGD"), R("D128", 0, 16), BIG)
+    ts(R("I128"), R("IOJ", 0, 128), p_, A.is_equal)
+    times(R("BIGI"), R("I128"), BIG)
+    times(R("NI"), R("I128"), -1.0)
+    times(R("P0"), R("IOJ", 0, 128), 0.0, p0)
+    times(R("SLOT"), R("IOS"), 1.0, r_)
+    either(R("SLS", 576, PW), R("IOS", 576, PW))
+    x = ts(B(128), R("IOM"), r_, A.is_gt, -256.0, A.mult)
+    y = tt(B(128), x, R("D128"), A.add)
+    tt(R("WM"), y, R("BD"), A.mult)
+    x = ts(F(16), R("IOM", 0, 16), r_, A.is_lt, -256.0, A.mult)
+    tt(R("WC"), x, R("D16f"), A.add)
+    for j in range(16):
+        times(R("PLW", 128 * j, 128 * j + 128), R("I128"), R("WC", j, j + 1))
     ts(R("RL8"), R("IOQ"), 0.0, A.mult, r_, A.add)
+    vc(R("S16"), R("IOJ", 0, 16))
+    fill(R("ZER"), 0.0)
     fill(R("LV", 576, PW), 0.0)
+    fill(R("C", 576, PW), 0.0)
+    fill(R("LF", 576, 624), 0.0)
     for t in (0, 1):
-        pc = 576 + 32 * t
-        ts(CK(16 + 4 * t), r_, float(608 - pc), A.add)
-        ts(CK(17 + 4 * t), r_, float(4864 + 16 * rank - 608 * rank - pc), A.add)
-        ts(CK(18 + 4 * t), i14, float(36 + t), A.mult)
-    ts(R("CV"), R("IOJ", 0, 128), 16.0, A.add, r0, A.mult)
-    vc(R("POSTF", 0, 576), R("POSTI"))
-    fill(R("POSTF", 576, 608), 0.0)
-    ts(R("POSTF", 608, PW), R("IOJ", 0, 128), 8416.0, A.add, r0, A.mult)
-    vc(R("NLU", 0, 576), R("NEI", 0, 576))
-    fill(R("NLU", 576, 608), 0)
-    fill(R("NEI", 576, PW), 0)
-    ts(R("M30"), R("IOM", 0, 16), -2.0, A.mult, 30.0, A.add)
-    ts(R("BW"), R("BD"), f16, A.mult)
-    x = ts(F(128), R("IOM"), -1.0, A.mult, 15.0, A.add)
-    y = ts(F(128), x, i14, A.mult, fN16, A.add)
-    tt(R("CW"), y, R("BD"), A.mult)
-    ts(R("R15"), R("BD"), i15, A.mult)
-    ts(R("R15f"), R("BDf"), i15, A.mult)
-    ts(R("BDm"), R("BD"), r_, A.mult)
-    ts(R("RST"), R("IOJ", 0, 224), 0.0, A.is_gt)
-    fill(R("RST", 0, 224, 16), 0.0)
-    fill(R("ONE"), 1.0)
-    x = ts(F(8), R("IOQ"), r_, A.add)
-    ts(R("TC"), x, 16.0, A.add)
-    ts(R("TCN"), R("TC"), -4096.0, A.mult)
-    ts(R("NJC"), x, -1.0, A.mult)
-    ts(R("C", 0, 576), R("CIN"), fm, A.mult, i14, A.add)
-    ts(R("C", 576, PW), R("IOS", 0, 160), 0.0, A.mult, i14, A.add)
-    for t in (0, 1):
+        last = 576 + 16 * t
+        times(CK(24 + 4 * t), r_, 1.0, float(608 - last))
+        times(CK(25 + 4 * t), r_, 1.0, float(4864 + 16 * rank - 608 * rank - last))
+        times(CK(26 + 4 * t), i14, float(36 + t))
         fill(R("BT%d" % t, 0, 16), 512.0)
-        ts(R("HV%d" % t), R("IOJ"), i15, A.mult, CK(18 + 4 * t), A.add)
-    fill(R("K1", 576, PW), 0.0)
-    fill(R("ST", 576, PW), 0.0)
-    fill(R("C255"), 255.0)
-    ts(R("K16"), R("IOJ", 0, 16), 16.0, A.mult)
-    x = ts(F(16), R("K16"), r_, A.add)
-    ts(R("DM"), x, 8416.0, A.add)
-    ts(CK(24), r_, 8544.0, A.add)
-    fill(CK(25), -15.5)
-    fill(R("X1", 8192, XW), 0.0)
-    fill(R("X2", 8304, XW), 0.0)
+        times(R("HV%d" % t), R("IOJ"), i15, CK(26 + 4 * t))
+    times(R("CV"), R("IOJ", 0, 128), 1.0, 16.0)
+    vc(R("POSTF", 0, 576), R("POSTI"))
+    fill(R("POSTF", 576, 624), 0.0)
+    times(R("POSTF", 624, PW), R("IOJ", 0, 144), r0, times(CK(33), r0, 8416.0))
+    vc(R("NLU", 0, 576), R("NEI", 0, 576))
+    fill(R("NEI", 576, 624), 0)
+    times(R("BW"), R("BD"), f16)
+    times(R("CW"), R("BD"), fN16)
+    ns = max(NS[0] + NS[1])
+    if ns:
+        x = ts(B(128), R("IOM"), ns - 0.5, A.is_gt, -2.0, A.mult)
+        x = ts(B(128), x, 1.0, A.add)
+        tt(R("CS"), x, R("BW"), A.mult)
+    times(R("BDm"), R("BD"), r_)
+    times(R("W32"), R("BD", 0, 128, 16), f32c)
+    times(R("WN32"), R("BD", 0, 128, 16), fNc)
+    times(g2, p_, 0.5)
+    ts(R("EY"), R("IOG"), g2, A.is_equal, -256.0, A.mult)
+    ts(R("EM"), R("IOG"), times(CK(34), p_, 0.5, -0.5), A.is_equal, -1.0, A.mult)
+    ts(R("RST"), R("M15"), 14.5, A.is_lt)
+    x = times(FL(8), R("IOQ"), 1.0, r_)
+    times(R("TC"), x, 1.0, -240.0)
+    times(R("TCN"), x, -4096.0, 4096.0 * 240)
+    times(R("NJC"), x, -1.0, -16.0)
+    times(R("DM"), R("K16"), 1.0, times(CK(35), r_, 1.0, 8416.0))
+    fill(R("X1", 8304, X1W), 0.0)
 
-    KEYQ = ["q0", "q1", "q0"]
+    KEYQ = [R("q0", 0, 256), R("q1", 0, 256), R("q0", 256, 384)]
 
-    def absorb(X, Y, t, a, n):
-        tt(R(Y, a, a + n), I(R(X, 0, 8416), R("ABU", 512 * t + a // 16, 512 * t + (a + n) // 16)), R("V", a, a + n), A.max)
+    def numbers():
+        for h, (c, f) in enumerate(((8, A.arith_shift_right), (255, A.bitwise_and))):
+            x = vc(R("E", 512 * h, 512 * h + 512), ts(R("XI"), R("ABI", 512, 1024), c, f))
+            for k in range(32):
+                mm(R("q%d" % (5 + h), 16 * k, 16 * k + 16), cols(x, k % 4, 512, 4), R("I128", 16 * (k // 4), 16 * (k // 4) + 16))
+            act(R("STG", 512 * h, 512 * h + 512), R("q%d" % (5 + h)))
+        for k in range(16):
+            p, c = 16 * (k // 2) + 14 + k % 2, 512 * (k % 2) + 64 * (k // 2)
+            dma("Y", T.V2[p:p + 1, 0:8192], T.STG[:, c:c + 64], [rows(R("V2", k, 8192, 16), 1)], [R("STG", c, c + 64)], 4500)
+
+    def absorb():
+        for a in range(0, 8192, AS):
+            tt(R("X1", a, a + AS), I(R("REC", 0, 8416), R("ABU", a // 16, (a + AS) // 16)), R("V1", a, a + AS), A.max)
+        for a, b in ((0, 4096), (4096, 7168), (7168, 8192)):
+            for h in (0, 1):
+                dma("Y", T.X1[14 + h:128:16, a:b], T.V2[14 + h:128:16, a:b], [rows(R("X1", a + h, b, 2), 1)], [R("V2", a, b)], 2000)
 
     def gather(o, win, lst, a, b, e="VS"):
-        for x in range(a, b, 56):
-            y = min(b, x + 56)
+        for x in range(a, b, GS):
+            y = min(b, x + GS)
             (act if e == "S" else either)(R(o, 16 * x, 16 * y), I(win, R(lst, x, y)))
 
-    def live(c):
-        a, b = CH[0][c]
-        q = R(KEYQ[c], 0, b - a)
-        spread(q, "PLH", lambda m: R("HG", 16 * a + m, 16 * b, 16), b - a)
+    def natural(o, src, a, b, left):
+        return group(o, [(o, left(m), R(src, 16 * a + m, 16 * b, 16)) for m in range(16)])
+
+    def live(a, b):
+        q = natural(R("q4", 0, b - a), "HG", a, b, lambda m: Z("ZH", m))
         tt(R("LV", a, b), q, R("SLOT", a, b), A.is_equal)
 
-    def count(t, c, S):
-        a, b = CH[t][c]
-        n = b - a
-        q = R("q7", 0, n)
-        mm(q, R("BD"), R("LV", a, b))
-        fu = ts(B(n), q, 12.5, A.is_ge)
-        scan(R("CUM", a, b), fu, R("ZER", 0, n), R("CUM", a - 1, a) if a else 0.0, A.add, A.add)
-        le = ts(B(n), R("CUM", a, b), r_, A.is_le)
-        red(cols(S["pc"], c, c + 1), le, A.add)
+    def lists(a, b, q):
+        q = natural(q, "V1", a, b, lambda m: Z("ZH", m))
+        vc(R("LU", a, b), q)
+        either(R("LF", a, b), q)
 
-    def split(t, S):
-        last = CH[t][2][1]
-        inv = ts(F(1), R("CUM", last - 1, last), r_, A.is_le)
-        pz = red(F(1), S["pc"], A.add)
-        z = R("RZ%d" % t, 4 * rank, 4 * rank + 1)
-        ts(z, inv, CK(17 + 4 * t), A.mult, pz, A.add)
+    def count(t, S, parts):
+        acc, cum = FL(4), 0.0
+        for c, (a, b) in enumerate(parts):
+            n = b - a
+            q = mm(R("q7", 0, n), R("BD"), R("LV", a, b))
+            fu = ts(B(n), q, 12.5, A.is_ge)
+            cu = scan(B(n), fu, R("SXT", 0, n), cum, A.add, A.min)
+            cum = cols(cu, n - 1, n)
+            if c + 1 < len(parts):
+                act(B(n), cu, AF.Sign, cols(acc, c, c + 1), bias=cH, scale=-1.0)
+        x = red(F(1), cols(acc, 0, c), A.add)
+        pre = ts(FL(1), x, 0.5, A.mult, a / 2.0, A.add)
+        prz = ts(FL(1), pre, float(608 * rank), A.add)
+        le = ts(B(n), cu, r_, A.is_le)
+        kz = ts(F(1), cum, r_, A.is_le, CK(25 + 4 * t), A.mult)
+        kp = ts(F(1), cum, r_, A.is_le, CK(24 + 4 * t), A.mult)
+        pc = red(F(1), le, A.add)
+        z = ts(R("RZ%d" % t, 4 * rank, 4 * rank + 1), pc, kz, A.add, prz, A.add)
         send_all(z, "mz%d" % t, z, [R("RZ%d" % t, 4 * s, 4 * s + 1) for s in range(8) if s != rank])
-        plf = ts(F(1), inv, CK(16 + 4 * t), A.mult, pz, A.add)
-        S["pl"] = ts(U(1), plf, float(-608 * rank), A.add)
-        vc(R("LVN"), R("LV"))
-        vc(I(R("LVN"), S["pl"]), R("ZER", 0, 16))
+        S["pl"] = ts(U(1), pc, kp, A.add, pre, A.add)
 
-    def centres(t, X, S):
+    def centres(t, S):
         pl = S["pl"]
-        PS = S["PS"] = vc(FL(16), I(R("POSTF"), pl))
         LS = S["LS"] = vc(BL(16), I(R("LV"), pl))
-        mm(R("q6", 0, 16), R("TRI"), LS)
-        PSu = vc(U(16), PS)
+        XS = S["XS"] = BL(256)
+        if t == 0:
+            either(XS, I(R("X1", 0, 8192), vc(U(16), I(R("POSTF"), pl))))
+        else:
+            x1 = either(B(256), I(R("V1"), vc(U(16), I(R("SLOT"), pl))))
+            tt(XS, I(R("X1"), vc(U(16), I(R("LF"), pl))), x1, A.max)
+        oneA = relu(B(16), mm(R("q6", 0, 16), R("WM"), LS))
         EXL = tt(B(128), I(LS, R("RL8")), R("BD"), A.mult)
-        cz = ts(B(16), R("q6", 0, 16), 0.5, A.is_lt)
-        mm(R("q7", 0, 16), EXL, R("D16"))
-        oneA = tt(F(16), cz, LS, A.mult)
-        XS = vc(BL(256), I(R(X), PSu))
-        PRA = tt(F(16), oneA, PS, A.mult)
-        mm(R("q6", 16, 32), R("BDf"), PRA)
-        EXP = tt(F(128), I(PS, R("RL8")), R("BDf"), A.mult)
-        rA = vc(U(16), R("q6", 16, 32))
-        DA = tt(BL(256), I(R(X), rA), XS, A.subtract)
-        LST = vc(FL(16), R("q7", 0, 16))
-        mm(R("q7", 32, 48), EXP, R("D16f"))
-        PST = vc(F(16), R("q7", 32, 48))
-        AA = act(B(256), DA, AF.Abs)
-        spread(R("q6", 32, 48), "PLF", lambda k: cols(AA, 16 * k, 16 * k + 16), 16)
-        kb = tt(F(16), R("q6", 32, 48), R("M30"), A.add)
-        kb = tt(F(16), kb, LST, A.mult)
-        mx = red(F(1), kb, A.max)
-        OB = ts(F(16), kb, mx, A.is_equal)
-        rb = tt(F(16), OB, PST, A.mult)
-        rB = red(FL(1), rb, A.add)
-        rBu = vc(U(1), rB)
-        bt = R("BT%d" % t, 16 + 16 * rank, 32 + 16 * rank)
-        vc(bt, I(R(X), rBu))
+        q = R("q6", 16, 32)
+        group(q, [(q, rows(R("P0"), 16), rows(R("K16"), 16)), (q, R("BDm"), oneA)])
+        ra = vc(U(16), q)
+        MA = S["MA"] = tt(BL(256), I(XS, ra), vc(B(256), XS), A.max)
+        q = R("q6", 32, 48)
+        group(q, [(q, rows(R("P0"), 16), rows(R("M15", 0, 16), 16)), (q, EXL, R("BIGD"))] + [(q, Z("ZM", k), cols(XS, 16 * k, 16 * k + 16)) for k in range(16)]
+              + [(q, Z("ZF", k), cols(MA, 16 * k, 16 * k + 16)) for k in range(16)])
+        mx = red(F(1), q, A.max)
+        h = ts(IT(1), mx, 1.0 / 16, A.mult, -0.46875, A.add)
+        w = ts(F(1), mx, -1.0, A.mult, cB, A.add)
+        rb = ts(U(1), h, 16.0, A.mult, w, A.add)
+        bt = S["bt"] = vc(R("BT%d" % t, 16 + 16 * rank, 32 + 16 * rank), I(XS, rb))
         S["sent"] = send_all(bt, "mb%d" % t, bt, [R("BT%d" % t, 16 + 16 * s, 32 + 16 * s) for s in range(8) if s != rank])
-        S["XS"], S["DA"], S["LST"], S["rB"], S["bt"] = XS, DA, LST, rB, bt
-        S["dA"] = vc(FL(16), R("q6", 32, 48))
+        vc(I(R("LV"), pl), R("ZER"))
+        S["PS"] = either(FL(16), I(R("POSTF"), pl))
+        S["AV"] = cols(either(BL(256), I(XS, ra)), 0, 256, 16)
 
-    def moved(t, X, S):
-        PS, LS, XS, LST = S["PS"], S["LS"], S["XS"], S["LST"]
-        dg = ts(F(16), R("D16f"), S["rB"], A.mult)
-        mm(R("q6", 64, 80), R("BDf"), dg)
-        rb = vc(U(16), R("q6", 64, 80))
-        DB = tt(B(256), I(R(X), rb), XS, A.subtract)
-        AB = act(B(256), DB, AF.Abs)
-        spread(R("q6", 96, 112), "PLF", lambda k: cols(AB, 16 * k, 16 * k + 16), 16)
-        go = tt(F(16), R("q6", 96, 112), S["dA"], A.is_lt)
-        go = tt(B(16), go, LST, A.mult)
-        EX = tt(B(128), I(go, R("RL8")), R("BD"), A.mult)
-        mm(R("q6", 128, 144), EX, R("D16"))
-        mm(R("q6", 160, 176), R("BD"), LS)
-        goN = S["goN"] = vc(BL(16), R("q6", 128, 144))
-        made = ts(F(16), R("q6", 160, 176), 0.5, A.is_gt)
-        nf = ts(B(16), goN, -1.0, A.mult, 1.0, A.add)
-        mm(R("q6", 192, 208), R("TRI"), nf)
-        pf = tt(F(16), PS, made, A.mult)
+    def moved(t, S):
+        PS, XS, MA = S["PS"], S["XS"], S["MA"]
+        MB = tt(B(256), I(S["bt"], R("S16")), XS, A.max)
+        q = R("q6", 64, 80)
+        group(q, [(q, R("BIGI"), S["LS"]), (q, R("CW"), S["AV"]), (q, R("BW"), S["bt"])] + [(q, Z("ZF", m), cols(MA, m, 256, 16)) for m in range(16)]
+              + [(q, Z("ZN", m), cols(MB, m, 256, 16)) for m in range(16)])
+        goN = S["goN"] = ts(BL(16), q, BIG + 0.5, A.is_gt)
+        nf = ts(B(16), q, BIG + 0.5, A.is_lt)
+        FR = S["FREE"] = relu(BL(16), mm(R("q6", 96, 112), R("WM"), nf))
+        q = R("q6", 128, 144)
+        group(q, [(q, rows(R("P0"), 16), rows(R("K16"), 16)), (q, R("BDm"), FR)])
+        S["WV"] = ts(BL(16), q, i15, A.mult, CK(26 + 4 * t), A.add)
         x = tt(F(16), PS, R("DM"), A.subtract)
-        cf = ts(B(16), R("q6", 192, 208), 0.5, A.is_lt)
         x = tt(F(16), x, goN, A.mult)
-        FR = S["FREE"] = tt(BL(16), cf, nf, A.mult)
-        mm(R("q6", 224, 240), R("BDm"), FR)
         x = tt(F(16), x, R("DM"), A.add)
-        pfr = tt(F(16), pf, FR, A.mult)
-        mm(R("q6", 256, 272), R("BDf"), pfr)
-        sl = vc(U(16), x)
-        S["PNF"] = tt(FL(16), pf, pfr, A.subtract)
-        w = tt(F(16), R("q6", 224, 240), R("K16"), A.add)
-        pv = tt(F(16), R("q6", 256, 272), R("D16f"), A.mult)
-        S["WV"] = ts(BL(16), w, i15, A.mult, CK(18 + 4 * t), A.add)
-        pv = red(F(1), pv, A.add)
+        vc(I(R("REC"), vc(U(16), x)), R("HV%d" % t))
+        S["BP"] = ts(FL(16), PS, -1.0, A.mult, 9000.0, A.add)
         S["CD"] = FL(16)
-        ts(cols(S["CD"], 0, 1), pv, -1.0, A.mult, 9000.0, A.add)
-        vc(I(R("REC"), sl), R("HV%d" % t))
+        ts(cols(S["CD"], 0, 1), r_, 8544.0 - 9000.0, A.add)
+        S["tab"] = ts(FL(7), R("IOQ", 0, 7), r_, A.add, float(8192 + 112 * t - 9000), A.add)
 
     def table(t):
         zl = vc(U(8), R("RZ%d" % t, 0, 32, 4))
@@ -507,171 +566,177 @@ def rank_program(g, core, T, topo):
     def target(t, c, S):
         a, b = CH[t][c]
         n = b - a
-        spread(R("q2", 0, n), "PL", lambda m: R("HG", 16 * a + m, 16 * b, 16), n)
-        x = either(B(n), R("q2", 0, n))
-        mm(R("q3", 0, n), R("WM"), x)
-        u = ts(B(n), R("q3", 0, n), 0.0, A.max)
-        spread(R("q3", 448, 448 + n // 16), "PL", lambda m: cols(u, m, n, 16), n // 16)
-        mm(R("q3", 224, 224 + n), R("BD"), u)
-        tu = vc(U(n // 16), R("q3", 448, 448 + n // 16))
-        S["tg%d" % c] = either(BL(n), R("q3", 224, 224 + n))
-        S["b%d" % c] = act(BL(n), I(R("BT%d" % t), tu))
+        q = natural(R("q4", 0, n), "HG", a, b, lambda j: R("PLW", 128 * j, 128 * j + 128))
+        u = S["u%d" % c] = relu(BL(n), q)
+        q = R("q6", 448, 448 + n // 16)
+        group(q, [(q, Z("Z1", m), cols(u, m, n, 16)) for m in range(16)])
+        S["b%d" % c] = either(BL(n), I(R("BT%d" % t), vc(U(n // 16), q)))
 
-    def gains(t, c, S):
+    def blocks(t, c):
         a, b = CH[t][c]
-        n = b - a
-        q = R(KEYQ[c], 0, n)
-        mm(q, R("CW"), R("C", a, b), True, False)
-        act(R("q5", 0, n), R("C", a, b))
+        return [(x - a, min(b, x + 128) - a) for x in range(a, b, 128)]
+
+    def gains(t, c, S, part):
+        a, b = CH[t][c]
+        n, q, V = b - a, KEYQ[c], "V2" if t else "V1"
+        ns = NS[t][c]
+        if part == 0:
+            mm(q, rows(R("P0"), 16), rows(R("M15", 0, wide(q)), 16), True, False)
+            other, w, buf, ps = R("C", a, b), "W32", "MC%d" % (c % 2), R("q2", 0, n)
+        else:
+            other, w, buf, ps = S["b%d" % c], "WN32", "MB%d" % (c % 2), R("q3", 0, n)
+        if part or ns < 16:
+            mm(ps, R("I128"), other)
+        for x, y in blocks(t, c):
+            o = rows(cols(q, x, x + 128), y - x)
+            mm(o, cols(other, x, y), R("BW" if part else "CS" if ns else "CW"), False, False)
+            if part:
+                mm(o, R("LV", a + x, a + y), R("BIGI"), False, False)
         for m in range(16):
-            o = R("MC%d" % (c % 2), m * n, m * n + n)
-            tt(o, R("V", 16 * a + m, 16 * b, 16), R("q5", 0, n), A.max)
-            mm(q, R("PLF", 128 * m, 128 * m + 128), o, False, False)
-        act(R("q4", 0, n), S["b%d" % c])
-        mm(q, R("BW"), S["b%d" % c], False, False)
-        for m in range(16):
-            o = R("MB%d" % (c % 2), m * n, m * n + n)
-            tt(o, R("V", 16 * a + m, 16 * b, 16), R("q4", 0, n), A.max)
-            mm(q, R("PLN", 128 * m, 128 * m + 128), o, False, m == 15)
+            o = R(buf, m * n, m * n + n)
+            v = R(V, 16 * a + m, 16 * b, 16)
+            if part == 0 and m < ns:
+                d = R("q5" if m % 2 else "q6", 0, n)
+                group(d, [(d, R("NI"), other), (d, R("I128"), v)])
+                act(o, d, AF.Relu)
+            else:
+                tt(o, v, ps, A.max)
+            for x, y in blocks(t, c):
+                mm(rows(cols(q, x + m, x + 128, 16), y - x), cols(o, x, y), R(w), False, False)
+        if part:
+            mm(q, rows(R("P0"), 16), rows(R("SXT", 0, wide(q)), 16), False, True)
 
     def best(t, c, S):
         a, b = CH[t][c]
-        n = b - a
-        tt(R("K1", a, b), R(KEYQ[c], 0, n), R("LVN", a, b), A.mult)
-        kt = turn(R("KT", 0, n), R("K1", a, b))
-        sc = scan(R("SG", 0, n), R("RST", 0, n), kt, 0.0, A.mult, A.max)
-        turn(R("ST", a, b), sc)
-        of = act(B(n), R("ST", a, b), AF.Sign, bias=CK(25))
-        mm(R("q7", 0, n), R("R15"), of)
-        tg = tt(B(n), R("q7", 0, n), S["tg%d" % c], A.mult)
-        QS = [0, 1, 2, 3] if c == 2 else [0, 1, 2, 3, 4, 5, 6, 7]
-        for q in range(8):
-            o, s = R("E", q * n, q * n + n), R("SC", q * n, q * n + n)
-            if q in QS:
-                act(o, tg, AF.Abs, bias=R("TCN", q, q + 1), scale=4096.0)
-            else:
-                ts(o, tg, R("TC", q, q + 1), A.not_equal, 4096.0, A.mult)
+        n, q = b - a, KEYQ[c]
+        w = wide(q)
+        sx = scan(R("SX%d" % (c % 2), 0, w), R("RST", 0, w), q, 0.0, A.mult, A.max)
+        s8 = cols(sx, 15, w, 16)
+        W = B(w // 8)
+        ts(cols(W, 0, w // 8, 2), s8, BIG + 31.5, A.is_gt)
+        i = vc(IT(w // 16), s8)
+        i = ts(IT(w // 16), i, 15, A.bitwise_and)
+        vc(cols(W, 1, w // 8, 2), i)
+        for x, y in blocks(t, c):
+            mm(R("q7", x, y, 1, 16), cols(W, x // 8, x // 8 + 16), R("I128", 0, y - x))
+        wt = either(rows(B(n), 16), R("q7", 0, n, 1, 16))
+        q = R("q5", 0, n)
+        group(q, [(q, R("BD"), S["u%d" % c]), (q, rows(R("EY"), 16), wt)])
+        tg = either(B(n), q)
+        q = R("q7", 256, 256 + n)
+        group(q, [(q, rows(R("P0"), 16), R("QA", a, b, 1, 16)), (q, rows(R("P0"), 16), R("QB", a, b, 1, 16)), (q, rows(R("EM"), 16), wt)])
+        either(R("SLS", a, b), q)
+        for k in range(8):
+            o, s, c1, c2 = R("E", k * n, k * n + n), R("SC", k * n, k * n + n), R("TC", k, k + 1), R("TCN", k, k + 1)
+            both(o, tg, lambda o=o, c1=c1: tsc(o, tg, c1, A.not_equal, 4096.0, A.mult),
+                 lambda o=o, c2=c2: g.scalar.activation(ap(o), ap(tg), AF.Abs, bias=ap(c2), scale=4096.0), [c1, c2])
             scan(s, o, R("ONE", 0, n), 4096.0, A.min, A.subtract)
         x = ts(F(8), R("SC", n - 1, 8 * n, n), -1.0, A.mult, float(608 - b), A.add)
         S["G"] = tt(FL(8), x, S["G"], A.max)
 
-    def movers(t, X, S):
-        arr = "ARR%d" % t
+    def movers(t, S):
         ql = ts(U(8), S["G"], -1.0, A.mult, 608.0, A.add)
         val = ts(FL(8), S["G"], 0.5, A.is_gt)
-        fill(R("RV%d" % t, 4 * rank, 4 * rank + 1), 0.0)
-        send_each(lambda d: cols(val, T.rank_of(d), T.rank_of(d) + 1), "mv%d" % t, lambda d: R("RV%d" % t, 4 * rank, 4 * rank + 1),
-                  [R("RV%d" % t, 4 * s, 4 * s + 1) for s in range(8) if s != rank])
-        st = vc(F(128), I(R("ST"), ql))
-        mm(R("q7", 0, 128), R("R15f"), st)
-        k1 = vc(F(128), I(R("K1"), ql))
-        pm = vc(F(128), I(R("POSTF"), ql))
-        OB = tt(BL(128), k1, R("q7", 0, 128), A.is_equal)
-        pr = tt(F(128), OB, pm, A.mult)
-        mm(R("q7", 128, 256), R("BDf"), pr)
-        dd = tt(F(128), R("q7", 128, 256), R("D128"), A.mult)
+        send_each(lambda d: cols(val, T.rank_of(d), T.rank_of(d) + 1), "mv%d" % t, lambda d: R("RV%d" % t, place(d), place(d) + 1), [R("RV%d" % t, 0, 7)])
+        dd = tt(F(128), I(R("SLS"), ql), R("D128"), A.mult)
+        sc = scan(F(128), R("RST", 0, 128), dd, 0.0, A.mult, A.max)
+        sl = ts(U(8), cols(sc, 15, 128, 16), 9728.0, A.min)
+        MV = ts(BL(128), I(R("V2") if t else R("V1"), sl), fm, A.mult, c33, A.add)
+        arr = R("ARR1") if t else R("X1", 8192, 8304)
+        send_each(lambda d: cols(MV, 16 * T.rank_of(d), 16 * T.rank_of(d) + 16), "ma%d" % t, lambda d: cols(arr, 16 * place(d), 16 * place(d) + 16), [arr])
+        sg = either(F(128), I(R("SLS"), ql))
+        OB = tt(BL(128), I(R("SLOT"), ql), sg, A.is_equal)
+        pr = tt(F(128), I(R("POSTF"), ql), OB, A.mult)
+        dd = tt(F(128), mm(R("q7", 0, 128), R("BDf"), pr), R("D128"), A.mult)
         sc = scan(FL(128), R("RST", 0, 128), dd, 0.0, A.mult, A.max)
         idl = vc(U(8), cols(sc, 15, 128, 16))
-        MV = vc(BL(128), I(R(X), idl))
-        send_each(lambda d: cols(MV, 16 * T.rank_of(d), 16 * T.rank_of(d) + 16), "ma%d" % t,
-                  lambda d: (lambda o: R(arr, 16 * o, 16 * o + 16))(rank if rank < T.rank_of(d) else rank - 1), [R(arr)])
-        S["ql"], S["OB"], S["val"] = ql, OB, val
-        S["own"] = cols(sc, 16 * rank + 15, 16 * rank + 16)
+        S["ql"], S["OB"] = ql, OB
+        ts(cols(S["CD"], 1, 2), cols(sc, 16 * rank + 15, 16 * rank + 16), -9000.0, A.add, cols(val, rank, rank + 1), A.mult)
         vc(I(R("REC"), idl), R("C255"))
 
     def winner(t, S):
-        RV, CD = "RV%d" % t, S["CD"]
-        tab = FL(8)
-        fill(tab, 0.0)
-        for s in range(8):
-            if s != rank:
-                ts(cols(tab, s, s + 1), r_, -1.0, A.mult, float(20000 - 8192 - (7 * t + (s if s < rank else s - 1)) * 16), A.add)
-        ow = ts(F(1), S["own"], -1.0, A.mult, 30000.0, A.add)
-        tt(cols(CD, 1, 2), ow, cols(S["val"], rank, rank + 1), A.mult)
-        tt(cols(CD, 2, 10), R(RV, 0, 32, 4), tab, A.mult)
-        c = red(F(1), cols(CD, 0, 10), A.max)
-        hw = ts(F(1), c, 10000.0, A.is_gt)
-        b1 = ts(F(1), c, 20500.0, A.is_gt, 10000.0, A.mult)
-        w = ts(F(1), hw, 11000.0, A.mult, c, A.subtract)
-        w = ts(F(1), w, b1, A.add, 9000.0, A.add)
-        dg = F(32)
-        ts(cols(dg, 0, 16), R("D16f"), w, A.mult)
-        ts(cols(dg, 16, 32), R("D16f"), hw, A.mult)
-        mm(R("q7", 288, 320), R("BDf"), dg)
-        x = ts(F(1), w, CK(24), A.subtract, hw, A.mult)
-        wl = ts(U(1), x, CK(24), A.add)
-        f = tt(F(16), S["FREE"], R("q7", 288, 304), A.mult)
+        CD = S["CD"]
+        tt(cols(CD, 2, 9), R("RV%d" % t, 0, 7), S["tab"], A.mult)
+        c = red(F(1), cols(CD, 0, 9), A.min)
+        hs = mm(R("q7", 304, 320), R("BD"), ts(B(16), R("D16f"), c, A.mult, -500.0, A.is_lt))
+        FH = tt(B(16), hs, S["FREE"], A.mult)
         n = 576 + 16 * t
-        tt(R("POSTF", n, n + 16), f, S["PNF"], A.add)
         if t == 0:
-            f = tt(B(16), S["FREE"], R("q7", 304, 320), A.mult)
-            tt(R("LV", n, n + 16), f, S["goN"], A.add)
+            tt(R("LV", n, n + 16), FH, S["goN"], A.add)
+        cs = mm(R("q7", 288, 304), R("BDf"), ts(F(16), R("D16f"), c, A.mult))
+        x = tt(F(16), cs, S["BP"], A.add)
+        x = tt(F(16), x, FH, A.mult)
+        tt(R("POSTF", n, n + 16), x, S["PS"], A.add)
+        if t == 0:
             vc(R("POSTU", n, n + 16), R("POSTF", n, n + 16))
-        vc(I(R("REC"), wl), S["WV"])
+            either(R("V1", 16 * n, 16 * n + 256), I(R("X1"), R("POSTU", n, n + 16)))
+            lists(n, n + 16, R("q6", 0, 16))
+        vc(I(R("REC"), ts(U(1), c, 9000.0, A.add)), S["WV"])
 
     def update(S):
         pl = S["pl"]
-        ls = tt(B(16), S["LS"], S["goN"], A.subtract)
-        vc(I(R("LV"), pl), ls)
-        lm = vc(B(128), I(R("LV"), S["ql"]))
-        lm = tt(B(128), lm, S["OB"], A.subtract)
-        lm = ts(B(128), lm, 0.0, A.max)
-        vc(I(R("LV"), S["ql"]), lm)
-        at = tt(B(16), cols(S["DA"], 0, 256, 16), cols(S["XS"], 0, 256, 16), A.add)
-        at = ts(B(16), at, fm, A.mult, i14, A.add)
-        vc(I(R("C"), pl), at)
-        ts(R("C", 576, 592), S["bt"], fm, A.mult, i14, A.add)
+        vc(I(R("LV"), pl), tt(B(16), S["LS"], S["goN"], A.subtract))
+        vc(I(R("LV"), S["ql"]), tt(B(128), I(R("LV"), S["ql"]), S["OB"], A.subtract))
+        vc(I(R("C"), pl), S["AV"])
+        either(R("C", 576, 592), S["bt"])
         vc(R("NLU", 576, 592), I(R("NEI"), pl))
 
-    SS = [{"pc": FL(4), "G": R("NJC")}, {"pc": FL(4), "G": R("NJC")}]
+    def soon(step, *args):
+        k = len(nodes)
+        step(*args)
+        for x in nodes[k:]:
+            x["soon"] = 1e6
+
+    soon(numbers)
+    SS = [{"G": R("NJC")}, {"G": R("NJC")}]
     for t in (0, 1):
-        S, X, W = SS[t], "X2" if t else "X1", "X1" if t else "REC"
-        fill(cols(S["pc"], 3, 4), float(608 * rank))
+        S = SS[t]
         if t == 0:
-            for c in range(3):
-                gather("HG", R("REC", 0, 8192), "POSTU", CH[0][c][0], CH[0][c][1], "S")
-                live(c)
-                count(0, c, S)
-        else:
-            for c in range(3):
-                count(1, c, S)
-        split(t, S)
-        if t:
-            vc(R("X1", 8192, 8304), R("ARR0"))
-            vc(R("X2", 8192, 8304), R("ARR0"))
-            for a in (0, 4096):
-                dma("Y", T.V[:, a:a + 4096], T.X1[:, a:a + 4096], [R("V", a, a + 4096)], [R("X1", a, a + 4096)], 5500)
-        for a in range(0, 8192, 2048):
-            absorb(W, X, t, a, 2048)
-        if t == 0:
+            for a, b in CH[0]:
+                gather("HG", R("REC", 0, 8192), "POSTU", a, b, "S")
+                soon(live, a, b)
+            soon(count, 0, S, CH[0])
+            absorb()
             fill(R("REC", 8192, 8416), 255.0)
-        centres(t, X, S)
+        else:
+            soon(count, 1, S, [(0, 512), (512, 592)])
+        soon(centres, t, S)
         if t == 0:
             for a in range(0, 4992, 1248):
-                iota(R("TAB1", a, a + 1248), [[0, 1248]], 0, [S["sent"]])
-        moved(t, X, S)
-        table(t)
+                iota(R("TAB1", a, a + 1248), [[0, 1248]], 0, 0, [S["sent"]])
+        soon(table, t)
         for c in range(3):
             gather("HG", R("TAB%d" % t), "NLU", *CH[t][c])
+        for a, b in CH[t]:
+            if t == 0:
+                gather("V1", R("X1", 0, 8192), "POSTU", a, b)
+            else:
+                for x in range(a, b, GS // 2):
+                    y = min(b, x + GS // 2)
+                    tt(R("V2", 16 * x, 16 * y), I(R("X1"), R("LU", x, y)), R("V1", 16 * x, 16 * y), A.max)
         for c in range(3):
-            gather("V", R(X, 0, 8304) if t else R(X, 0, 8192), "POSTU", *CH[t][c])
+            soon(target, t, c, S)
+        moved(t, S)
+        gains(t, 0, S, 0)
+        gains(t, 1, S, 0)
         for c in range(3):
-            target(t, c, S)
-        for c in range(3):
-            gains(t, c, S)
+            gains(t, c, S, 1)
             best(t, c, S)
-        movers(t, X, S)
+            if c == 0:
+                gains(t, 2, S, 0)
+        if t == 0:
+            for a, b in CH[0]:
+                lists(a, b, R("q4", 0, b - a))
+        movers(t, S)
         if t == 0:
             update(S)
         winner(t, S)
-    dma("Y", T.ypost[:], T.POSTF[:, 0:608], [], [R("POSTF", 0, 608)], 3000)
-    for k in range(8):
-        dma("YS"[k % 2], T.yh[2 * k:2 * k + 2, :], T.REC[16 * k + 14:16 * k + 16, 0:8192], [], [R("REC", 0, 8192)], 3000)
-    y = ts(B(224), R("REC", 8192, 8416), fm, A.mult)
-    h = tt(B(224), R("REC", 8192, 8416), y, A.subtract)
-    y = B(224)
-    ts(cols(y, 0, 112), R("ARR0"), fm, A.mult)
-    ts(cols(y, 112, 224), R("ARR1"), fm, A.mult)
-    ya = tt(B(224), y, h, A.add)
-    dma("Y", T.ya[:], ap(ya), [], [ya], 2500)
+    dma("Y", T.ypost[:], T.POSTF[:, 0:608], [], [R("POSTF", 0, 608)], 2500)
+    for h in (0, 1):
+        dma("YS"[h], T.yh[h:16:2, :], T.REC[14 + h:128:16, 0:8192], [], [R("REC", 0, 8192)], 2500)
+    h = ts(B(224), R("REC", 8192, 8416), nfm, A.mult, cN33, A.add)
+    ya = B(224)
+    tt(cols(ya, 0, 112), R("X1", 8192, 8304), cols(h, 0, 112), A.add)
+    tt(cols(ya, 112, 224), R("ARR1"), cols(h, 112, 224), A.add)
+    dma("S", T.ya[:], ap(ya), [], [ya], 2500)
     emit()

@@ -9,22 +9,30 @@ BIG = 131072.0
 CH = [[(0, 256), (256, 512), (512, 576)], [(0, 256), (256, 512), (512, 592)]]
 SCRATCH = {}
 for _d, _l in [("bfloat16", "REC:8704 X1:8464 V1:9984 V2:9744 MC0:4096 MC1:4096 MB0:4096 MB1:4096 HG:9472 TAB0:4992 TAB1:4992 PLW:2048 ZH:144 Z1:144 ZF:144 ZN:144 ZM:144 "
-                "BD:128 D128:128 I128:128 BIGI:128 BIGD:16 TRI:128 WM:128 BDm:128 CW:128 CS:128 BW:128 NI:128 CV:128 EY:128 EM:128 P0:128 W32:8 WN32:8 HV0:256 HV1:256 C255:128 RST:256 ONE:256 "
-                "ZER:16 SXT:512 LV:768 C:768 BT0:144 BT1:144 ARR1:112 BA:4096 BL:5120 E:2048 SC:2048 STG:1024 QA:608 QB:608 M15:256 K16:16"),
-               ("float32", "BDf:128 If:128 D16f:16 WC:16 TC:8 TCN:8 NJC:8 DM:16 CK:64 IOJ:256 IOG:128 IOM:128 IOS:768 IOQ:8 SLOT:768 SLS:768 LF:624 "
-                "RZ0:32 RZ1:32 RV0:8 RV1:8 POSTF:768 FT:2048 FLT:768 SX0:256 SX1:256"),
-               ("int32", "PI:8 XI:512 POSTI:576 NEI:624 ABI:1024 IT:256"), ("uint16", "RL8:8 S16:16 ABU:512 POSTU:592 NLU:592 LU:592 UT:1024")]:
+                "BD:128 D128:128 I128:128 BIGI:128 BIGD:16 WM:128 BDm:128 CW:128 CS:128 BW:128 NI:128 CV:128 N128:128 R14:128 RS8:128 WQ:608 EM:128 P0:128 W32:16 WN32:8 HV0:256 HV1:256 C255:128 RST:256 ONE:256 "
+                "ZER:16 SXT:512 LV:768 C:768 BT0:144 BT1:144 ARR1:112 BA:2816 BL:4672 E:2048 STG:1024 QA:608 QB:608 M15:512 K16:16"),
+               ("float32", "BDf:128 If:128 D16f:16 WC:16 TC:8 TCN:8 NJC:8 DM:16 CK:64 IOJ:256 IOG:128 IOM:128 IOS:768 IOQ:8 SLOT:768 SLS:768 LF:768 "
+                "RZ0:32 RZ1:32 TS0:128 TS1:128 POSTF:768 FT:1152 FLT:1024 SX0:256 SX1:256"), ("float16", "SC:2048"),
+               ("int32", "PI:8 XI:512 POSTI:576 NEI:624 ABI:1024 IT:256"), ("uint16", "L15:16 RL8:8 S16:16 ABU:512 POSTU:592 NLU:592 LU:592 UT:1024")]:
     for _x in _l.split():
         SCRATCH[_x.split(":")[0]] = ("sbuf", [128, int(_x.split(":")[1])], _d)
 for _i in range(8):
     SCRATCH["q%d" % _i] = ("psum", [128, 512], "float32")
-NDMA = 38
-SEMAPHORES = ["V", "S", "P", "G", "LS"] + ["d%d" % i for i in range(NDMA)] + [m + str(t) for m in ("mz", "mb", "mv", "ma") for t in (0, 1)]
-CY, GA, SCA = 0.83, 1.3, 3.1
-EPS, WAKE, MSG, ISSUE = 150, 80, 3500, 800
+NDMA = 44
+SEMAPHORES = ["V", "S", "P", "G", "LS"] + ["d%d" % i for i in range(NDMA)] + [m + str(t) for m in ("mz", "mb", "ma") for t in (0, 1)]
+CY, GA, SCA = 0.83, 1.5, 3.1
+EPS, WAKE, MSG, ISSUE = 50, 80, 4200, 800
 FLEX = 1200
-SHORT, TURNS, KEPT = 200, 8, {}
-GS, AS = 64, 1024
+SHORT, TURNS, KEPT = 200, 6, {}
+LONG, HOLD = 400, 0.5
+ES = [1, 1]
+SUMS = [0, 0, 0]
+AHEAD = [20000, 5000, 5000, 5000, 5000, 3000, 3000, 5000, 5000, 0, 0]
+CUT, JS, SPLIT = [1024, 4096], [0, 256], False
+PV0, PV1 = "A G0 G1 G2 C00 G7 C01 N5 B00 C02 B01 B02", "U Y0 Y1 Y2 C10 J K C11 B10 C12 B11 B12"
+PS0, PS1 = "H0 H1 H2 H3 H4 H5 H6 H7 H8 G3 G4 G5 G6 N0 N1 N2 N3 N4 N6 N7 G8 N8", "W0 W1 W2 M0 M1 M2 M3 M4 M5 M6 M7 M8 M9"
+PLAN = {"V": PV0 + " " + PV1, "S": PS0 + " " + PS1}
+GS, GV, G1, NB, AS = 64, 16, 16, 64, 512
 NS = [[0, 0, 0], [0, 0, 0]]
 
 
@@ -33,7 +41,7 @@ def rank_program(g, core, T, topo):
     if rank is None:
         return
     eng = {"V": g.vector, "S": g.scalar, "P": g.tensor, "G": g, "Y": g.sync}
-    nodes, wlist, rlist, bank, top = [], {}, {}, {}, {}
+    nodes, wlist, rlist, bank, top, named = [], {}, {}, {}, {}, {}
 
     def R(name, a=0, b=None, st=1, pn=128):
         return (name, a, SCRATCH[name][1][1] if b is None else b, st, pn)
@@ -58,7 +66,7 @@ def rank_program(g, core, T, topo):
         return 16 * (r[2][2] - r[2][1]) if r[0] == "I" else (r[2] - r[1] + r[3] - 1) // r[3]
 
     def two(*rs):
-        return all([SCRATCH[r[0]][2] in ("bfloat16", "uint16") for r in rs if isinstance(r, tuple) and r[0] != "I" and wide(r) > 1])
+        return all([SCRATCH[r[0]][2] in ("bfloat16", "uint16", "float16") for r in rs if isinstance(r, tuple) and r[0] != "I" and wide(r) > 1])
 
     def meet(x, y):
         if x[1] >= y[2] or y[1] >= x[2]:
@@ -105,13 +113,24 @@ def rank_program(g, core, T, topo):
         nodes.append({"e": e, "call": call, "deps": deps, "cost": cost if isinstance(cost, dict) else {e: cost}, "lat": lat, "kind": kind, "src": src, "amount": amount})
         return k
 
+    def call(name):
+        named[name] = named.get(name, []) + [len(nodes) - 1]
+
     def schedule():
         n = len(nodes)
-        users = [[] for _ in nodes]
+        users, deps, row = [[] for _ in nodes], [set(x["deps"]) for x in nodes], set()
+        for e in PLAN:
+            ks = [k for name in PLAN[e].split() for k in named[name]]
+            for a, b in zip(ks[:-1], ks[1:]):
+                if a not in deps[b]:
+                    deps[b].add(a)
+                    row.update([(a, b), (b, a)])
+            for k in ks:
+                nodes[k]["e"] = e
         for k in range(n):
-            for d in nodes[k]["deps"]:
+            for d in deps[k]:
                 users[d].append(k)
-        gap = lambda a, b: 0 if nodes[a]["e"] == "P" and nodes[b]["e"] == "P" else WAKE
+        gap = lambda a, b: 0 if (nodes[a]["e"] == "P" and nodes[b]["e"] == "P") or (a, b) in row else WAKE
 
         def lay(before, after, where, prio, back):
             left, end, at, on = [len(x) for x in before], [0] * n, [0] * n, [None] * n
@@ -134,6 +153,25 @@ def rank_program(g, core, T, topo):
                     at[u] = t + (nodes[u]["lat"] if back else 0)
                     for e in where[u]:
                         ready[e].append(u)
+
+            def due(u, memo):
+                if left[u] == 0:
+                    return at[u]
+                if u not in memo:
+                    t = 0
+                    for d in before[u]:
+                        if end[d]:
+                            t = max(t, end[d] + gap(u, d))
+                        elif d in urgent or where[d] == "P" or nodes[d]["kind"] == "a":
+                            f = where[d][-1]
+                            t = max(t, max(due(d, memo), free[f]) + nodes[d]["cost"][f] + nodes[d]["lat"] + gap(u, d))
+                        else:
+                            t = 1e9
+                        if t >= 1e9:
+                            break
+                    memo[u] = t
+                return memo[u]
+            urgent = set([k for k in range(n) if nodes[k]["kind"] != "a" and where[k] != "P" and (nodes[k]["cost"][where[k][-1]] <= LONG or nodes[k]["kind"] == "r")]) if not back else set()
             for k in [k for k in range(n) if not before[k]]:
                 offer(k)
             while len(order) < n:
@@ -159,6 +197,17 @@ def rank_program(g, core, T, topo):
                             pick = (s, e, ok)
                 s, e, ok = pick
                 k = max(ok, key=lambda k: (prio[k], -k))
+                c = nodes[k]["cost"][e]
+                if not back and e in "VS" and c > LONG and k not in urgent:
+                    memo = {}
+                    t = min([1e9] + [due(u, memo) for u in urgent if prio[u] > prio[k] and e in where[u] and not (len(where[u]) > 1 and e == "V")])
+                    if max(s, at[k]) < t < max(s, at[k]) + c * HOLD:
+                        ok = [j for j in ok if max(s, at[j]) + nodes[j]["cost"][e] <= t + WAKE]
+                        if not ok:
+                            free[e] = t
+                            continue
+                        k = max(ok, key=lambda k: (prio[k], -k))
+                urgent.discard(k)
                 while not back and nodes[k].get("behind") in ready[e]:
                     k = nodes[k]["behind"]
                 for f in where[k]:
@@ -168,11 +217,17 @@ def rank_program(g, core, T, topo):
                 done(k, free[e] + (0 if back else nodes[k]["lat"]))
             return end, order, on
 
-        deps, where = [x["deps"] for x in nodes], [x["e"] for x in nodes]
+        where = [x["e"] for x in nodes]
         if "prio" not in KEPT:
-            prio, best = [0] * n, None
-            for k in range(n - 1, -1, -1):
-                prio[k] = min(nodes[k]["cost"].values()) + nodes[k]["lat"] + max([0] + [prio[u] + gap(k, u) for u in users[k]])
+            prio, best, left = [0] * n, None, [len(x) for x in users]
+            todo = [k for k in range(n) if not users[k]]
+            for k in todo:
+                prio[k] = nodes[k]["cost"][where[k][0]] + nodes[k]["lat"] + max([0] + [prio[u] + gap(k, u) for u in users[k]])
+                for d in deps[k]:
+                    left[d] -= 1
+                    if left[d] == 0:
+                        todo.append(d)
+            assert len(todo) == n
             for turn in range(TURNS):
                 end, order, on = lay(deps, users, where, prio, False)
                 if best is None or max(end) < best[0]:
@@ -306,23 +361,33 @@ def rank_program(g, core, T, topo):
         a = topo.addr(d)
         return DstId(rid=a[0], pnc=a[1])
 
-    lanes = [i for i in topo.engines(core, dests()[0]) if all([i in topo.engines(core, d) for d in dests()])][:8]
+    def ways(c, each):
+        j = T.cores.index(c)
+        ds = T.cores[j + 1:] + T.cores[:j]
+        far = [d for d in ds if topo.chip(d) != topo.chip(c)]
+        out = [i for i in topo.engines(c, far[0]) if all([i in topo.engines(c, d) for d in far])]
+        home = [([d], [i for i in topo.engines(c, d) if i not in out][:2]) for d in ds if d not in far]
+        if not each:
+            return [[(far, out)] + home]
+        if not SPLIT:
+            return [[([d], out[i:i + 1]) for i, d in enumerate(far)] + home]
+        return [[(far[0:1], out[0:2]), (far[1:2], out[2:4]), (far[2:3], out[4:8])] + home, [(far[3:4], out[0:4]), (far[4:5], out[4:6]), (far[5:6], out[6:8])]]
 
-    def arrive(sem, cnt, outs, sent):
-        node("G", None, outs, [], 0, MSG, "a", sem, cnt, [sent])
-
-    def send_all(src, sem, dst, lands):
-        mask = sum([1 << i for i in lanes])
-        k = node("G", lambda e: g.remote_dma_fused([RemoteDMATransfer(dst_ids=[ident(d) for d in dests()], dma_engine_mask=mask, remote_sem=T.sem[sem], srcs=[ap(src)],
-                                                                      dsts=[ap(dst) for d in dests()])], local_sem=T.sem.LS), [], [src], ISSUE, 0, "r", None, len(lanes))
-        arrive(sem, 7 * len(lanes), lands, k)
+    def send(src, sem, dst, lands, each):
+        k = None
+        for parts in ways(core, each):
+            make = lambda e, parts=parts: g.remote_dma_fused([RemoteDMATransfer(dst_ids=[ident(d) for d in ds], dma_engine_mask=sum([1 << i for i in en]), remote_sem=T.sem[sem],
+                                                                                srcs=[ap(src(ds[0]))], dsts=[ap(dst(d)) for d in ds]) for ds, en in parts], local_sem=T.sem.LS)
+            k = node("G", make, [], [src(ds[0]) for ds, en in parts], ISSUE, 0, "r", None, sum([len(en) for ds, en in parts]), [k] if k else [])
+        cnt = sum([len(en) for c in dests() for parts in ways(c, each) for ds, en in parts if core in ds])
+        node("G", None, lands, [], 0, MSG - (ISSUE if each and SPLIT else 0), "a", sem, cnt, [k])
         return k
 
+    def send_all(src, sem, dst, lands):
+        return send(lambda d: src, sem, lambda d: dst, lands, False)
+
     def send_each(src, sem, dst, lands):
-        ds = dests()
-        k = node("G", lambda e: g.remote_dma_fused([RemoteDMATransfer(dst_ids=[ident(d)], dma_engine_mask=1 << lanes[i], remote_sem=T.sem[sem], srcs=[ap(src(d))], dsts=[ap(dst(d))])
-                                                    for i, d in enumerate(ds)], local_sem=T.sem.LS), [], [src(d) for d in ds], ISSUE, 0, "r", None, len(ds))
-        arrive(sem, 7, lands, k)
+        send(src, sem, dst, lands, True)
 
     def Z(z, m):
         return R(z, 15 - m, 143 - m)
@@ -344,29 +409,30 @@ def rank_program(g, core, T, topo):
 
     dma("S", T.POSTI[:], T.post[:], [R("POSTI")], [], 2500)
     k = dma("Y", T.ABI[:], T.absorb[:], [R("ABI")], [], 2800)
-    k = dma("Y", T.V1[:, 0:1024], T.rec[:, 0:1024], [R("V1", 0, 1024)], [], 3300, k)
-    k = dma("Y", T.REC[:, 0:8192], T.rec[:], [R("REC", 0, 8192)], [], 6700, k)
-    for a, b in ((1024, 3072), (3072, 5120), (5120, 8192)):
+    k = dma("Y", T.V1[:, 0:512], T.rec[:, 0:512], [R("V1", 0, 512)], [], 3100, k)
+    k = dma("Y", T.REC[:, 0:8192], T.rec[:], [R("REC", 0, 8192)], [], 6500, k)
+    for a, b in ((512, 3072), (3072, 5120), (5120, 8192)):
         k = dma("Y", T.V1[:, a:b], T.rec[:, a:b], [R("V1", a, b)], [], 6300 + b * 0.45, k)
     k = dma("Y", T.NEI[:, 0:576], T.near[:], [R("NEI", 0, 576)], [], 10500, k)
     dma("Y", T.C[:, 0:576], T.cen[:], [R("C", 0, 576)], [], 11000, k)
 
     PI = lambda k: R("PI", k, k + 1)
     CK = lambda k: R("CK", k, k + 1)
-    r_, g_, fm, i14, i15, f32c, fNc, hc, r0, f16, fN16, p_, p0, c15, c33, cN33, nfm, cB, g2, cH = [CK(k) for k in range(20)]
+    r_, g_, fm, i14, i15, f32c, fNc, hc, r0, f16, fN16, p_, p0, c15, cM, cX, c255, cB, cT, cH = [CK(k) for k in range(20)]
     iota(PI(0), [[0, 1]], 0, 1)
     iota(R("IOJ"), [[1, 256]])
     iota(R("IOG"), [[1, 8], [0, 16]])
     iota(R("IOM"), [[0, 8], [1, 16]])
     iota(R("IOS"), [[16, PW]])
     iota(R("IOQ"), [[16, 8]])
-    iota(R("M15"), [[0, 16], [-1, 16]], 15)
+    iota(R("M15"), [[0, 32], [-1, 16]], 15)
     iota(R("K16"), [[16, 16]])
     iota(R("SXT"), [[0, 512]], 16)
     iota(R("QA"), [[256, 38], [0, 16]])
     iota(R("QB"), [[0, 38], [16, 16]], 15)
     iota(R("ONE"), [[0, 256]], 1)
-    iota(R("C255"), [[0, 128]], 255)
+    for t in (0, 1):
+        iota(R("TS%d" % t), [[1, 16], [16, 8]], 8192 + 112 * t - 16 - 9000)
     for a in range(0, 4992, 1248):
         iota(R("TAB0", a, a + 1248), [[0, 1248]])
     iota(R("V1", 9216, 9984), [[0, 768]])
@@ -376,15 +442,15 @@ def rank_program(g, core, T, topo):
     vc(r_, PI(1))
     ts(g_, p_, r_, A.subtract, 1.0 / 16, A.mult)
     ts(fm, r_, 13.5, A.is_lt)
-    ts(nfm, r_, 13.5, A.is_gt)
     ts(i14, r_, 14.0, A.is_equal)
     ts(i15, r_, 15.0, A.is_equal)
     ts(r0, r_, 0.0, A.is_equal)
     ts(p0, p_, 0.0, A.is_equal)
     times(hc, i14, 256.0, i15)
     times(c15, g_, 16.0, 15.0)
-    times(c33, i14, 33.0)
-    times(cN33, i14, -33.0)
+    times(cM, fm, 255.0, i14)
+    times(c255, fm, -255.0, 255.0)
+    fill(cT, -BIG - 31.5)
     times(cB, r_, 16.0, 15.0)
     times(cH, r_, 1.0, 0.5)
     for c, v in ((f32c, 32.0), (fNc, -32.0), (f16, 16.0), (fN16, -16.0)):
@@ -419,6 +485,7 @@ def rank_program(g, core, T, topo):
     fill(R("LV", 576, PW), 0.0)
     fill(R("C", 576, PW), 0.0)
     fill(R("LF", 576, 624), 0.0)
+    fill(R("LF", 624, PW), 8448.0)
     for t in (0, 1):
         last = 576 + 16 * t
         times(CK(24 + 4 * t), r_, 1.0, float(608 - last))
@@ -440,24 +507,35 @@ def rank_program(g, core, T, topo):
         x = ts(B(128), x, 1.0, A.add)
         tt(R("CS"), x, R("BW"), A.mult)
     times(R("BDm"), R("BD"), r_)
-    times(R("W32"), R("BD", 0, 128, 16), f32c)
+    times(R("W32", 0, 8), R("BD", 0, 128, 16), f32c)
+    times(R("W32", 8, 16), R("BD", 0, 128, 16), hc)
+    times(R("C", 0, 576), R("C", 0, 576), fm)
+    either(R("If"), R("I128"))
+    cL = times(CK(36), r_, 1.0, -256.0 - 31.0)
     times(R("WN32"), R("BD", 0, 128, 16), fNc)
-    times(g2, p_, 0.5)
-    ts(R("EY"), R("IOG"), g2, A.is_equal, -256.0, A.mult)
-    ts(R("EM"), R("IOG"), times(CK(34), p_, 0.5, -0.5), A.is_equal, -1.0, A.mult)
-    ts(R("RST"), R("M15"), 14.5, A.is_lt)
+    times(R("EM"), ts(B(128), R("IOG"), p_, A.is_equal), -1.0, ts(CK(37), p_, 7.5, A.is_gt))
+    dma("Y", T.WQ[8:9, :], T.QA[0:1, :], [rows(R("WQ", 0, 608, 2), 1)], [R("QA")], 2000)
+    dma("Y", T.WQ[9:10, :], T.QB[0:1, :], [rows(R("WQ", 1, 608, 2), 1)], [R("QB")], 2000)
+    ts(R("RST"), R("M15", 0, 256), 14.5, A.is_lt)
+    fill(R("RS8"), 1.0)
+    fill(R("RS8", 0, 128, 8), 0.0)
+    times(R("R14"), R("BD"), i14)
+    times(R("N128"), R("I128"), -128.0)
+    times(R("C255"), R("ONE", 0, 128), c255)
+    vc(R("L15"), R("QB", 0, 16))
     x = times(FL(8), R("IOQ"), 1.0, r_)
-    times(R("TC"), x, 1.0, -240.0)
-    times(R("TCN"), x, -4096.0, 4096.0 * 240)
-    times(R("NJC"), x, -1.0, -16.0)
+    times(R("TC"), x, 1.0, -112.0)
+    times(R("TCN"), x, -4096.0, 4096.0 * 112)
+    times(R("NJC"), x, 1.0, 624.0)
     times(R("DM"), R("K16"), 1.0, times(CK(35), r_, 1.0, 8416.0))
     fill(R("X1", 8304, X1W), 0.0)
 
-    KEYQ = [R("q0", 0, 256), R("q1", 0, 256), R("q0", 256, 384)]
+    def keys(t, c):
+        return R("q%d" % (c % 2), 0, 128 * (2 - t) * len(blocks(t, c)))
 
     def numbers():
         for h, (c, f) in enumerate(((8, A.arith_shift_right), (255, A.bitwise_and))):
-            x = vc(R("E", 512 * h, 512 * h + 512), ts(R("XI"), R("ABI", 512, 1024), c, f))
+            x = ts(R("E", 512 * h, 512 * h + 512), ts(R("XI"), R("ABI", 512, 1024), c, f), 1.0 - h, A.add)
             for k in range(32):
                 mm(R("q%d" % (5 + h), 16 * k, 16 * k + 16), cols(x, k % 4, 512, 4), R("I128", 16 * (k // 4), 16 * (k // 4) + 16))
             act(R("STG", 512 * h, 512 * h + 512), R("q%d" % (5 + h)))
@@ -466,34 +544,58 @@ def rank_program(g, core, T, topo):
             dma("Y", T.V2[p:p + 1, 0:8192], T.STG[:, c:c + 64], [rows(R("V2", k, 8192, 16), 1)], [R("STG", c, c + 64)], 4500)
 
     def absorb():
-        for a in range(0, 8192, AS):
-            tt(R("X1", a, a + AS), I(R("REC", 0, 8416), R("ABU", a // 16, (a + AS) // 16)), R("V1", a, a + AS), A.max)
+        larger("X1", R("REC", 0, 8416), "ABU", "V1", 0, 8192, 8192, AS, None, "A", None)
         for a, b in ((0, 4096), (4096, 7168), (7168, 8192)):
             for h in (0, 1):
                 dma("Y", T.X1[14 + h:128:16, a:b], T.V2[14 + h:128:16, a:b], [rows(R("X1", a + h, b, 2), 1)], [R("V2", a, b)], 2000)
 
+    def larger(out, win, lst, own, a, b, cut, small, via, names, banks):
+        for x in range(a, min(b, cut), small):
+            y = min(b, cut, x + small)
+            tt(R(out, x, y), I(win, R(lst, x // 16, y // 16)), R(own, x, y), A.max)
+            call(names[0])
+        for x in range(max(a, cut), b, 1024):
+            y = min(b, x + 1024)
+            u = act(via(x, y), I(win, R(lst, x // 16, y // 16)))
+            top[names] = top.get(names, -1) + 1
+            call("%s%d" % (names[1], top[names]))
+            for z in range(x, y, 512):
+                n = min(512, y - z)
+                tt(R(out, z, z + n), mm(R(banks[(z - x) // 512], 0, n), R("I128"), cols(u, z - x, z - x + n)), R(own, z, z + n), A.max)
+                call("%s%d" % (names[2], top[names]))
+
     def gather(o, win, lst, a, b, e="VS"):
         for x in range(a, b, GS):
-            y = min(b, x + GS)
-            (act if e == "S" else either)(R(o, 16 * x, 16 * y), I(win, R(lst, x, y)))
+            name = "%s%d" % (e, x // GS)
+            step = GV if name in PLAN["V"].split() else GS
+            for y in range(x, min(b, x + GS), step):
+                z = min(b, y + step)
+                either(R(o, 16 * y, 16 * z), I(win, R(lst, y, z)))
+                call(name)
 
     def natural(o, src, a, b, left):
-        return group(o, [(o, left(m), R(src, 16 * a + m, 16 * b, 16)) for m in range(16)])
+        for x in range(a, b, NB):
+            y = min(b, x + NB)
+            part = cols(o, x - a, y - a)
+            group(part, [(part, left(m), R(src, 16 * x + m, 16 * y, 16)) for m in range(16)])
+        return o
 
     def live(a, b):
         q = natural(R("q4", 0, b - a), "HG", a, b, lambda m: Z("ZH", m))
         tt(R("LV", a, b), q, R("SLOT", a, b), A.is_equal)
 
-    def lists(a, b, q):
-        q = natural(q, "V1", a, b, lambda m: Z("ZH", m))
-        vc(R("LU", a, b), q)
-        either(R("LF", a, b), q)
+    def lists(c, S):
+        a, b = CH[0][c]
+        for x, y in blocks(0, c):
+            mm(R("q4", x, y), cols(S["L%d" % c], x, x + 128), R("If", 0, y - x))
+        ts(R("LU", a, b), R("q4", 0, b - a), cL, A.add)
+        times(R("LF", a, b), R("q4", 0, b - a), 1.0, cL)
 
     def count(t, S, parts):
         acc, cum = FL(4), 0.0
         for c, (a, b) in enumerate(parts):
             n = b - a
-            q = mm(R("q7", 0, n), R("BD"), R("LV", a, b))
+            q = mm(R("q5" if t else "q7", 0, n), R("BD"), R("LV", a, b))
             fu = ts(B(n), q, 12.5, A.is_ge)
             cu = scan(B(n), fu, R("SXT", 0, n), cum, A.add, A.min)
             cum = cols(cu, n - 1, n)
@@ -554,10 +656,8 @@ def rank_program(g, core, T, topo):
         x = tt(F(16), x, goN, A.mult)
         x = tt(F(16), x, R("DM"), A.add)
         vc(I(R("REC"), vc(U(16), x)), R("HV%d" % t))
-        S["BP"] = ts(FL(16), PS, -1.0, A.mult, 9000.0, A.add)
-        S["CD"] = FL(16)
-        ts(cols(S["CD"], 0, 1), r_, 8544.0 - 9000.0, A.add)
-        S["tab"] = ts(FL(7), R("IOQ", 0, 7), r_, A.add, float(8192 + 112 * t - 9000), A.add)
+        S["BP"] = times(FL(16), PS, -1.0, 9000.0)
+        S["THR"] = times(FL(16), FR, 1e6 - 584.5, -1e6)
 
     def table(t):
         zl = vc(U(8), R("RZ%d" % t, 0, 32, 4))
@@ -578,17 +678,17 @@ def rank_program(g, core, T, topo):
 
     def gains(t, c, S, part):
         a, b = CH[t][c]
-        n, q, V = b - a, KEYQ[c], "V2" if t else "V1"
+        n, q, V, z = b - a, keys(t, c), "V2" if t else "V1", 2 - t
         ns = NS[t][c]
         if part == 0:
             mm(q, rows(R("P0"), 16), rows(R("M15", 0, wide(q)), 16), True, False)
-            other, w, buf, ps = R("C", a, b), "W32", "MC%d" % (c % 2), R("q2", 0, n)
+            other, w, buf, ps = R("C", a, b), R("W32", 0, 8 * z), "MC%d" % (c % 2), R("q2", 0, n)
         else:
-            other, w, buf, ps = S["b%d" % c], "WN32", "MB%d" % (c % 2), R("q3", 0, n)
+            other, w, buf, ps = S["b%d" % c], R("WN32"), "MB%d" % (c % 2), R("q3", 0, n)
         if part or ns < 16:
             mm(ps, R("I128"), other)
         for x, y in blocks(t, c):
-            o = rows(cols(q, x, x + 128), y - x)
+            o = rows(cols(q, z * x, z * x + 128), y - x)
             mm(o, cols(other, x, y), R("BW" if part else "CS" if ns else "CW"), False, False)
             if part:
                 mm(o, R("LV", a + x, a + y), R("BIGI"), False, False)
@@ -596,81 +696,107 @@ def rank_program(g, core, T, topo):
             o = R(buf, m * n, m * n + n)
             v = R(V, 16 * a + m, 16 * b, 16)
             if part == 0 and m < ns:
-                d = R("q5" if m % 2 else "q6", 0, n)
-                group(d, [(d, R("NI"), other), (d, R("I128"), v)])
-                act(o, d, AF.Relu)
+                if m % 2 == 0:
+                    for j in (0, 1):
+                        d = R("q5", j * n, j * n + n)
+                        group(d, [(d, R("NI"), other), (d, R("I128"), R(V, 16 * a + m + j, 16 * b, 16))])
+                    act(R(buf, m * n, m * n + 2 * n), R("q5", 0, 2 * n), AF.Relu)
+                    call("D%d%d" % (c, m // 2))
             else:
                 tt(o, v, ps, A.max)
-            for x, y in blocks(t, c):
-                mm(rows(cols(q, x + m, x + 128, 16), y - x), cols(o, x, y), R(w), False, False)
+                call("%s%d%d" % ("CB"[part], t, c))
+            sums = [(rows(cols(q, z * x + m, z * x + 16 * wide(w), 16), y - x), cols(o, x, y), w) for x, y in blocks(t, c)]
+            if part == 0 and m < ns:
+                S["late%d" % c] = S.get("late%d" % c, []) + sums
+            else:
+                late = S.get("late%d" % c, []) if part else []
+                for x in sums + late[2 * m:2 * m + 2]:
+                    mm(x[0], x[1], x[2], False, False)
+                    nodes[-1]["soon"] = SUMS[c]
         if part:
             mm(q, rows(R("P0"), 16), rows(R("SXT", 0, wide(q)), 16), False, True)
 
     def best(t, c, S):
         a, b = CH[t][c]
-        n, q = b - a, KEYQ[c]
-        w = wide(q)
-        sx = scan(R("SX%d" % (c % 2), 0, w), R("RST", 0, w), q, 0.0, A.mult, A.max)
-        s8 = cols(sx, 15, w, 16)
-        W = B(w // 8)
-        ts(cols(W, 0, w // 8, 2), s8, BIG + 31.5, A.is_gt)
-        i = vc(IT(w // 16), s8)
-        i = ts(IT(w // 16), i, 15, A.bitwise_and)
-        vc(cols(W, 1, w // 8, 2), i)
+        n, q = b - a, keys(t, c)
+        w = 128 * len(blocks(t, c))
+        sx = R("SX%d" % (c % 2), 0, w)
+        if t:
+            scan(sx, R("RST", 0, w), q, 0.0, A.mult, A.max)
+        else:
+            S["L%d" % c] = FL(w)
+            for x in range(0, w, 128):
+                scan(cols(sx, x, x + 128), R("RST", 0, 128), cols(q, 2 * x, 2 * x + 128), 0.0, A.mult, A.max)
+            for x in range(0, w, 128):
+                act(cols(S["L%d" % c], x, x + 128), cols(q, 2 * x + 128, 2 * x + 256))
+        sg = act(B(w), I(sx, R("L15", 0, w // 16)), AF.Sign, bias=cT)
+        q = R("q4" if t else "q5", 0, n)
         for x, y in blocks(t, c):
-            mm(R("q7", x, y, 1, 16), cols(W, x // 8, x // 8 + 16), R("I128", 0, y - x))
-        wt = either(rows(B(n), 16), R("q7", 0, n, 1, 16))
-        q = R("q5", 0, n)
-        group(q, [(q, R("BD"), S["u%d" % c]), (q, rows(R("EY"), 16), wt)])
-        tg = either(B(n), q)
-        q = R("q7", 256, 256 + n)
-        group(q, [(q, rows(R("P0"), 16), R("QA", a, b, 1, 16)), (q, rows(R("P0"), 16), R("QB", a, b, 1, 16)), (q, rows(R("EM"), 16), wt)])
-        either(R("SLS", a, b), q)
+            o = cols(q, x, y)
+            group(o, [(o, R("BD"), cols(S["u%d" % c], x, y)), (o, cols(sg, x, x + 128), R("N128", 0, y - x))])
+        tg = either(B(n), q) if n > 128 else q
+        i = vc(IT(w // 16), cols(sx, 15, w, 16))
+        W = vc(B(w // 16), ts(IT(w // 16), i, 15, A.bitwise_and))
+        for x, y in blocks(t, c):
+            mm(R("q7", x, y, 1, 8), cols(W, x // 16, x // 16 + 8), R("I128", 0, y - x))
+        either(R("WQ", a, b, 1, 8), R("q7", 0, n, 1, 8))
+        either(R("SLS", a, b), mm(R("q7", 256, 256 + n), rows(R("EM"), 10), R("WQ", a, b, 1, 10)))
         for k in range(8):
             o, s, c1, c2 = R("E", k * n, k * n + n), R("SC", k * n, k * n + n), R("TC", k, k + 1), R("TCN", k, k + 1)
-            both(o, tg, lambda o=o, c1=c1: tsc(o, tg, c1, A.not_equal, 4096.0, A.mult),
-                 lambda o=o, c2=c2: g.scalar.activation(ap(o), ap(tg), AF.Abs, bias=ap(c2), scale=4096.0), [c1, c2])
-            scan(s, o, R("ONE", 0, n), 4096.0, A.min, A.subtract)
-        x = ts(F(8), R("SC", n - 1, 8 * n, n), -1.0, A.mult, float(608 - b), A.add)
-        S["G"] = tt(FL(8), x, S["G"], A.max)
+            if c < ES[t]:
+                act(o, tg, AF.Abs, bias=c2, scale=4096.0)
+            elif n > 128:
+                both(o, tg, lambda o=o, c1=c1: tsc(o, tg, c1, A.not_equal, 4096.0, A.mult),
+                     lambda o=o, c2=c2: g.scalar.activation(ap(o), ap(tg), AF.Abs, bias=ap(c2), scale=4096.0), [c1, c2])
+            else:
+                ts(o, tg, c1, A.not_equal, 4096.0, A.mult)
+            scan(s, o, R("ONE", 0, n), cols(S["G"], k, k + 1), A.min, A.subtract)
+        S["G"] = R("SC", n - 1, 8 * n, n)
+        if c < 2:
+            S["G"] = vc(FL(8), S["G"])
 
     def movers(t, S):
-        ql = ts(U(8), S["G"], -1.0, A.mult, 608.0, A.add)
-        val = ts(FL(8), S["G"], 0.5, A.is_gt)
-        send_each(lambda d: cols(val, T.rank_of(d), T.rank_of(d) + 1), "mv%d" % t, lambda d: R("RV%d" % t, place(d), place(d) + 1), [R("RV%d" % t, 0, 7)])
+        ql = S["ql"] = ts(U(8), S["G"], float(CH[t][2][1]), A.add)
         dd = tt(F(128), I(R("SLS"), ql), R("D128"), A.mult)
         sc = scan(F(128), R("RST", 0, 128), dd, 0.0, A.mult, A.max)
         sl = ts(U(8), cols(sc, 15, 128, 16), 9728.0, A.min)
-        MV = ts(BL(128), I(R("V2") if t else R("V1"), sl), fm, A.mult, c33, A.add)
-        arr = R("ARR1") if t else R("X1", 8192, 8304)
+        MV = ts(BL(128), I(R("V2") if t else R("V1"), sl), cM, A.min)
+        arr = S["arr"] = R("ARR1") if t else R("X1", 8192, 8304)
         send_each(lambda d: cols(MV, 16 * T.rank_of(d), 16 * T.rank_of(d) + 16), "ma%d" % t, lambda d: cols(arr, 16 * place(d), 16 * place(d) + 16), [arr])
+
+    def left(t, S):
+        ql = S["ql"]
         sg = either(F(128), I(R("SLS"), ql))
-        OB = tt(BL(128), I(R("SLOT"), ql), sg, A.is_equal)
+        OB = S["OB"] = tt(BL(128), I(R("SLOT"), ql), sg, A.is_equal)
         pr = tt(F(128), I(R("POSTF"), ql), OB, A.mult)
-        dd = tt(F(128), mm(R("q7", 0, 128), R("BDf"), pr), R("D128"), A.mult)
-        sc = scan(FL(128), R("RST", 0, 128), dd, 0.0, A.mult, A.max)
-        idl = vc(U(8), cols(sc, 15, 128, 16))
-        S["ql"], S["OB"] = ql, OB
-        ts(cols(S["CD"], 1, 2), cols(sc, 16 * rank + 15, 16 * rank + 16), -9000.0, A.add, cols(val, rank, rank + 1), A.mult)
-        vc(I(R("REC"), idl), R("C255"))
+        q = mm(R("q7", 0, 128), R("BDf"), pr)
+        ts(R("TS%d" % t, 0, 128, 8), cols(q, 16 * rank, 16 * rank + 16), -9000.0, A.add)
+        dd = tt(F(128), q, R("D128"), A.mult)
+        sc = scan(F(128), R("RST", 0, 128), dd, 0.0, A.mult, A.max)
+        vc(I(R("REC"), vc(U(8), cols(sc, 15, 128, 16))), R("C255"))
+        if t == 0:
+            S["LP"] = either(FL(16), I(R("LF"), S["pl"]))
+            x = tt(F(128), I(R("LF"), ql), OB, A.mult)
+            S["LW"] = tt(FL(16), mm(R("q7", 256, 272), R("BDf"), cols(x, 16 * rank, 16 * rank + 16)), S["LP"], A.subtract)
 
     def winner(t, S):
-        CD = S["CD"]
-        tt(cols(CD, 2, 9), R("RV%d" % t, 0, 7), S["tab"], A.mult)
-        c = red(F(1), cols(CD, 0, 9), A.min)
-        hs = mm(R("q7", 304, 320), R("BD"), ts(B(16), R("D16f"), c, A.mult, -500.0, A.is_lt))
-        FH = tt(B(16), hs, S["FREE"], A.mult)
+        q = R("q7", 128, 256)
+        mm(cols(q, 0, 128, 8), rows(R("P0"), 16), R("ONE", 0, 16, 1, 16))
+        for o in range(7):
+            mm(cols(q, 1 + o, 128, 8), R("R14"), cols(S["arr"], 16 * o, 16 * o + 16))
+        cs = cols(scan(F(128), R("RS8"), tt(F(128), q, R("TS%d" % t), A.mult), 0.0, A.mult, A.min), 7, 128, 8)
+        FH = tt(B(16), cs, S["THR"], A.is_lt)
         n = 576 + 16 * t
         if t == 0:
             tt(R("LV", n, n + 16), FH, S["goN"], A.add)
-        cs = mm(R("q7", 288, 304), R("BDf"), ts(F(16), R("D16f"), c, A.mult))
         x = tt(F(16), cs, S["BP"], A.add)
         x = tt(F(16), x, FH, A.mult)
         tt(R("POSTF", n, n + 16), x, S["PS"], A.add)
         if t == 0:
             vc(R("POSTU", n, n + 16), R("POSTF", n, n + 16))
             either(R("V1", 16 * n, 16 * n + 256), I(R("X1"), R("POSTU", n, n + 16)))
-            lists(n, n + 16, R("q6", 0, 16))
+            vc(R("LU", n, n + 16), tt(R("LF", n, n + 16), tt(F(16), S["LW"], FH, A.mult), S["LP"], A.add))
+        c = red(F(1), tt(F(16), cs, R("D16f"), A.mult), A.add)
         vc(I(R("REC"), ts(U(1), c, 9000.0, A.add)), S["WV"])
 
     def update(S):
@@ -681,41 +807,46 @@ def rank_program(g, core, T, topo):
         either(R("C", 576, 592), S["bt"])
         vc(R("NLU", 576, 592), I(R("NEI"), pl))
 
-    def soon(step, *args):
-        k = len(nodes)
-        step(*args)
-        for x in nodes[k:]:
-            x["soon"] = 1e6
+    def soon(step, ahead):
+        def run(*args):
+            k = len(nodes)
+            step(*args)
+            for x in nodes[k:]:
+                x["soon"] = ahead
+        return run
+    numbers, live, count, centres, table, target, best, movers, winner, update, left = [
+        soon(f, a) for f, a in zip((numbers, live, count, centres, table, target, best, movers, winner, update, left), AHEAD)]
 
-    soon(numbers)
+    numbers()
     SS = [{"G": R("NJC")}, {"G": R("NJC")}]
     for t in (0, 1):
         S = SS[t]
         if t == 0:
             for a, b in CH[0]:
-                gather("HG", R("REC", 0, 8192), "POSTU", a, b, "S")
-                soon(live, a, b)
-            soon(count, 0, S, CH[0])
+                gather("HG", R("REC", 0, 8192), "POSTU", a, b, "H")
+                live(a, b)
+            count(0, S, CH[0])
             absorb()
-            fill(R("REC", 8192, 8416), 255.0)
+            times(R("REC", 8192, 8416), R("ONE", 0, 224), c255)
         else:
-            soon(count, 1, S, [(0, 512), (512, 592)])
-        soon(centres, t, S)
+            count(1, S, [(0, 512), (512, 592)])
+        centres(t, S)
         if t == 0:
             for a in range(0, 4992, 1248):
                 iota(R("TAB1", a, a + 1248), [[0, 1248]], 0, 0, [S["sent"]])
-        soon(table, t)
+        table(t)
         for c in range(3):
-            gather("HG", R("TAB%d" % t), "NLU", *CH[t][c])
-        for a, b in CH[t]:
-            if t == 0:
-                gather("V1", R("X1", 0, 8192), "POSTU", a, b)
-            else:
-                for x in range(a, b, GS // 2):
-                    y = min(b, x + GS // 2)
-                    tt(R("V2", 16 * x, 16 * y), I(R("X1"), R("LU", x, y)), R("V1", 16 * x, 16 * y), A.max)
+            gather("HG", R("TAB%d" % t), "NLU", CH[t][c][0], CH[t][c][1], "NM"[t])
+        if t == 0:
+            gather("V1", R("X1", 0, 8192), "POSTU", 0, 576, "G")
+        else:
+            a, b = CUT
+            larger("V2", R("X1"), "LU", "V1", 0, b, a, 16 * G1, lambda x, y: R("MB1", x - a, y - a), "UWY", ("q3", "q5"))
+            larger("V2", R("X1"), "LU", "V1", b, b + JS[0], 8192, JS[1], None, "I", None)
+            larger("V2", R("X1"), "LU", "V1", b + JS[0], 8192, 8192, 1024, None, "J", None)
+            larger("V2", R("X1"), "LU", "V1", 8192, 9472, 9472, 1280, None, "K", None)
         for c in range(3):
-            soon(target, t, c, S)
+            target(t, c, S)
         moved(t, S)
         gains(t, 0, S, 0)
         gains(t, 1, S, 0)
@@ -725,18 +856,19 @@ def rank_program(g, core, T, topo):
             if c == 0:
                 gains(t, 2, S, 0)
         if t == 0:
-            for a, b in CH[0]:
-                lists(a, b, R("q4", 0, b - a))
+            for c in range(3):
+                lists(c, S)
         movers(t, S)
+        left(t, S)
         if t == 0:
             update(S)
         winner(t, S)
     dma("Y", T.ypost[:], T.POSTF[:, 0:608], [], [R("POSTF", 0, 608)], 2500)
     for h in (0, 1):
         dma("YS"[h], T.yh[h:16:2, :], T.REC[14 + h:128:16, 0:8192], [], [R("REC", 0, 8192)], 2500)
-    h = ts(B(224), R("REC", 8192, 8416), nfm, A.mult, cN33, A.add)
-    ya = B(224)
-    tt(cols(ya, 0, 112), R("X1", 8192, 8304), cols(h, 0, 112), A.add)
-    tt(cols(ya, 112, 224), R("ARR1"), cols(h, 112, 224), A.add)
+    y, ya = B(224), B(224)
+    times(cols(y, 0, 112), R("X1", 8192, 8304), fm)
+    times(cols(y, 112, 224), R("ARR1"), fm)
+    tt(ya, y, R("REC", 8192, 8416), A.add)
     dma("S", T.ya[:], ap(ya), [], [ya], 2500)
     emit()

import comms_topo
from concourse.bass import DstId, RemoteDMATransfer
from concourse.mybir import AluOpType as A, AxisListType as AX, ActivationFunctionType as AF

XW = 8704
X1W = 8464
PW = 768
BIG = 131072.0
CH = [[(0, 256), (256, 512), (512, 576)], [(0, 256), (256, 512), (512, 592)]]
SCRATCH = {}
for _d, _l in [("bfloat16", "REC:8704 X1:8464 V1:9984 V2:9744 MC0:4096 MC1:4096 MB0:4096 MB1:4096 HG:9472 TAB0:4992 TAB1:4992 PLW:2048 ZH:144 Z1:144 ZF:144 ZN:144 ZM:144 "
                "BD:128 D128:128 I128:128 BIGI:128 BIGD:16 WM:128 BDm:128 CW:128 CS:128 BW:128 NI:128 CV:128 N128:128 R14:128 RS8:128 WQ:608 EM:128 P0:128 W32:16 WN32:8 HV0:256 HV1:256 C255:128 RST:256 ONE:256 "
                "ZER:16 SXT:512 LV:768 C:768 BT0:144 BT1:144 ARR1:112 BA:2816 BL:4672 E:2048 STG:1024 QA:608 QB:608 M15:512 K16:16"),
               ("float32", "BDf:128 If:128 D16f:16 WC:16 TC:8 TCN:8 NJC:8 DM:16 CK:64 IOJ:256 IOG:128 IOM:128 IOS:768 IOQ:8 SLOT:768 SLS:768 LF:768 "
                "RZ0:32 RZ1:32 TS0:128 TS1:128 POSTF:768 FT:1152 FLT:1024 SX0:256 SX1:256"), ("float16", "SC:2048"),
               ("int32", "PI:8 XI:512 POSTI:576 NEI:624 ABI:1024 IT:256"), ("uint16", "L15:16 RL8:8 S16:16 ABU:512 POSTU:592 NLU:592 LU:592 UT:1024")]:
    for _x in _l.split():
        SCRATCH[_x.split(":")[0]] = ("sbuf", [128, int(_x.split(":")[1])], _d)
for _i in range(8):
    SCRATCH["q%d" % _i] = ("psum", [128, 512], "float32")
NDMA = 44
SEMAPHORES = ["V", "S", "P", "G", "LS"] + ["d%d" % i for i in range(NDMA)] + [m + str(t) for m in ("mz", "mb", "ma") for t in (0, 1)]
CY, GA, SCA = 0.83, 1.5, 3.1
EPS, WAKE, MSG, ISSUE = 50, 80, 4200, 800
FLEX = 1200
SHORT, TURNS, KEPT = 200, 6, {}
LONG, HOLD = 400, 0.5
ES = [1, 1]
SUMS = [0, 0, 0]
AHEAD = [20000, 5000, 5000, 5000, 5000, 3000, 3000, 5000, 5000, 0, 0]
CUT, JS, SPLIT = [1024, 4096], [0, 256], False
PV0, PV1 = "A G0 G1 G2 C00 G7 C01 N5 B00 C02 B01 B02", "U Y0 Y1 Y2 C10 J K C11 B10 C12 B11 B12"
PS0, PS1 = "H0 H1 H2 H3 H4 H5 H6 H7 H8 G3 G4 G5 G6 N0 N1 N2 N3 N4 N6 N7 G8 N8", "W0 W1 W2 M0 M1 M2 M3 M4 M5 M6 M7 M8 M9"
PLAN = {"V": PV0 + " " + PV1, "S": PS0 + " " + PS1}
GS, GV, G1, NB, AS = 64, 16, 16, 64, 512
NS = [[0, 0, 0], [0, 0, 0]]


def rank_program(g, core, T, topo):
    rank = T.rank_of(core)
    if rank is None:
        return
    eng = {"V": g.vector, "S": g.scalar, "P": g.tensor, "G": g, "Y": g.sync}
    nodes, wlist, rlist, bank, top, named = [], {}, {}, {}, {}, {}

    def R(name, a=0, b=None, st=1, pn=128):
        return (name, a, SCRATCH[name][1][1] if b is None else b, st, pn)

    def I(win, off):
        return ("I", win, off)

    def cols(r, a, b, st=1):
        return (r[0], r[1] + a, r[1] + b, st, r[4])

    def rows(r, pn):
        return r[:4] + (pn,)

    def ap(r):
        if not isinstance(r, tuple):
            return r
        if r[0] == "I":
            return ap(r[1]).indirect(ap(r[2]))
        return T[r[0]][0:r[4], r[1]:r[2]] if r[3] == 1 else T[r[0]][0:r[4], r[1]:r[2]:r[3]]

    def wide(r):
        return 16 * (r[2][2] - r[2][1]) if r[0] == "I" else (r[2] - r[1] + r[3] - 1) // r[3]

    def two(*rs):
        return all([SCRATCH[r[0]][2] in ("bfloat16", "uint16", "float16") for r in rs if isinstance(r, tuple) and r[0] != "I" and wide(r) > 1])

    def meet(x, y):
        if x[1] >= y[2] or y[1] >= x[2]:
            return False
        return not (x[3] > 1 and x[3] == y[3] and (x[1] - y[1]) % x[3])

    def node(e, call, outs, ins, cost, lat=0, kind="c", src=None, amount=1, after=()):
        k = len(nodes)
        deps = set(after)
        w, rd = [], []
        for o in outs:
            if o[0] == "I":
                w.append(o[1])
                rd.append(o[2])
            else:
                w.append(o)
        for i in ins:
            if isinstance(i, tuple):
                rd += [i[1], i[2]] if i[0] == "I" else [i]
        for wr, rs in ((False, rd), (True, w)):
            for r in rs:
                b = r[0]
                if b[0] == "q":
                    old = bank.get(b, [])
                    for (j, r2, wr2, e2) in old:
                        if j != k and (e2 != e or e == "P" or len(e) > 1 or ((wr or wr2) and meet(r, r2))):
                            deps.add(j)
                    if e == "P" or (wr and all([r[1] <= x[1][1] and x[1][2] <= r[2] and r[3] == 1 for x in old])):
                        old = []
                    bank[b] = old + [(k, r, wr, e)]
                    continue
                for j, r2 in wlist.get(b, []):
                    if j != k and meet(r, r2):
                        deps.add(j)
                if wr:
                    for j, r2 in rlist.get(b, []):
                        if j != k and meet(r, r2):
                            deps.add(j)
                    for L in (wlist, rlist):
                        L[b] = [x for x in L.get(b, []) if x[0] == k or not (r[3] == 1 and r[4] == 128 and r[1] <= x[1][1] and x[1][2] <= r[2])]
                    wlist[b] = wlist[b] + [(k, r)]
                else:
                    rlist[b] = rlist.get(b, []) + [(k, r)]
        nodes.append({"e": e, "call": call, "deps": deps, "cost": cost if isinstance(cost, dict) else {e: cost}, "lat": lat, "kind": kind, "src": src, "amount": amount})
        return k

    def call(name):
        named[name] = named.get(name, []) + [len(nodes) - 1]

    def schedule():
        n = len(nodes)
        users, deps, row = [[] for _ in nodes], [set(x["deps"]) for x in nodes], set()
        for e in PLAN:
            ks = [k for name in PLAN[e].split() for k in named[name]]
            for a, b in zip(ks[:-1], ks[1:]):
                if a not in deps[b]:
                    deps[b].add(a)
                    row.update([(a, b), (b, a)])
            for k in ks:
                nodes[k]["e"] = e
        for k in range(n):
            for d in deps[k]:
                users[d].append(k)
        gap = lambda a, b: 0 if (nodes[a]["e"] == "P" and nodes[b]["e"] == "P") or (a, b) in row else WAKE

        def lay(before, after, where, prio, back):
            left, end, at, on = [len(x) for x in before], [0] * n, [0] * n, [None] * n
            prio = [p + (0 if back else x.get("soon", 0)) for p, x in zip(prio, nodes)]
            free, ready, order = {e: 0 for e in eng}, {e: [] for e in eng}, []

            def done(k, t):
                end[k] = t
                order.append(k)
                for u in after[k]:
                    left[u] -= 1
                    if left[u] == 0:
                        offer(u)

            def offer(u):
                t = max([0] + [end[d] + gap(u, d) for d in before[u]])
                if nodes[u]["kind"] == "a":
                    done(u, t + nodes[u]["lat"])
                else:
                    at[u] = t + (nodes[u]["lat"] if back else 0)
                    for e in where[u]:
                        ready[e].append(u)

            def due(u, memo):
                if left[u] == 0:
                    return at[u]
                if u not in memo:
                    t = 0
                    for d in before[u]:
                        if end[d]:
                            t = max(t, end[d] + gap(u, d))
                        elif d in urgent or where[d] == "P" or nodes[d]["kind"] == "a":
                            f = where[d][-1]
                            t = max(t, max(due(d, memo), free[f]) + nodes[d]["cost"][f] + nodes[d]["lat"] + gap(u, d))
                        else:
                            t = 1e9
                        if t >= 1e9:
                            break
                    memo[u] = t
                return memo[u]
            urgent = set([k for k in range(n) if nodes[k]["kind"] != "a" and where[k] != "P" and (nodes[k]["cost"][where[k][-1]] <= LONG or nodes[k]["kind"] == "r")]) if not back else set()
            for k in [k for k in range(n) if not before[k]]:
                offer(k)
            while len(order) < n:
                pick = None
                for e in eng:
                    if ready[e]:
                        s = max(free[e], min([at[k] for k in ready[e]]))
                        ok = [k for k in ready[e] if at[k] <= s + EPS]
                        if e == "V" and not back:
                            own = [k for k in ok if len(where[k]) == 1]
                            best = max(ok, key=lambda k: prio[k])
                            if len(where[best]) > 1 and nodes[best]["cost"]["V"] < SHORT and free["S"] > s + SHORT:
                                ok = [best]
                            elif own:
                                ok = own
                            elif free["S"] + sum([nodes[k]["cost"]["S"] for k in ready["S"] if at[k] <= s + EPS]) - s < FLEX:
                                later = [k for k in ready[e] if len(where[k]) == 1]
                                if not later:
                                    continue
                                s = max(free[e], min([at[k] for k in later]))
                                ok = [k for k in later if at[k] <= s + EPS]
                        if pick is None or s < pick[0]:
                            pick = (s, e, ok)
                s, e, ok = pick
                k = max(ok, key=lambda k: (prio[k], -k))
                c = nodes[k]["cost"][e]
                if not back and e in "VS" and c > LONG and k not in urgent:
                    memo = {}
                    t = min([1e9] + [due(u, memo) for u in urgent if prio[u] > prio[k] and e in where[u] and not (len(where[u]) > 1 and e == "V")])
                    if max(s, at[k]) < t < max(s, at[k]) + c * HOLD:
                        ok = [j for j in ok if max(s, at[j]) + nodes[j]["cost"][e] <= t + WAKE]
                        if not ok:
                            free[e] = t
                            continue
                        k = max(ok, key=lambda k: (prio[k], -k))
                urgent.discard(k)
                while not back and nodes[k].get("behind") in ready[e]:
                    k = nodes[k]["behind"]
                for f in where[k]:
                    ready[f].remove(k)
                on[k] = e
                free[e] = max(free[e], at[k]) + nodes[k]["cost"][e]
                done(k, free[e] + (0 if back else nodes[k]["lat"]))
            return end, order, on

        where = [x["e"] for x in nodes]
        if "prio" not in KEPT:
            prio, best, left = [0] * n, None, [len(x) for x in users]
            todo = [k for k in range(n) if not users[k]]
            for k in todo:
                prio[k] = nodes[k]["cost"][where[k][0]] + nodes[k]["lat"] + max([0] + [prio[u] + gap(k, u) for u in users[k]])
                for d in deps[k]:
                    left[d] -= 1
                    if left[d] == 0:
                        todo.append(d)
            assert len(todo) == n
            for turn in range(TURNS):
                end, order, on = lay(deps, users, where, prio, False)
                if best is None or max(end) < best[0]:
                    best = (max(end), prio)
                prio = lay(users, deps, on, end, True)[0]
            KEPT["prio"], KEPT["end"] = best[1], best[0]
        end, order, on = lay(deps, users, where, KEPT["prio"], False)
        for k in range(n):
            nodes[k]["e"] = on[k] or nodes[k]["e"]
        return order

    def emit():
        seq, know, clocks, total = {}, {e: {} for e in eng}, {}, {}
        for k in schedule():
            x = nodes[k]
            if x["kind"] == "a":
                x["num"], x["amt"], clocks[(x["src"], 1)] = 1, x["amount"], {}
                total[x["src"]] = x["amount"]
                continue
            e = x["e"]
            need = {}
            for d in x["deps"]:
                y = nodes[d]
                if y["kind"] == "r" or (e == "P" and y["e"] == "P"):
                    continue
                need[y["src"]] = max(need.get(y["src"], (0, 0)), (y["num"], y["num"] * y["amt"]))
            for s, (num, val) in sorted(need.items()):
                if know[e].get(s, 0) < num:
                    eng[e].wait_ge(T.sem[s], val)
                    for c, v in clocks[(s, num)].items():
                        know[e][c] = max(know[e].get(c, 0), v)
                    know[e][s] = num
            if x["kind"] == "r":
                x["call"](e)
                total["LS"] = total.get("LS", 0) + x["amount"]
                continue
            if x["kind"] == "c":
                x["src"] = e
                seq[e] = seq.get(e, 0) + 1
                x["num"], x["amt"] = seq[e], 1
            else:
                x["num"], x["amt"] = 1, 16
            x["call"](e).then_inc(T.sem[x["src"]], x["amt"])
            total[x["src"]] = x["num"] * x["amt"]
            clocks[(x["src"], x["num"])] = dict(know[e])
            clocks[(x["src"], x["num"])][x["src"]] = x["num"]
        for s, v in sorted(total.items()):
            g.wait_ge(T.sem[s], v)

    def vcost(o, i, f):
        if o[0] == "I":
            return 50 + SCA * wide(i)
        return 50 + GA * wide(o) if i[0] == "I" else max(64, max(wide(o), wide(i)) * f) * CY

    def scost(o, i):
        return 65 + wide(o) * (GA if i[0] == "I" else CY)

    def fill(o, c):
        node("V", lambda e: g.vector.memset(ap(o), c), [o], [], vcost(o, o, 0.5 if two(o) else 1))

    def vc(o, i):
        node("V", lambda e: g.vector.tensor_copy(ap(o), ap(i)), [o], [i], vcost(o, i, 0.5 if two(o, i) else 1))
        return o

    def tt(o, a, b, f):
        node("V", lambda e: g.vector.tensor_tensor(ap(o), ap(a), ap(b), f), [o], [a, b], vcost(o, a, 1 if "q" in (a[0][0], b[0][0]) else 2))
        return o

    def tsc(o, a, s1, f1, s2, f2):
        if f2 is None:
            return g.vector.tensor_scalar(ap(o), ap(a), ap(s1), None, f1)
        return g.vector.tensor_scalar(ap(o), ap(a), ap(s1), ap(s2), f1, f2)

    def ts(o, a, s1, f1, s2=None, f2=None):
        node("V", lambda e: tsc(o, a, s1, f1, s2, f2), [o], [a, s1, s2], vcost(o, a, 0.5 if two(o, a) else 1))
        return o

    def red(o, i, f):
        node("V", lambda e: g.vector.tensor_reduce(ap(o), ap(i), AX.X, f), [o], [i], vcost(o, i, 1))
        return o

    def scan(o, a, b, init, f0, f1):
        node("V", lambda e: g.vector.tensor_tensor_scan(ap(o), ap(a), ap(b), ap(init), f0, f1), [o], [a, b, init], vcost(o, a, 0.5 if two(o, a, b) else 1))
        return o

    def act(o, i, f=AF.Copy, acc=None, **kw):
        k2 = {k: ap(v) for k, v in kw.items()}
        if acc:
            k2["accum_out"] = ap(acc)
        node("S", lambda e: g.scalar.activation(ap(o), ap(i), f, **k2), [o] + ([acc] if acc else []), [i] + list(kw.values()), scost(o, i))
        return o

    def both(o, i, fv, fs, more=()):
        node("VS", lambda e: fv() if e == "V" else fs(), [o], [i] + list(more), {"V": vcost(o, i, 0.5 if two(o, i) else 1), "S": scost(o, i)})
        return o

    def either(o, i):
        return both(o, i, lambda: g.vector.tensor_copy(ap(o), ap(i)), lambda: g.scalar.activation(ap(o), ap(i), AF.Copy))

    def relu(o, i):
        return both(o, i, lambda: tsc(o, i, 0.0, A.max, None, None), lambda: g.scalar.activation(ap(o), ap(i), AF.Relu))

    def times(o, i, c, d=0.0):
        return both(o, i, lambda: tsc(o, i, c, A.mult, d, A.add),
                    lambda: g.scalar.activation(ap(o), ap(i), AF.Identity if isinstance(d, tuple) else AF.Copy, scale=ap(c), bias=ap(d)), [c, d])

    def mm(o, l, r, start=True, stop=True):
        node("P", lambda e: g.tensor.matmul(ap(o), ap(l), ap(r), start, stop), [o], [l, r], max(min(64, wide(l)), wide(o)) * CY * (1 if two(l) else 4))
        return o

    def group(o, terms):
        for j, (x, l, r) in enumerate(terms):
            mm(x, l, r, j == 0, j == len(terms) - 1)
        return o

    def iota(o, pat, base=0, mult=0, after=()):
        kw = {} if SCRATCH[o[0]][2] == "int32" else {"allow_small_or_imprecise_dtypes": True}
        return node("G", lambda e: g.iota(ap(o), pat, base, mult, **kw), [o], [], 130 + 2 * CY * wide(o), 0, "c", None, 1, after)

    def dma(e, out, in_, outs, ins, lat, behind=None):
        src = "d%d" % top.get("d", 0)
        top["d"] = top.get("d", 0) + 1
        k = node(e, lambda e: eng[e].dma_start(out, in_), outs, ins, 60, lat, "d", src)
        nodes[k]["behind"] = behind
        return k

    def dests():
        return [d for d in T.cores if d != core]

    def ident(d):
        a = topo.addr(d)
        return DstId(rid=a[0], pnc=a[1])

    def ways(c, each):
        j = T.cores.index(c)
        ds = T.cores[j + 1:] + T.cores[:j]
        far = [d for d in ds if topo.chip(d) != topo.chip(c)]
        out = [i for i in topo.engines(c, far[0]) if all([i in topo.engines(c, d) for d in far])]
        home = [([d], [i for i in topo.engines(c, d) if i not in out][:2]) for d in ds if d not in far]
        if not each:
            return [[(far, out)] + home]
        if not SPLIT:
            return [[([d], out[i:i + 1]) for i, d in enumerate(far)] + home]
        return [[(far[0:1], out[0:2]), (far[1:2], out[2:4]), (far[2:3], out[4:8])] + home, [(far[3:4], out[0:4]), (far[4:5], out[4:6]), (far[5:6], out[6:8])]]

    def send(src, sem, dst, lands, each):
        k = None
        for parts in ways(core, each):
            make = lambda e, parts=parts: g.remote_dma_fused([RemoteDMATransfer(dst_ids=[ident(d) for d in ds], dma_engine_mask=sum([1 << i for i in en]), remote_sem=T.sem[sem],
                                                                                srcs=[ap(src(ds[0]))], dsts=[ap(dst(d)) for d in ds]) for ds, en in parts], local_sem=T.sem.LS)
            k = node("G", make, [], [src(ds[0]) for ds, en in parts], ISSUE, 0, "r", None, sum([len(en) for ds, en in parts]), [k] if k else [])
        cnt = sum([len(en) for c in dests() for parts in ways(c, each) for ds, en in parts if core in ds])
        node("G", None, lands, [], 0, MSG - (ISSUE if each and SPLIT else 0), "a", sem, cnt, [k])
        return k

    def send_all(src, sem, dst, lands):
        return send(lambda d: src, sem, lambda d: dst, lands, False)

    def send_each(src, sem, dst, lands):
        send(src, sem, dst, lands, True)

    def Z(z, m):
        return R(z, 15 - m, 143 - m)

    def place(d):
        return rank if rank < T.rank_of(d) else rank - 1

    def arena(name, ring):
        def new(n):
            w = (n + 15) // 16 * 16
            a = top.get(name, 0)
            if a + w > SCRATCH[name][1][1]:
                assert ring, name
                a = 0
            top[name] = a + w
            return R(name, a, a + n)
        return new
    F, B, U, FL, BL, IT = arena("FT", True), arena("BA", True), arena("UT", False), arena("FLT", False), arena("BL", False), arena("IT", True)

    dma("S", T.POSTI[:], T.post[:], [R("POSTI")], [], 2500)
    k = dma("Y", T.ABI[:], T.absorb[:], [R("ABI")], [], 2800)
    k = dma("Y", T.V1[:, 0:512], T.rec[:, 0:512], [R("V1", 0, 512)], [], 3100, k)
    k = dma("Y", T.REC[:, 0:8192], T.rec[:], [R("REC", 0, 8192)], [], 6500, k)
    for a, b in ((512, 3072), (3072, 5120), (5120, 8192)):
        k = dma("Y", T.V1[:, a:b], T.rec[:, a:b], [R("V1", a, b)], [], 6300 + b * 0.45, k)
    k = dma("Y", T.NEI[:, 0:576], T.near[:], [R("NEI", 0, 576)], [], 10500, k)
    dma("Y", T.C[:, 0:576], T.cen[:], [R("C", 0, 576)], [], 11000, k)

    PI = lambda k: R("PI", k, k + 1)
    CK = lambda k: R("CK", k, k + 1)
    r_, g_, fm, i14, i15, f32c, fNc, hc, r0, f16, fN16, p_, p0, c15, cM, cX, c255, cB, cT, cH = [CK(k) for k in range(20)]
    iota(PI(0), [[0, 1]], 0, 1)
    iota(R("IOJ"), [[1, 256]])
    iota(R("IOG"), [[1, 8], [0, 16]])
    iota(R("IOM"), [[0, 8], [1, 16]])
    iota(R("IOS"), [[16, PW]])
    iota(R("IOQ"), [[16, 8]])
    iota(R("M15"), [[0, 32], [-1, 16]], 15)
    iota(R("K16"), [[16, 16]])
    iota(R("SXT"), [[0, 512]], 16)
    iota(R("QA"), [[256, 38], [0, 16]])
    iota(R("QB"), [[0, 38], [16, 16]], 15)
    iota(R("ONE"), [[0, 256]], 1)
    for t in (0, 1):
        iota(R("TS%d" % t), [[1, 16], [16, 8]], 8192 + 112 * t - 16 - 9000)
    for a in range(0, 4992, 1248):
        iota(R("TAB0", a, a + 1248), [[0, 1248]])
    iota(R("V1", 9216, 9984), [[0, 768]])
    iota(R("V2", 9472, 9744), [[0, 272]])
    node("V", lambda e: g.vector.tensor_scalar(ap(PI(1)), ap(PI(0)), 15, None, A.bitwise_and), [PI(1)], [PI(0)], 60)
    vc(p_, PI(0))
    vc(r_, PI(1))
    ts(g_, p_, r_, A.subtract, 1.0 / 16, A.mult)
    ts(fm, r_, 13.5, A.is_lt)
    ts(i14, r_, 14.0, A.is_equal)
    ts(i15, r_, 15.0, A.is_equal)
    ts(r0, r_, 0.0, A.is_equal)
    ts(p0, p_, 0.0, A.is_equal)
    times(hc, i14, 256.0, i15)
    times(c15, g_, 16.0, 15.0)
    times(cM, fm, 255.0, i14)
    times(c255, fm, -255.0, 255.0)
    fill(cT, -BIG - 31.5)
    times(cB, r_, 16.0, 15.0)
    times(cH, r_, 1.0, 0.5)
    for c, v in ((f32c, 32.0), (fNc, -32.0), (f16, 16.0), (fN16, -16.0)):
        times(c, fm, v)
    vc(R("POSTU", 0, 576), R("POSTI"))
    vc(R("ABU"), R("ABI", 0, 512))
    fill(R("REC", 8192, XW), 0.0)
    ts(R("Z1"), R("IOJ", 0, 144), c15, A.is_equal)
    for z, c in (("ZH", hc), ("ZF", f32c), ("ZN", fNc), ("ZM", fN16)):
        times(R(z), R("Z1"), c)
    ts(R("BD"), R("IOG"), g_, A.is_equal)
    either(R("BDf"), R("BD"))
    ts(R("D128"), R("IOM"), r_, A.is_equal)
    either(R("D16f"), R("D128", 0, 16))
    times(R("BIGD"), R("D128", 0, 16), BIG)
    ts(R("I128"), R("IOJ", 0, 128), p_, A.is_equal)
    times(R("BIGI"), R("I128"), BIG)
    times(R("NI"), R("I128"), -1.0)
    times(R("P0"), R("IOJ", 0, 128), 0.0, p0)
    times(R("SLOT"), R("IOS"), 1.0, r_)
    either(R("SLS", 576, PW), R("IOS", 576, PW))
    x = ts(B(128), R("IOM"), r_, A.is_gt, -256.0, A.mult)
    y = tt(B(128), x, R("D128"), A.add)
    tt(R("WM"), y, R("BD"), A.mult)
    x = ts(F(16), R("IOM", 0, 16), r_, A.is_lt, -256.0, A.mult)
    tt(R("WC"), x, R("D16f"), A.add)
    for j in range(16):
        times(R("PLW", 128 * j, 128 * j + 128), R("I128"), R("WC", j, j + 1))
    ts(R("RL8"), R("IOQ"), 0.0, A.mult, r_, A.add)
    vc(R("S16"), R("IOJ", 0, 16))
    fill(R("ZER"), 0.0)
    fill(R("LV", 576, PW), 0.0)
    fill(R("C", 576, PW), 0.0)
    fill(R("LF", 576, 624), 0.0)
    fill(R("LF", 624, PW), 8448.0)
    for t in (0, 1):
        last = 576 + 16 * t
        times(CK(24 + 4 * t), r_, 1.0, float(608 - last))
        times(CK(25 + 4 * t), r_, 1.0, float(4864 + 16 * rank - 608 * rank - last))
        times(CK(26 + 4 * t), i14, float(36 + t))
        fill(R("BT%d" % t, 0, 16), 512.0)
        times(R("HV%d" % t), R("IOJ"), i15, CK(26 + 4 * t))
    times(R("CV"), R("IOJ", 0, 128), 1.0, 16.0)
    vc(R("POSTF", 0, 576), R("POSTI"))
    fill(R("POSTF", 576, 624), 0.0)
    times(R("POSTF", 624, PW), R("IOJ", 0, 144), r0, times(CK(33), r0, 8416.0))
    vc(R("NLU", 0, 576), R("NEI", 0, 576))
    fill(R("NEI", 576, 624), 0)
    times(R("BW"), R("BD"), f16)
    times(R("CW"), R("BD"), fN16)
    ns = max(NS[0] + NS[1])
    if ns:
        x = ts(B(128), R("IOM"), ns - 0.5, A.is_gt, -2.0, A.mult)
        x = ts(B(128), x, 1.0, A.add)
        tt(R("CS"), x, R("BW"), A.mult)
    times(R("BDm"), R("BD"), r_)
    times(R("W32", 0, 8), R("BD", 0, 128, 16), f32c)
    times(R("W32", 8, 16), R("BD", 0, 128, 16), hc)
    times(R("C", 0, 576), R("C", 0, 576), fm)
    either(R("If"), R("I128"))
    cL = times(CK(36), r_, 1.0, -256.0 - 31.0)
    times(R("WN32"), R("BD", 0, 128, 16), fNc)
    times(R("EM"), ts(B(128), R("IOG"), p_, A.is_equal), -1.0, ts(CK(37), p_, 7.5, A.is_gt))
    dma("Y", T.WQ[8:9, :], T.QA[0:1, :], [rows(R("WQ", 0, 608, 2), 1)], [R("QA")], 2000)
    dma("Y", T.WQ[9:10, :], T.QB[0:1, :], [rows(R("WQ", 1, 608, 2), 1)], [R("QB")], 2000)
    ts(R("RST"), R("M15", 0, 256), 14.5, A.is_lt)
    fill(R("RS8"), 1.0)
    fill(R("RS8", 0, 128, 8), 0.0)
    times(R("R14"), R("BD"), i14)
    times(R("N128"), R("I128"), -128.0)
    times(R("C255"), R("ONE", 0, 128), c255)
    vc(R("L15"), R("QB", 0, 16))
    x = times(FL(8), R("IOQ"), 1.0, r_)
    times(R("TC"), x, 1.0, -112.0)
    times(R("TCN"), x, -4096.0, 4096.0 * 112)
    times(R("NJC"), x, 1.0, 624.0)
    times(R("DM"), R("K16"), 1.0, times(CK(35), r_, 1.0, 8416.0))
    fill(R("X1", 8304, X1W), 0.0)

    def keys(t, c):
        return R("q%d" % (c % 2), 0, 128 * (2 - t) * len(blocks(t, c)))

    def numbers():
        for h, (c, f) in enumerate(((8, A.arith_shift_right), (255, A.bitwise_and))):
            x = ts(R("E", 512 * h, 512 * h + 512), ts(R("XI"), R("ABI", 512, 1024), c, f), 1.0 - h, A.add)
            for k in range(32):
                mm(R("q%d" % (5 + h), 16 * k, 16 * k + 16), cols(x, k % 4, 512, 4), R("I128", 16 * (k // 4), 16 * (k // 4) + 16))
            act(R("STG", 512 * h, 512 * h + 512), R("q%d" % (5 + h)))
        for k in range(16):
            p, c = 16 * (k // 2) + 14 + k % 2, 512 * (k % 2) + 64 * (k // 2)
            dma("Y", T.V2[p:p + 1, 0:8192], T.STG[:, c:c + 64], [rows(R("V2", k, 8192, 16), 1)], [R("STG", c, c + 64)], 4500)

    def absorb():
        larger("X1", R("REC", 0, 8416), "ABU", "V1", 0, 8192, 8192, AS, None, "A", None)
        for a, b in ((0, 4096), (4096, 7168), (7168, 8192)):
            for h in (0, 1):
                dma("Y", T.X1[14 + h:128:16, a:b], T.V2[14 + h:128:16, a:b], [rows(R("X1", a + h, b, 2), 1)], [R("V2", a, b)], 2000)

    def larger(out, win, lst, own, a, b, cut, small, via, names, banks):
        for x in range(a, min(b, cut), small):
            y = min(b, cut, x + small)
            tt(R(out, x, y), I(win, R(lst, x // 16, y // 16)), R(own, x, y), A.max)
            call(names[0])
        for x in range(max(a, cut), b, 1024):
            y = min(b, x + 1024)
            u = act(via(x, y), I(win, R(lst, x // 16, y // 16)))
            top[names] = top.get(names, -1) + 1
            call("%s%d" % (names[1], top[names]))
            for z in range(x, y, 512):
                n = min(512, y - z)
                tt(R(out, z, z + n), mm(R(banks[(z - x) // 512], 0, n), R("I128"), cols(u, z - x, z - x + n)), R(own, z, z + n), A.max)
                call("%s%d" % (names[2], top[names]))

    def gather(o, win, lst, a, b, e="VS"):
        for x in range(a, b, GS):
            name = "%s%d" % (e, x // GS)
            step = GV if name in PLAN["V"].split() else GS
            for y in range(x, min(b, x + GS), step):
                z = min(b, y + step)
                either(R(o, 16 * y, 16 * z), I(win, R(lst, y, z)))
                call(name)

    def natural(o, src, a, b, left):
        for x in range(a, b, NB):
            y = min(b, x + NB)
            part = cols(o, x - a, y - a)
            group(part, [(part, left(m), R(src, 16 * x + m, 16 * y, 16)) for m in range(16)])
        return o

    def live(a, b):
        q = natural(R("q4", 0, b - a), "HG", a, b, lambda m: Z("ZH", m))
        tt(R("LV", a, b), q, R("SLOT", a, b), A.is_equal)

    def lists(c, S):
        a, b = CH[0][c]
        for x, y in blocks(0, c):
            mm(R("q4", x, y), cols(S["L%d" % c], x, x + 128), R("If", 0, y - x))
        ts(R("LU", a, b), R("q4", 0, b - a), cL, A.add)
        times(R("LF", a, b), R("q4", 0, b - a), 1.0, cL)

    def count(t, S, parts):
        acc, cum = FL(4), 0.0
        for c, (a, b) in enumerate(parts):
            n = b - a
            q = mm(R("q5" if t else "q7", 0, n), R("BD"), R("LV", a, b))
            fu = ts(B(n), q, 12.5, A.is_ge)
            cu = scan(B(n), fu, R("SXT", 0, n), cum, A.add, A.min)
            cum = cols(cu, n - 1, n)
            if c + 1 < len(parts):
                act(B(n), cu, AF.Sign, cols(acc, c, c + 1), bias=cH, scale=-1.0)
        x = red(F(1), cols(acc, 0, c), A.add)
        pre = ts(FL(1), x, 0.5, A.mult, a / 2.0, A.add)
        prz = ts(FL(1), pre, float(608 * rank), A.add)
        le = ts(B(n), cu, r_, A.is_le)
        kz = ts(F(1), cum, r_, A.is_le, CK(25 + 4 * t), A.mult)
        kp = ts(F(1), cum, r_, A.is_le, CK(24 + 4 * t), A.mult)
        pc = red(F(1), le, A.add)
        z = ts(R("RZ%d" % t, 4 * rank, 4 * rank + 1), pc, kz, A.add, prz, A.add)
        send_all(z, "mz%d" % t, z, [R("RZ%d" % t, 4 * s, 4 * s + 1) for s in range(8) if s != rank])
        S["pl"] = ts(U(1), pc, kp, A.add, pre, A.add)

    def centres(t, S):
        pl = S["pl"]
        LS = S["LS"] = vc(BL(16), I(R("LV"), pl))
        XS = S["XS"] = BL(256)
        if t == 0:
            either(XS, I(R("X1", 0, 8192), vc(U(16), I(R("POSTF"), pl))))
        else:
            x1 = either(B(256), I(R("V1"), vc(U(16), I(R("SLOT"), pl))))
            tt(XS, I(R("X1"), vc(U(16), I(R("LF"), pl))), x1, A.max)
        oneA = relu(B(16), mm(R("q6", 0, 16), R("WM"), LS))
        EXL = tt(B(128), I(LS, R("RL8")), R("BD"), A.mult)
        q = R("q6", 16, 32)
        group(q, [(q, rows(R("P0"), 16), rows(R("K16"), 16)), (q, R("BDm"), oneA)])
        ra = vc(U(16), q)
        MA = S["MA"] = tt(BL(256), I(XS, ra), vc(B(256), XS), A.max)
        q = R("q6", 32, 48)
        group(q, [(q, rows(R("P0"), 16), rows(R("M15", 0, 16), 16)), (q, EXL, R("BIGD"))] + [(q, Z("ZM", k), cols(XS, 16 * k, 16 * k + 16)) for k in range(16)]
              + [(q, Z("ZF", k), cols(MA, 16 * k, 16 * k + 16)) for k in range(16)])
        mx = red(F(1), q, A.max)
        h = ts(IT(1), mx, 1.0 / 16, A.mult, -0.46875, A.add)
        w = ts(F(1), mx, -1.0, A.mult, cB, A.add)
        rb = ts(U(1), h, 16.0, A.mult, w, A.add)
        bt = S["bt"] = vc(R("BT%d" % t, 16 + 16 * rank, 32 + 16 * rank), I(XS, rb))
        S["sent"] = send_all(bt, "mb%d" % t, bt, [R("BT%d" % t, 16 + 16 * s, 32 + 16 * s) for s in range(8) if s != rank])
        vc(I(R("LV"), pl), R("ZER"))
        S["PS"] = either(FL(16), I(R("POSTF"), pl))
        S["AV"] = cols(either(BL(256), I(XS, ra)), 0, 256, 16)

    def moved(t, S):
        PS, XS, MA = S["PS"], S["XS"], S["MA"]
        MB = tt(B(256), I(S["bt"], R("S16")), XS, A.max)
        q = R("q6", 64, 80)
        group(q, [(q, R("BIGI"), S["LS"]), (q, R("CW"), S["AV"]), (q, R("BW"), S["bt"])] + [(q, Z("ZF", m), cols(MA, m, 256, 16)) for m in range(16)]
              + [(q, Z("ZN", m), cols(MB, m, 256, 16)) for m in range(16)])
        goN = S["goN"] = ts(BL(16), q, BIG + 0.5, A.is_gt)
        nf = ts(B(16), q, BIG + 0.5, A.is_lt)
        FR = S["FREE"] = relu(BL(16), mm(R("q6", 96, 112), R("WM"), nf))
        q = R("q6", 128, 144)
        group(q, [(q, rows(R("P0"), 16), rows(R("K16"), 16)), (q, R("BDm"), FR)])
        S["WV"] = ts(BL(16), q, i15, A.mult, CK(26 + 4 * t), A.add)
        x = tt(F(16), PS, R("DM"), A.subtract)
        x = tt(F(16), x, goN, A.mult)
        x = tt(F(16), x, R("DM"), A.add)
        vc(I(R("REC"), vc(U(16), x)), R("HV%d" % t))
        S["BP"] = times(FL(16), PS, -1.0, 9000.0)
        S["THR"] = times(FL(16), FR, 1e6 - 584.5, -1e6)

    def table(t):
        zl = vc(U(8), R("RZ%d" % t, 0, 32, 4))
        vc(I(R("TAB%d" % t), zl), R("CV"))

    def target(t, c, S):
        a, b = CH[t][c]
        n = b - a
        q = natural(R("q4", 0, n), "HG", a, b, lambda j: R("PLW", 128 * j, 128 * j + 128))
        u = S["u%d" % c] = relu(BL(n), q)
        q = R("q6", 448, 448 + n // 16)
        group(q, [(q, Z("Z1", m), cols(u, m, n, 16)) for m in range(16)])
        S["b%d" % c] = either(BL(n), I(R("BT%d" % t), vc(U(n // 16), q)))

    def blocks(t, c):
        a, b = CH[t][c]
        return [(x - a, min(b, x + 128) - a) for x in range(a, b, 128)]

    def gains(t, c, S, part):
        a, b = CH[t][c]
        n, q, V, z = b - a, keys(t, c), "V2" if t else "V1", 2 - t
        ns = NS[t][c]
        if part == 0:
            mm(q, rows(R("P0"), 16), rows(R("M15", 0, wide(q)), 16), True, False)
            other, w, buf, ps = R("C", a, b), R("W32", 0, 8 * z), "MC%d" % (c % 2), R("q2", 0, n)
        else:
            other, w, buf, ps = S["b%d" % c], R("WN32"), "MB%d" % (c % 2), R("q3", 0, n)
        if part or ns < 16:
            mm(ps, R("I128"), other)
        for x, y in blocks(t, c):
            o = rows(cols(q, z * x, z * x + 128), y - x)
            mm(o, cols(other, x, y), R("BW" if part else "CS" if ns else "CW"), False, False)
            if part:
                mm(o, R("LV", a + x, a + y), R("BIGI"), False, False)
        for m in range(16):
            o = R(buf, m * n, m * n + n)
            v = R(V, 16 * a + m, 16 * b, 16)
            if part == 0 and m < ns:
                if m % 2 == 0:
                    for j in (0, 1):
                        d = R("q5", j * n, j * n + n)
                        group(d, [(d, R("NI"), other), (d, R("I128"), R(V, 16 * a + m + j, 16 * b, 16))])
                    act(R(buf, m * n, m * n + 2 * n), R("q5", 0, 2 * n), AF.Relu)
                    call("D%d%d" % (c, m // 2))
            else:
                tt(o, v, ps, A.max)
                call("%s%d%d" % ("CB"[part], t, c))
            sums = [(rows(cols(q, z * x + m, z * x + 16 * wide(w), 16), y - x), cols(o, x, y), w) for x, y in blocks(t, c)]
            if part == 0 and m < ns:
                S["late%d" % c] = S.get("late%d" % c, []) + sums
            else:
                late = S.get("late%d" % c, []) if part else []
                for x in sums + late[2 * m:2 * m + 2]:
                    mm(x[0], x[1], x[2], False, False)
                    nodes[-1]["soon"] = SUMS[c]
        if part:
            mm(q, rows(R("P0"), 16), rows(R("SXT", 0, wide(q)), 16), False, True)

    def best(t, c, S):
        a, b = CH[t][c]
        n, q = b - a, keys(t, c)
        w = 128 * len(blocks(t, c))
        sx = R("SX%d" % (c % 2), 0, w)
        if t:
            scan(sx, R("RST", 0, w), q, 0.0, A.mult, A.max)
        else:
            S["L%d" % c] = FL(w)
            for x in range(0, w, 128):
                scan(cols(sx, x, x + 128), R("RST", 0, 128), cols(q, 2 * x, 2 * x + 128), 0.0, A.mult, A.max)
            for x in range(0, w, 128):
                act(cols(S["L%d" % c], x, x + 128), cols(q, 2 * x + 128, 2 * x + 256))
        sg = act(B(w), I(sx, R("L15", 0, w // 16)), AF.Sign, bias=cT)
        q = R("q4" if t else "q5", 0, n)
        for x, y in blocks(t, c):
            o = cols(q, x, y)
            group(o, [(o, R("BD"), cols(S["u%d" % c], x, y)), (o, cols(sg, x, x + 128), R("N128", 0, y - x))])
        tg = either(B(n), q) if n > 128 else q
        i = vc(IT(w // 16), cols(sx, 15, w, 16))
        W = vc(B(w // 16), ts(IT(w // 16), i, 15, A.bitwise_and))
        for x, y in blocks(t, c):
            mm(R("q7", x, y, 1, 8), cols(W, x // 16, x // 16 + 8), R("I128", 0, y - x))
        either(R("WQ", a, b, 1, 8), R("q7", 0, n, 1, 8))
        either(R("SLS", a, b), mm(R("q7", 256, 256 + n), rows(R("EM"), 10), R("WQ", a, b, 1, 10)))
        for k in range(8):
            o, s, c1, c2 = R("E", k * n, k * n + n), R("SC", k * n, k * n + n), R("TC", k, k + 1), R("TCN", k, k + 1)
            if c < ES[t]:
                act(o, tg, AF.Abs, bias=c2, scale=4096.0)
            elif n > 128:
                both(o, tg, lambda o=o, c1=c1: tsc(o, tg, c1, A.not_equal, 4096.0, A.mult),
                     lambda o=o, c2=c2: g.scalar.activation(ap(o), ap(tg), AF.Abs, bias=ap(c2), scale=4096.0), [c1, c2])
            else:
                ts(o, tg, c1, A.not_equal, 4096.0, A.mult)
            scan(s, o, R("ONE", 0, n), cols(S["G"], k, k + 1), A.min, A.subtract)
        S["G"] = R("SC", n - 1, 8 * n, n)
        if c < 2:
            S["G"] = vc(FL(8), S["G"])

    def movers(t, S):
        ql = S["ql"] = ts(U(8), S["G"], float(CH[t][2][1]), A.add)
        dd = tt(F(128), I(R("SLS"), ql), R("D128"), A.mult)
        sc = scan(F(128), R("RST", 0, 128), dd, 0.0, A.mult, A.max)
        sl = ts(U(8), cols(sc, 15, 128, 16), 9728.0, A.min)
        MV = ts(BL(128), I(R("V2") if t else R("V1"), sl), cM, A.min)
        arr = S["arr"] = R("ARR1") if t else R("X1", 8192, 8304)
        send_each(lambda d: cols(MV, 16 * T.rank_of(d), 16 * T.rank_of(d) + 16), "ma%d" % t, lambda d: cols(arr, 16 * place(d), 16 * place(d) + 16), [arr])

    def left(t, S):
        ql = S["ql"]
        sg = either(F(128), I(R("SLS"), ql))
        OB = S["OB"] = tt(BL(128), I(R("SLOT"), ql), sg, A.is_equal)
        pr = tt(F(128), I(R("POSTF"), ql), OB, A.mult)
        q = mm(R("q7", 0, 128), R("BDf"), pr)
        ts(R("TS%d" % t, 0, 128, 8), cols(q, 16 * rank, 16 * rank + 16), -9000.0, A.add)
        dd = tt(F(128), q, R("D128"), A.mult)
        sc = scan(F(128), R("RST", 0, 128), dd, 0.0, A.mult, A.max)
        vc(I(R("REC"), vc(U(8), cols(sc, 15, 128, 16))), R("C255"))
        if t == 0:
            S["LP"] = either(FL(16), I(R("LF"), S["pl"]))
            x = tt(F(128), I(R("LF"), ql), OB, A.mult)
            S["LW"] = tt(FL(16), mm(R("q7", 256, 272), R("BDf"), cols(x, 16 * rank, 16 * rank + 16)), S["LP"], A.subtract)

    def winner(t, S):
        q = R("q7", 128, 256)
        mm(cols(q, 0, 128, 8), rows(R("P0"), 16), R("ONE", 0, 16, 1, 16))
        for o in range(7):
            mm(cols(q, 1 + o, 128, 8), R("R14"), cols(S["arr"], 16 * o, 16 * o + 16))
        cs = cols(scan(F(128), R("RS8"), tt(F(128), q, R("TS%d" % t), A.mult), 0.0, A.mult, A.min), 7, 128, 8)
        FH = tt(B(16), cs, S["THR"], A.is_lt)
        n = 576 + 16 * t
        if t == 0:
            tt(R("LV", n, n + 16), FH, S["goN"], A.add)
        x = tt(F(16), cs, S["BP"], A.add)
        x = tt(F(16), x, FH, A.mult)
        tt(R("POSTF", n, n + 16), x, S["PS"], A.add)
        if t == 0:
            vc(R("POSTU", n, n + 16), R("POSTF", n, n + 16))
            either(R("V1", 16 * n, 16 * n + 256), I(R("X1"), R("POSTU", n, n + 16)))
            vc(R("LU", n, n + 16), tt(R("LF", n, n + 16), tt(F(16), S["LW"], FH, A.mult), S["LP"], A.add))
        c = red(F(1), tt(F(16), cs, R("D16f"), A.mult), A.add)
        vc(I(R("REC"), ts(U(1), c, 9000.0, A.add)), S["WV"])

    def update(S):
        pl = S["pl"]
        vc(I(R("LV"), pl), tt(B(16), S["LS"], S["goN"], A.subtract))
        vc(I(R("LV"), S["ql"]), tt(B(128), I(R("LV"), S["ql"]), S["OB"], A.subtract))
        vc(I(R("C"), pl), S["AV"])
        either(R("C", 576, 592), S["bt"])
        vc(R("NLU", 576, 592), I(R("NEI"), pl))

    def soon(step, ahead):
        def run(*args):
            k = len(nodes)
            step(*args)
            for x in nodes[k:]:
                x["soon"] = ahead
        return run
    numbers, live, count, centres, table, target, best, movers, winner, update, left = [
        soon(f, a) for f, a in zip((numbers, live, count, centres, table, target, best, movers, winner, update, left), AHEAD)]

    numbers()
    SS = [{"G": R("NJC")}, {"G": R("NJC")}]
    for t in (0, 1):
        S = SS[t]
        if t == 0:
            for a, b in CH[0]:
                gather("HG", R("REC", 0, 8192), "POSTU", a, b, "H")
                live(a, b)
            count(0, S, CH[0])
            absorb()
            times(R("REC", 8192, 8416), R("ONE", 0, 224), c255)
        else:
            count(1, S, [(0, 512), (512, 592)])
        centres(t, S)
        if t == 0:
            for a in range(0, 4992, 1248):
                iota(R("TAB1", a, a + 1248), [[0, 1248]], 0, 0, [S["sent"]])
        table(t)
        for c in range(3):
            gather("HG", R("TAB%d" % t), "NLU", CH[t][c][0], CH[t][c][1], "NM"[t])
        if t == 0:
            gather("V1", R("X1", 0, 8192), "POSTU", 0, 576, "G")
        else:
            a, b = CUT
            larger("V2", R("X1"), "LU", "V1", 0, b, a, 16 * G1, lambda x, y: R("MB1", x - a, y - a), "UWY", ("q3", "q5"))
            larger("V2", R("X1"), "LU", "V1", b, b + JS[0], 8192, JS[1], None, "I", None)
            larger("V2", R("X1"), "LU", "V1", b + JS[0], 8192, 8192, 1024, None, "J", None)
            larger("V2", R("X1"), "LU", "V1", 8192, 9472, 9472, 1280, None, "K", None)
        for c in range(3):
            target(t, c, S)
        moved(t, S)
        gains(t, 0, S, 0)
        gains(t, 1, S, 0)
        for c in range(3):
            gains(t, c, S, 1)
            best(t, c, S)
            if c == 0:
                gains(t, 2, S, 0)
        if t == 0:
            for c in range(3):
                lists(c, S)
        movers(t, S)
        left(t, S)
        if t == 0:
            update(S)
        winner(t, S)
    dma("Y", T.ypost[:], T.POSTF[:, 0:608], [], [R("POSTF", 0, 608)], 2500)
    for h in (0, 1):
        dma("YS"[h], T.yh[h:16:2, :], T.REC[14 + h:128:16, 0:8192], [], [R("REC", 0, 8192)], 2500)
    y, ya = B(224), B(224)
    times(cols(y, 0, 112), R("X1", 8192, 8304), fm)
    times(cols(y, 112, 224), R("ARR1"), fm)
    tt(ya, y, R("REC", 8192, 8416), A.add)
    dma("S", T.ya[:], ap(ya), [], [ya], 2500)
    emit()
